import numpy as np, ml_dtypes
CORES = [3,11,19,27,35,43,51,59]
N = 8
BF = ml_dtypes.bfloat16
def gentries(a):
    return np.ascontiguousarray(a.reshape(8, 16, -1).transpose(0, 2, 1)).reshape(8, -1)
def gtable(e):
    e = np.asarray(e); return np.ascontiguousarray(e.reshape(8, -1, 16).transpose(0, 2, 1)).reshape(128, -1).astype(np.int32)
XI, M, E, L, S, RO, D = 4096, 2048, 2048, 2048, 256, 2, 4
LB = 11
def forest(rng):
    o = np.argsort(rng.random((N, 8, M)), axis=-1); k = np.arange(M)
    inner = (2 * k + 2 < M) & (rng.random((N, 8, M)) >= 0.12); sw = rng.integers(0, 2, (N, 8, M))
    k0 = np.zeros_like(o); k1 = np.zeros_like(o)
    np.put_along_axis(k0, o, np.take_along_axis(o, np.where(inner, 2 * k + 1 + sw, k), 2), 2)
    np.put_along_axis(k1, o, np.take_along_axis(o, np.where(inner, 2 * k + 2 - sw, k), 2), 2)
    return o, k0, k1
def begin(rng, o, lo, hi):
    lv = rng.integers(lo, hi, (N, 8, L))
    return np.take_along_axis(o, 2 ** lv - 1 + (rng.random((N, 8, L)) * 2 ** lv).astype(np.int64), 2)
def vals(rng, n):
    return rng.integers(0, 256, (N, 8, 16, n))
def parts(rng):
    o, k0, k1 = forest(rng)
    return dict(o=o, x=vals(rng, XI), prev=rng.integers(0, XI, (N, 8, XI)), z=vals(rng, M), rs=vals(rng, M), kid0=k0, kid1=k1, env=vals(rng, E),
                start=begin(rng, o, LB - 3 - D, LB - 1), cur=rng.integers(0, XI, (N, 8, L)), w=rng.integers(1, 128, (N, 8, 16)), th=rng.integers(1000, 1500, (N, 8, 1)))
def pack(d):
    r = {}
    for k in ("x", "prev", "z", "rs", "kid0", "kid1", "env", "start", "cur", "w", "th"):
        if k in ("x", "z", "rs", "env"): r[k] = np.ascontiguousarray(d[k].reshape(N, 128, -1)).astype(np.float32).astype(BF)
        elif k in ("start", "cur"): r[k] = np.stack([gtable(a) for a in d[k]])
        elif k == "w": r[k] = d[k].reshape(N, 128, 1).astype(np.int32)
        else: r[k] = np.ascontiguousarray(d[k]).astype(np.int32)
    return r
def setup_inputs(rng):
    return pack(parts(rng))
def setup_inputs_full(rng):
    d = parts(rng)
    d["start"][:, ::2, :S] = d["o"][:, ::2, M // 2:M // 2 + S]; d["th"][:, ::2] = 0
    d["start"][::2, :, :S] = d["o"][::2, :, M // 2:M // 2 + S]; d["th"][::2] = 0
    return pack(d)
def setup_inputs_ties(rng):
    d = parts(rng)
    for k in ("x", "z", "rs", "env"): d[k] = d[k] // 64 * 64
    d["th"] = 64 * rng.integers(18, 22, (N, 8, 1))
    return pack(d)
def setup_inputs_alike(rng):
    d = parts(rng); m = np.arange(M)
    d["start"][:, 0] = d["o"][:, 0, M - 1:M]; d["th"][:, 0] = 0
    d["start"][:, 1] = rng.choice(np.array([0, M - 1]), (N, L)); d["cur"][:, 1] = rng.choice(np.array([0, XI - 1]), (N, L))
    d["prev"][:, 1] = np.where(rng.random((N, XI)) < 0.5, np.arange(XI), rng.choice(np.array([0, XI - 1]), (N, XI)))
    d["kid0"][:, 2] = (m + 1) & (M - 1); d["kid1"][:, 2] = (m + 1 + rng.integers(0, M - 1, (N, M))) & (M - 1)
    d["kid0"][:, 3] = m; d["kid1"][:, 3] = m
    d["start"][:, 3] = np.take_along_axis(rng.integers(0, M, (N, 40)), rng.integers(0, 40, (N, L)), 1)
    d["w"][:, 4] = 0; d["th"][:, 4] = 4096
    d["z"][:, 5] = 0; d["rs"][:, 5] = rng.choice(np.array([0, 255]), (N, 16, M))
    d["kid1"][:, 6] = d["kid0"][:, 6]; d["prev"][:, 6] = np.arange(XI)
    d["x"][:, 7] = 255; d["env"][:, 7] = 255; d["w"][:, 7] = 127; d["th"][:, 7] = 0
    return pack(d)
def setup_inputs_edges(rng):
    d = parts(rng); r = np.arange(N)[:, None]
    d["start"][:, :2, :S] = d["o"][:, :2, M // 2:M // 2 + S]; d["env"][:, :2] = 0
    c = rng.integers(0, 256, (16, 1)); d["x"][:, 0] = c
    d["rs"][:, 0] = np.where(rng.random((N, 1, M)) < 0.5, c, d["rs"][:, 0]); d["th"][:, 0] = r & 1
    c = 255 * rng.integers(0, 2, (16, 1)); d["x"][:, 1] = c
    d["rs"][:, 1] = 255 - c; d["rs"][:, 1, 0] = np.abs(255 - c[0] - rng.integers(0, 3, (N, M)))
    d["th"][:, 1] = np.array([4080, 4081, 4096, 4079])[r & 3]
    d["x"][:, 2:4] = rng.integers(250, 256, (N, 2, 16, XI)); d["w"][:, 2:4] = 127; d["env"][:, 3] = 0
    d["th"][:, 3] = rng.integers(2040, 2060, (N, 1))
    d["kid1"][:, 4] = np.where(rng.random((N, M)) < 0.5, d["kid0"][:, 4], d["kid1"][:, 4])
    return pack(d)
def setup_inputs_spread(rng):
    d = parts(rng); m = np.arange(M); lf = rng.random((N, 4, M)) < 0.5
    for k in ("kid0", "kid1"): d[k][:, 1::2] = np.where(lf, m, (m + rng.integers(1, M, (N, 4, M))) & (M - 1))
    for k, n in (("x", XI), ("z", M), ("rs", M), ("env", E)):
        d[k] = np.minimum((np.exp2(8 * rng.random((N, 8, 1, n))) * rng.random((N, 8, 16, n))).astype(np.int64), 255)
    d["w"] = np.minimum(np.exp2(7 * rng.random((N, 8, 16))).astype(np.int64), 127)
    d["th"] = np.minimum(np.exp2(12 * rng.random((N, 8, 1))).astype(np.int64), 4096); d["th"][:, 0] = 1; d["th"][:, 1] = 0
    d["start"] = begin(rng, d["o"], 0, LB)
    d["cur"] = np.minimum((XI * rng.random((N, 8, L)) ** 3).astype(np.int64), XI - 1)
    d["prev"] = np.where(rng.random((N, 8, XI)) < 0.5, np.maximum(np.arange(XI) - rng.integers(0, 40, (N, 8, XI)), 0), d["prev"])
    return pack(d)
def check_inputs(d):
    bad = []
    for k, lo, hi in (("x", 0, 255), ("prev", 0, XI - 1), ("z", 0, 255), ("rs", 0, 255), ("kid0", 0, M - 1), ("kid1", 0, M - 1), ("env", 0, 255), ("start", 0, M - 1), ("cur", 0, XI - 1), ("w", 0, 127), ("th", 0, 4096)):
        a = np.asarray(d[k]).astype(np.float32)
        if not np.all((a >= lo) & (a <= hi) & (a == np.floor(a))): bad.append("range of " + k)
    m = np.arange(M)
    if np.any((np.asarray(d["kid0"]) == m) != (np.asarray(d["kid1"]) == m)): bad.append("one kid of a node is the node itself, the other isn't")
    return bad
def pick(a, ix):
    return np.take_along_axis(a, ix[:, :, None, :], 3)
def reference(x, prev, z, rs, kid0, kid1, env, start, cur, w, th):
    def cols(a, more):
        b = a.astype(np.float32).astype(np.int32).reshape(N, 8, 16, -1)
        return np.concatenate([b, np.zeros((N, 8, 16, more), np.int32)], axis=3)
    X = cols(x, RO * L); Z = cols(z, 2 * S * RO); R = cols(rs, 2 * S * RO); EN = cols(env, 0)
    P = np.concatenate([prev.astype(np.int64), np.zeros((N, 8, RO * L), np.int64)], axis=2)
    own = np.zeros((N, 8, 1), np.int64) + np.arange(M, M + 2 * S * RO)
    K0 = np.concatenate([kid0.astype(np.int64), own], axis=2); K1 = np.concatenate([kid1.astype(np.int64), own], axis=2)
    F0 = np.stack([gentries(a) for a in start]).astype(np.int64); C = np.stack([gentries(a) for a in cur]).astype(np.int64)
    W = w.reshape(N, 8, 16, 1).astype(np.int32); TH = th.reshape(N, 8, 1).astype(np.int64)
    lower = np.arange(S)[None, :] < np.arange(S)[:, None]
    for t in range(RO):
        f = F0; s = C
        for step in range(D):
            k0 = np.take_along_axis(K0, f, 2); k1 = np.take_along_axis(K1, f, 2); go = k0 != f
            b = np.sum(pick(X, s) >= pick(Z, f), axis=2) >= 9
            f = np.where(go, np.where(b, k1, k0), f); s = np.where(go, np.take_along_axis(P, s, 2), s)
        xc = pick(X, C); rf = pick(R, f); a = np.sum(rf > xc, axis=2)
        y = pick(EN, (np.sum(W * xc, axis=2) + 97 * a) & (E - 1)); v = (xc + y) & 255
        fs = f[:, :, :S]; leaf = np.take_along_axis(K0, fs, 2) == fs
        first = ~np.any((fs[:, :, :, None] == fs[:, :, None, :]) & lower, axis=3)
        far = np.sum(np.abs(rf[..., :S] - v[..., :S]), axis=2) >= TH
        q, g, i = np.nonzero(leaf & first & far); at = fs[q, g, i]; n0 = M + 2 * S * t + 2 * i; xs = pick(X, s[:, :, :S])
        Z[q, g, :, at] = xs[q, g, :, i]; K0[q, g, at] = n0; K1[q, g, at] = n0 + 1
        R[q, g, :, n0] = rf[q, g, :, i]; R[q, g, :, n0 + 1] = (rf[q, g, :, i] + v[q, g, :, i]) >> 1
        came = np.roll(v, 1, axis=0)
        h = np.sum(W * came, axis=2) & (L - 1); lo = XI + L * t
        X[..., lo:lo + L] = came; P[..., lo:lo + L] = np.take_along_axis(C, h, 2)
        C = np.zeros((N, 8, 1), np.int64) + np.arange(lo, lo + L)
    return {"yk0": K0.astype(np.float32), "yk1": K1.astype(np.float32), "yr": np.ascontiguousarray(R[..., M:].reshape(N, 128, 2 * S * RO)).astype(np.float32).astype(BF), "yp": np.ascontiguousarray(P[..., XI:]).astype(np.float32)}

@@ -1,0 +1,613 @@
+from concourse.bass import DstId, RemoteDMATransfer
+from concourse.mybir import AluOpType as A, ActivationFunctionType as F
+
+S, HL = 256, 1024
+MW = 2560
+DUMP, WW = 3072, 3328
+BIG = 8192.0
+BFB, FP, I4, U2 = "bfloat16", "float32", "int32", "uint16"
+SCRATCH = {}
+
+
+def _decl(where, dtype, text):
+    for w in text.split():
+        nm, c = w.split(":")
+        p = 128
+        if "x" in c:
+            p, c = c.split("x")
+        SCRATCH[nm] = (where, [int(p), int(c)], dtype)
+
+
+_decl("sbuf", BFB, "XW:4096 PW:4096 ZW:3328 KW:3328 RW:2560 EW:2048 OW:2560 HIW:2560 VL:2048 KDl:256 KDh:256 PDl:256 PDh:256 ONB:128 ZB:256 "
+      "IDB:128 I8K:128 BC8:8 BLK:128 I4B:256 BASE:256 DR:256 WN8:8 EH:16x256 RHS:24 RT:8 OB:128 OBN:128 WQ1:2048 WQP:2048 WQW:2048 LOI:256 "
+      "HII:256 NK:256 NKb:256 YR1:512 XF:256 PT2:256 RF:256 KQ:256 OQ:256 FBI:256 FE:256 FO:256 LF:256 DUP:16 DUT:16x128 JK:1024 AD:256 SP:256 "
+      "XS0:2048 XS1:2048 XS2:2048 XS3:2048 YS1:2048 YS2:2048 YS3:2048 CK0:2048 CK1:2048 CR0:1024 CR1:1024 PT0:1024 PT1:1024 SS0:1024 SS1:1024 MM0:1024 MM1:1024")
+_decl("sbuf", FP, "KF:3328 CF:2048 HG:2048 thF:8x1 THC:1 KDf:256 cuF:128 cuT:128 ONF:128 IDF:128 E8:8x128 COL:32 CT:32x16 EQ:16x128 EQ2:32x128 DW:16 NV0:256 "
+      "NV1:256 FW:80 SW:80 SFa:64 SFb:64 HR:128 HS:128 HFT:128 DM:16 TG:80 A97:128 MA0:64x128 MA1:64x128 MB0:64x128 MB1:64x128 FT0:64x128 FT1:64x128")
+_decl("sbuf", I4, "stI:128 cuI:128 KD:256 PD:256 wI:1 wN:1 thI:8x1 KDt:256 KDu:256 PDt:256 PDu:256 FI:256 FB:256 RS1:256 RS2:256 IT:512")
+_decl("sbuf", U2, "LL:1536")
+_decl("psum", FP, "bMI:512 bSP:512 bTP0:512 bTP1:512 bLP0:512 bLP1:512 bOP0:512 bOP1:512")
+SEMAPHORES = ["cv", "cs", "ct", "cg"] + ["d%d" % _k for _k in range(48)] + ["aw", "lw", "aA0", "aA1", "lA0", "lA1", "aH", "lH"]
+
+CYC, GAT = 0.83e-3, 1.56
+WAKE, SELF, DBW, DLAT = 0.12, 0.08, 250.0, 2.0
+PREF = {"ki": 0, "xs": 0, "pv": 1, "ys": 0, "cu": 0}
+BETA, TRIES, PCF, SEED0 = 0.03, 6000, 1.15, 7
+MODELS = ((1.2, 1.0, 0.12, 1.0, 1.0), (1.2, 0.72, 0.25, 1.5, 1.3), (1.3, 1.25, 0.1, 0.8, 1.0))
+PLANS = {}
+
+
+def make_plan(ops):
+    n = len(ops)
+    succ = [[] for _ in range(n)]
+    for i, o in enumerate(ops):
+        for d in o["deps"]:
+            succ[d].append(i)
+    rq = [[a[0][0] if a[0] in ("yd", "sd", "gr") else a[0] for a in o["alts"]] for o in ops]
+    dma = [o["alts"][0][0] in ("yd", "sd") for o in ops]
+    pri = [0.0] * n
+    for i in range(n - 1, -1, -1):
+        o = ops[i]
+        pri[i] = min(a[1] for a in o["alts"]) + o["lat"] + (DLAT if dma[i] else 0.0) + max([pri[j] + WAKE for j in succ[i]] or [0.0])
+
+    def schedule(boost, pick, beta):
+        left, ready = [len(o["deps"]) for o in ops], [0.0] * n
+        open_ = [i for i in range(n) if not left[i]]
+        free, order, bw = {}, [], 0.0
+        while open_:
+            best = None
+            for i in open_:
+                p = pri[i] + boost[i]
+                for j in range(len(rq[i])):
+                    if pick[i] >= 0 and pick[i] != j:
+                        continue
+                    st = ready[i] if rq[i][j] == "arr" else max(ready[i], free.get(rq[i][j], 0.0))
+                    key = (st - beta * p, -p, i, j)
+                    if best is None or key < best[0]:
+                        best = (key, i, j, st)
+            _, i, j, st = best
+            open_.remove(i)
+            q, d = rq[i][j], ops[i]["alts"][j][1] * (PCF if rq[i][j] in "vstg" else 1.0)
+            if q != "arr":
+                free[q] = st + d
+            fin = st + d + ops[i]["lat"]
+            if dma[i]:
+                bw = max(bw, st + d) + ops[i]["lat"]
+                fin = bw + DLAT
+            order.append((i, j))
+            for s_ in succ[i]:
+                ready[s_] = max(ready[s_], fin + (SELF if rq[s_] == [q] else WAKE))
+                left[s_] -= 1
+                if not left[s_]:
+                    open_.append(s_)
+        return order
+
+    def score(order, watch):
+        tot, way = 0.0, []
+        for mi, (cf, gf, wk, bf, lf) in enumerate(MODELS):
+            fin, free, bw, mx, end = [0.0] * n, {}, 0.0, 0.0, 0
+            prev, why = {}, [None] * n
+            for i, j in order:
+                o, q = ops[i], rq[i][j]
+                d = o["alts"][j][1]
+                if q in "vstg" and not dma[i]:
+                    d *= cf * (gf if o["gat"] else 1.0)
+                t = 0.0 if q == "arr" else free.get(q, 0.0)
+                w = (prev.get(q), True)
+                for x in o["deps"]:
+                    if fin[x] + wk > t:
+                        t = fin[x] + wk
+                        w = (x, False)
+                why[i], prev[q] = w, i
+                e = t + d
+                if q != "arr":
+                    free[q] = e
+                if dma[i]:
+                    bw = max(bw, e) + o["lat"] / bf
+                    e = bw + DLAT * lf
+                else:
+                    e += o["lat"] * lf
+                fin[i] = e
+                if e > mx:
+                    mx, end = e, i
+            tot += mx / (cf * (1 + gf))
+            if mi == watch:
+                x = end
+                while x is not None:
+                    way.append((x, why[x][0] if why[x][1] else None))
+                    x = why[x][0]
+        return tot, way
+    boost, pick = [o["boost"] for o in ops], [o["pref"] for o in ops]
+    two = [i for i in range(n) if len(rq[i]) == 2]
+    order = schedule(boost, pick, BETA)
+    seed = [SEED0]
+    best, way = score(order, 0)
+
+    def rnd():
+        seed[0] = (seed[0] * 1103515245 + 12345) % 2147483648
+        return seed[0] / 2147483648.0
+    for it in range(TRIES):
+        b2, p2 = list(boost), list(pick)
+        share, amp = 0.02 + 0.4 * rnd() ** 2, 1.0 + 12.0 * rnd()
+        for i, before in way:
+            if before is not None and rnd() < share:
+                b2[i] += amp * rnd()
+                b2[before] -= amp * rnd()
+        if rnd() < 0.5:
+            for i in two:
+                if rnd() < 0.04:
+                    p2[i] = int(3 * rnd()) - 1
+        if rnd() < 0.3:
+            for i in range(n):
+                if rnd() < 0.04:
+                    b2[i] += amp * (2 * rnd() - 1)
+        o2 = schedule(b2, p2, BETA)
+        s2, w2 = score(o2, int(rnd() * len(MODELS)))
+        if s2 <= best:
+            best, order, boost, pick, way = s2, o2, b2, p2, w2
+    return order, best
+
+
+def rank_program(g, core, T, topo):
+    rank = T.rank_of(core)
+    if rank is None:
+        return
+    n_ranks = len(T.cores)
+    nxt, prv = T.cores[(rank + 1) % n_ranks], T.cores[(rank - 1) % n_ranks]
+    ops, last, readers, fore = [], {}, {}, [0.0]
+
+    def LI(k, a, b):
+        return T.LL[:, 128 * k + a:128 * k + b]
+
+    def op(alts, R, W, nm="", lat=0.0, tok=None, boost=0.0, gat=False, pref=-1):
+        i, deps = len(ops), set()
+        for k in list(R) + list(W):
+            if k in last:
+                deps.add(last[k])
+        for k in W:
+            deps.update(readers.get(k, ()))
+        for k in R:
+            readers.setdefault(k, []).append(i)
+        for k in W:
+            last[k] = i
+            readers[k] = []
+        deps.discard(i)
+        ops.append(dict(alts=alts, deps=deps, nm=nm, lat=lat, tok=tok, boost=boost + (fore[0] if alts[0][0] in "vstg" else 0.0), gat=gat, pref=pref))
+
+    def vc(n, half=False):
+        return 0.05 + max(64, n * (0.5 if half else 1)) * CYC
+
+    def PE(fn, cyc, R, W, nm=""):
+        op([("t", 0.05 + cyc * CYC, fn)], R, W, nm)
+    nd = [0]
+
+    def DMA(out, in_, R, W, nm="", q="y", kb=64, boost=0.0):
+        s = "d%d" % nd[0]
+        nd[0] += 1
+        op([(q + "d", 0.07, lambda e: e.dma_start(out, in_).then_inc(T.sem[s], 16))], R, W, nm, lat=kb / DBW, tok=(s, 16), boost=boost)
+
+    def vcopy(out, in_, R, W, nm=""):
+        op([("v", vc(out.shape[1]), lambda e: e.tensor_copy(out, in_))], R, W, nm)
+
+    def vts(out, in0, s1, s2, o0, o1, R, W, nm="", half=False):
+        if o1 is None:
+            op([("v", vc(out.shape[1], half), lambda e: e.tensor_scalar(out, in0, s1, None, o0))], R, W, nm)
+        else:
+            op([("v", vc(out.shape[1], half), lambda e: e.tensor_scalar(out, in0, s1, s2, o0, o1))], R, W, nm)
+
+    def vtt(out, i0, i1, o, R, W, nm="", two=True):
+        op([("v", vc(out.shape[1] * (2 if two else 1)), lambda e: e.tensor_tensor(out, i0, i1, o))], R, W, nm)
+
+    def act(out, in_, func, R, W, nm="", **k):
+        op([("s", 0.065 + max(64, in_.shape[1]) * CYC, lambda e: e.activation(out, in_, func, **k))], R, W, nm)
+
+    def gather(out, win, off, n, R, W, nm):
+        d = n * GAT * CYC
+        a = [("s", 0.07 + d, lambda e: e.activation(out, win.indirect(off), F.Copy)),
+             ("v", 0.06 + d, lambda e: e.tensor_copy(out, win.indirect(off)))]
+        op(a, R, W, nm, gat=True, pref=PREF.get(nm[:2], -1))
+
+    def gatherop(out, win, off, in1, o, R, W, nm):
+        op([("v", 0.06 + HL * GAT * CYC, lambda e: e.tensor_tensor(out, win.indirect(off), in1, o))], R, W, nm, gat=True)
+
+    def ms(ap, c, W, half=True):
+        op([("v", vc(ap.shape[1], half), lambda e: e.memset(ap, c))], [], W, "ms")
+
+    def cnt_(pat):
+        n = 1
+        for a_, b_ in pat:
+            n *= b_
+        return 0.15 + 2 * n * CYC
+
+    def aff(out, in_, pat, cmpo, fill, base, cm, R, W):
+        op([("g", cnt_(pat), lambda e: e.affine_select(out, in_, pat, cmpo, fill, base, cm))], R, W)
+
+    def iota(out, pat, base, cm, W, R=()):
+        op([("g", cnt_(pat), lambda e: e.iota(out, pat, base, cm, allow_small_or_imprecise_dtypes=True))], R, W)
+
+    B, KWK, KTK = 90.0, ["KW0", "KW1", "KW2", "KW3"], ["KT0", "KT1", "KT2", "KT3"]
+    DMA(T.KD[:, 0:128], T.kid0[:], [], ["KD0"], "kid0", "y", boost=B)
+    DMA(T.PD[:], T.prev[:], [], ["PD"], "prev", "s", 128, boost=B)
+    DMA(T.KD[:, 128:256], T.kid1[:], [], ["KD1"], "kid1", "y", boost=B - 1)
+    DMA(T.cuI[:], T.cur[:], [], ["cuI"], "cur", "s", boost=B - 1)
+    DMA(T.stI[:], T.start[:], [], ["stI"], "start", "y", boost=B - 2)
+    DMA(T.XW[:], T.x[:], [], ["XW"], "x", "s", 1024, boost=B - 60)
+    DMA(T.ZW[:, 0:2048], T.z[:], [], ["ZW"], "z", "y", 512, boost=B - 70)
+    DMA(T.wI[:], T.w[:], [], ["wI"], "w", "y", 1, boost=B - 3)
+    DMA(T.thI[:], T.th[:], [], ["thI"], "th", "y", 1, boost=B - 7)
+
+    fore[0] = 80.0
+    ms(T.ONB[:], 1.0, ["ONB"])
+    ms(T.ZB[:], 0.0, ["ZB"])
+    ms(T.WQP[:], 0.0, ["WQP"])
+    fore[0] = 0.0
+    ms(T.PW[:], 0.0, ["PW0", "PW1"])
+    fore[0] = 60.0
+    act(T.KW[:, 0:2048], T.WQP[:], F.Copy, ["WQP"], KWK, "zero")
+    fore[0] = 0.0
+    ms(T.ONF[:], 1.0, ["ONF"], half=False)
+    ms(T.ZW[:, 2048:MW], 0.0, ["ZT"])
+    fore[0] = 70.0
+    aff(T.BC8[:], T.ONB[:, 0:8], [[-16, 8]], A.is_ge, 0.0, 0, 1, ["ONB"], ["BC8"])
+    aff(T.BC8[:], T.BC8[:], [[16, 8]], A.is_ge, 0.0, 15, -1, ["BC8"], ["BC8"])
+    fore[0] = 0.0
+    aff(T.IDF[:], T.ONF[:], [[-1, 128]], A.is_equal, 0.0, 0, 1, ["ONF"], ["IDF"])
+    aff(T.BLK[:], T.ONB[:], [[-16, 8], [0, 16]], A.is_ge, 0.0, 0, 1, ["ONB"], ["BLK"])
+    aff(T.BLK[:], T.BLK[:], [[16, 8], [0, 16]], A.is_ge, 0.0, 15, -1, ["BLK"], ["BLK"])
+    iota(T.KW[:, 2048:MW], [[0, MW - 2048]], 0, 0, KTK)
+    fore[0] = -60.0
+    iota(T.OW[:], [[0, 10], [1, 256]], 0, 0, ["OW0", "OW1"])
+    iota(T.HIW[:], [[1, 10], [0, 256]], 0, 0, ["HIW"])
+    fore[0] = 0.0
+    iota(T.I4B[:], [[4, 256]], 0, 0, ["I4B"])
+    aff(T.EH[:], T.ZB[0:16, :], [[-8, 2], [-1, 8], [0, 16]], A.not_equal, -BIG, 0, 1, ["ZB"], ["EH"])
+    aff(T.E8[:], T.ONF[0:8, :], [[-1, 8], [0, 16]], A.is_equal, 0.0, 0, 1, ["ONF"], ["E8"])
+    iota(T.DW[:], [[16, 16]], DUMP, 0, ["DW"])
+    iota(T.NV0[:], [[2, 256]], 2048, 0, ["NV0"])
+    iota(T.LOI[:], [[0, 2], [2, 128]], 0, 0, ["LOI"])
+    iota(T.HII[:], [[1, 2], [0, 128]], 8, 0, ["HII"])
+    fore[0] = -60.0
+    iota(T.KF[:, 2048:3072], [[1, 1024]], 2048, 0, ["KFt"])
+    iota(T.CF[:], [[0, 2048]], 0, 0, ["CF"])
+
+    TAB = {"k": (), "e1": ((1, 1),), "e2": ((2, 1),), "e02": ((0, 1), (2, 1)), "e13": ((1, 1), (3, 1)), "pc": ((0, 1), (1, 256)),
+           "pn": ((0, -1), (1, -256)), "sc": tuple((k, 2 ** (11 - k)) for k in range(12)), "e12": ((12, 1),), "c12": ()}
+    NT = len(TAB)
+    C = dict((nm, j) for j, nm in enumerate(list(TAB) + ["me", "mo", "q0b", "q1b", "p", "q0", "q1", "w", "wn"]))
+
+    def col(nm):
+        return T.COL[:, C[nm]:C[nm] + 1]
+    fore[0] = 40.0
+    ms(T.CT[:], 0.0, ["CT" + nm for nm in C], half=False)
+    fore[0] = 0.0
+    for nm in TAB:
+        c, ck = T.CT[0:16, C[nm]:C[nm] + 1], ["CT" + nm]
+        if nm == "k":
+            iota(c, [[0, 1]], 0, 1, ck)
+        if nm == "c12":
+            aff(c, c, [[0, 1]], A.is_equal, -1024.0, -12, 1, ck, ck)
+        for k, v in TAB[nm]:
+            aff(c, c, [[0, 1]], A.not_equal, float(v), -k, 1, ck, ck)
+    u = 2.0 ** -20
+    for nm, o in (("me", 0), ("mo", 16)):
+        c, ck = T.CT[:, C[nm]:C[nm] + 1], ["CT" + nm]
+        aff(c, c, [[0, 1]], A.is_gt, u, 16 if o else -11, -1 if o else 1, ck, ck)
+        for k, v in ((12, -u), (13, -5.5 * u), (14, -5.5 * u)) + (((15, 0.0),) if o else ()):
+            aff(c, c, [[0, 1]], A.not_equal, v, -k - o, 1, ck, ck)
+    aff(T.EQ[:], T.ONF[0:16, :], [[0, 8], [1, 16]], A.is_equal, 0.0, 0, -1, ["ONF"], ["EQ"])
+    aff(T.EQ2[:], T.ONF[0:32, :], [[0, 4], [1, 32]], A.is_equal, 0.0, 0, -1, ["ONF"], ["EQ2"])
+    PE(lambda e: [e.matmul(T.bMI[:, 0:NT], T.EQ[:], T.CT[0:16, 0:NT], True, True), e.matmul(T.bMI[:, NT:NT + 2], T.EQ2[:], T.CT[:, NT:NT + 2], True, True)],
+       512, ["EQ", "EQ2"] + ["CT" + nm for nm in C], ["bMI"], "cols")
+    op([("s", 0.12, lambda e: e.activation(T.COL[:, 0:NT + 2], T.bMI[:, 0:NT + 2], F.Copy))], [], list(TAB) + ["me", "mo", "bMI"], "cols")
+    iota(col("p"), [[0, 1]], 0, 1, ["p"])
+    for nm, ad in (("q0", 0.0), ("q1", 128.0)):
+        act(col(nm), col("p"), F.Copy, ["p"], [nm], "q", scale=1.0 / 256, bias=ad / 256)
+        act(col(nm), col(nm), F.Square, [nm], [nm], "q")
+        act(col(nm + "b"), col(nm), F.Copy, [nm], [nm + "b"], "q", bias=-1.0)
+    act(T.BASE[:], T.I4B[:], F.Identity, ["I4B", "e12", "c12"], ["BASE"], "base", scale=col("e12"), bias=col("c12"))
+
+    def fills(out, vals, W):
+        src, rd = T.ZB[:, 0:8], "ZB"
+        for k, v in vals:
+            aff(out, src, [[-16, 8]], A.not_equal, v, -k, 1, [rd], [W])
+            src, rd = out, W
+    fore[0] = 80.0
+    fills(T.RT[:, 0:8], ((0, 1.0), (1, 256.0)), "P01")
+    fore[0] = 60.0
+    iota(T.WQ1[:], [[0, 2048]], 0, 0, ["WQ1"], ["P01"])
+    fore[0] = 0.0
+    fills(T.RHS[:, 8:16], ((0, 0.5), (1, 128.0), (2, 0.5), (3, 128.0)), "RHSb")
+    fills(T.RHS[:, 16:24], ((0, -1.0), (1, -256.0), (2, 1.0), (3, 256.0)), "RHSd")
+    act(T.RHS[:, 0:8], T.BC8[:], F.Copy, ["BC8"], ["RHSa"], "rhs")
+    RH = ["RHSa", "RHSb", "RHSd"]
+
+    def fillq(dst, src, R, W):
+        op([("s", 16 * (0.065 + 64 * CYC), lambda e: [e.activation(dst[:, 129 * q:128 * q + 128:16], src, F.Copy) for q in range(16)])], R + W, W, "fill")
+    fore[0] = 60.0
+    fillq(T.WQP, T.RT[:, 0:8], ["P01"], ["WQP"])
+    fore[0] = 0.0
+    fillq(T.WQ1, T.BC8[:], ["BC8"], ["WQ1"])
+    vcopy(col("w"), T.wI[:], ["wI"], ["w"])
+    op([("s", 1.77, lambda e: e.activation(T.WQW[:], T.WQ1[:], F.Copy, scale=col("w"))),
+        ("v", 0.9, lambda e: e.tensor_scalar(T.WQW[:], T.WQ1[:], col("w"), None, A.mult))], ["WQ1", "w"], ["WQW"], "WQW")
+    act(T.IDB[:], T.IDF[:], F.Copy, ["IDF"], ["IDB"], "cst")
+    act(T.I8K[:], T.IDF[:], F.Copy, ["IDF"], ["I8K"], "cst", scale=BIG)
+    act(T.OB[:], T.BLK[:], F.Copy, ["BLK", "pc"], ["OB"], "cst", scale=col("pc"))
+    act(T.OBN[:], T.BLK[:], F.Copy, ["BLK", "pn"], ["OBN"], "cst", scale=col("pn"))
+    act(T.DW[:], T.DW[:], F.Identity, ["DW", "k"], ["DW"], "cst", bias=col("k"))
+    act(T.NV0[:], T.NV0[:], F.Identity, ["NV0", "e1"], ["NV0"], "cst", bias=col("e1"))
+    act(T.NV1[:], T.NV0[:], F.Copy, ["NV0"], ["NV1"], "cst", bias=512.0)
+    act(T.NK[:], T.LOI[:], F.Identity, ["LOI", "e02", "e2"], ["NK"], "cst", scale=col("e02"), bias=col("e2"))
+    act(T.NKb[:], T.HII[:], F.Copy, ["HII", "e13"], ["NKb"], "cst", scale=col("e13"))
+    vtt(T.NK[:], T.NK[:], T.NKb[:], A.add, ["NK", "NKb"], ["NK"])
+
+    vcopy(LI(0, 0, 128), T.stI[:], ["stI"], ["L0_0", "L0_1"])
+    vcopy(LI(5, 0, 128), T.cuI[:], ["cuI"], ["SL0_0", "SL0_1"])
+    vts(T.PDt[:], T.PD[:], 255, None, A.bitwise_and, None, ["PD"], ["PDt"])
+    vts(T.PDu[:], T.PD[:], 8, None, A.arith_shift_right, None, ["PD"], ["PDu"])
+    vcopy(T.PDl[:], T.PDt[:], ["PDt"], ["PDl"])
+    vcopy(T.PDh[:], T.PDu[:], ["PDu"], ["PDh"])
+    DMA(T.PW[0:128:16, :], T.PDl[:], ["PDl"], ["PW0"], "pw0")
+    DMA(T.PW[1:128:16, :], T.PDh[:], ["PDh"], ["PW1"], "pw1")
+    vts(T.KDt[:], T.KD[:], 255, None, A.bitwise_and, None, ["KD0", "KD1"], ["KDt"])
+    vts(T.KDu[:], T.KD[:], 8, None, A.arith_shift_right, None, ["KD0", "KD1"], ["KDu"])
+    vcopy(T.KDl[:], T.KDt[:], ["KDt"], ["KDl"])
+    vcopy(T.KDh[:], T.KDu[:], ["KDu"], ["KDh"])
+    DMA(T.KW[0:128:16, 0:2048], T.KDl[:, 0:128], ["KDl"], ["KW0"], "kw0", kb=32)
+    DMA(T.KW[1:128:16, 0:2048], T.KDh[:, 0:128], ["KDh"], ["KW1"], "kw1", kb=32)
+    DMA(T.KW[2:128:16, 0:2048], T.KDl[:, 128:256], ["KDl"], ["KW2"], "kw2", kb=32)
+    DMA(T.KW[3:128:16, 0:2048], T.KDh[:, 128:256], ["KDh"], ["KW3"], "kw3", kb=32)
+    DMA(T.RW[:, 0:2048], T.rs[:], ["KDl", "KDh", "PDl", "PDh"], ["RW"], "rs", "y", 512, boost=-200.0)
+    DMA(T.EW[:], T.env[:], ["KDl", "KDh", "PDl", "PDh"], ["EW"], "env", "y", 512, boost=-210.0)
+    DMA(T.OW[1:128:16, :], T.HIW[0:8, :], ["HIW", "KDh"], ["OW1"], "ow1", kb=40, boost=-220.0)
+    DMA(T.KW[0:128:16, 2048:MW], T.OW[0:128:16, 2048:MW], ["OW0"], ["KT0"], "kt0", kb=8, boost=-220.0)
+    DMA(T.KW[1:128:16, 2048:MW], T.HIW[0:8, 2048:MW], ["HIW"], ["KT1"], "kt1", kb=8, boost=-220.0)
+    DMA(T.KW[2:128:16, 2048:MW], T.OW[0:128:16, 2048:MW], ["OW0"], ["KT2"], "kt2", kb=8, boost=-220.0)
+    DMA(T.KW[3:128:16, 2048:MW], T.HIW[0:8, 2048:MW], ["HIW"], ["KT3"], "kt3", kb=8, boost=-220.0)
+
+    def wrap(bank, c0, wq, src, s0, n, R, W, nm):
+        PE(lambda e: [e.matmul(bank[:, c0:c0 + n], wq[:, 128 * q:128 * q + 128], src[:, s0 + q:s0 + 16 * n:16], q == 0, q == 15) for q in range(16)],
+           16 * max(64, n), R, W, nm)
+
+    def step(t, k, h, X, xk):
+        hs, win = str(h), (MW if t else 2048)
+        ck, tp, lp, tk = T["CK" + hs], T["bTP" + hs], T["bLP" + hs], "bTP" + hs
+        off, lk = LI(k, 64 * h, 64 * h + 64), ["L%d_%d" % (k, h)]
+        gather(ck[:, 0:HL], T.KW[:, 0:win], off, HL, lk + KWK + (KTK if t else []), ["CKk" + hs], "kid")
+        gatherop(ck[:, HL:2 * HL], T.ZW[:, 0:win], off, X[:, HL * h:HL * h + HL], A.is_le, lk + ["ZW", xk] + (["ZT"] if t else []), ["CKz" + hs], "z")
+        PE(lambda e: [e.matmul(tp[:, q:384:16], ck[:, q:2 * HL:16], T.RHS[:], True, True) for q in range(16)], 1024, ["CKk" + hs, "CKz" + hs] + RH, [tk], "T")
+        ma, mb_, ft = T["MA" + hs], T["MB" + hs], T["FT" + hs]
+        vts(ma[:], tp[64:128, 0:128], 8.5, 0.5, A.is_ge, A.subtract, [], ["MA" + hs, tk], "m")
+        vtt(mb_[:], ma[:], tp[0:64, 256:384], A.mult, ["MA" + hs, tk], ["MB" + hs], "t", two=False)
+        vtt(ft[:], mb_[:], tp[0:64, 128:256], A.add, ["MB" + hs, tk], ["FT" + hs], "f", two=False)
+        PE(lambda e: e.matmul(lp[:, 0:64], ft[:, 0:128], T.IDF[0:64, 0:64], True, True), 256, ["FT" + hs, "IDF"], ["bLP" + hs], "tr")
+        vcopy(LI(k + 1, 64 * h, 64 * h + 64), lp[:, 0:64], [], ["L%d_%d" % (k + 1, h), "bLP" + hs], "list")
+
+    def outcome(t, X, xk):
+        win = MW if t else 2048
+        for h in range(2):
+            wrap(T["bOP%d" % h], 0, T.WQW, X, HL * h, 64, ["WQW", xk[h]], ["bOP%d" % h], "wc")
+        for h in range(2):
+            hs = str(h)
+            bo, cr, ss, mm = T["bOP" + hs], T["CR" + hs], T["SS" + hs], T["MM" + hs]
+            xh, a97 = X[:, HL * h:HL * h + HL], T.A97[:, 64 * h:64 * h + 64]
+            gatherop(cr[:], T.RW[:, 0:win], LI(4, 64 * h, 64 * h + 64), xh, A.is_gt, ["L4_%d" % h, "RW", xk[h]] + (["RTa", "RTb"] if t else []), ["CR" + hs], "R")
+            wrap(bo, 128, T.WQ1, cr, 0, 64, ["WQ1", "CR" + hs], ["bOP" + hs], "a")
+            i1, i2, ix = T.IT[:, 64 * h:64 * h + 64], T.IT[:, 128 + 64 * h:192 + 64 * h], LI(10, 64 * h, 64 * h + 64)
+            act(a97, bo[:, 128:192], F.Copy, [], ["A97" + hs, "bOP" + hs], "a97", scale=97.0)
+            vtt(i1, a97, bo[:, 0:64], A.add, ["A97" + hs], ["XI1" + hs, "bOP" + hs], "i1", two=False)
+            vts(i2, i1, 2047, None, A.bitwise_and, None, ["XI1" + hs], ["XI2" + hs], "i2")
+            vcopy(ix, i2, ["XI2" + hs], ["IX" + hs], "ix")
+            gatherop(ss[:], T.EW[:], ix, xh, A.add, ["IX" + hs, "EW", xk[h]], ["SS" + hs], "env")
+            vts(mm[:], ss[:], 0.0, 256.0, A.is_lt, A.mult, ["SS" + hs], ["MM" + hs], "mm", half=True)
+
+    def send(srcs, out, dst, rs, ls, R, W, nm, kb):
+        rid, pid = topo.addr(dst)[0], topo.addr(dst)[1]
+        k = dict(dst_ids=[DstId(rid=rid, pnc=pid)], dma_engine_mask=topo.mask(core, dst), remote_sem=T.sem[rs])
+        tr = RemoteDMATransfer(srcs=srcs, dsts=[out], alu_op=1, **k) if len(srcs) > 1 else RemoteDMATransfer(src=srcs[0], dst=out, **k)
+        op([("gr", 1.0, lambda e: e.remote_dma_fused([tr], local_sem=T.sem[ls]))], R, [nm], nm, lat=kb / 60.0, tok=(ls, len(topo.engines(core, dst))))
+        op([("arr", 0.0, None)], [nm], W, nm + "arr", lat=2.5, tok=(rs, len(topo.engines(prv if dst == nxt else nxt, core))))
+
+    def splits(t):
+        win, off = (MW if t else 2048), LI(4, 0, 16)
+        gather(T.OQ[:], T.OW[:, 0:win], off, S, ["L4_0", "OW0", "OW1"], ["OQ"], "oq")
+        gather(T.KQ[:], T.KW[:, 0:win], off, S, ["L4_0"] + KWK + (KTK if t else []), ["KQ"], "kq")
+        gather(T.RF[:], T.RW[:, 0:win], off, S, ["L4_0", "RW"] + (["RTa", "RTb"] if t else []), ["RF"], "rf")
+        PE(lambda e: [e.matmul(T.bMI[:, 0:256], T.OB[:], T.OQ[:], True, True)], 256, ["OB", "OQ"], ["bMI"], "FR")
+        PE(lambda e: [e.matmul(T.bLP0[:, 256:512], T.OB[:], T.KQ[:], True, False),
+                      e.matmul(T.bLP0[:, 256:512], T.OBN[:], T.OQ[:], False, True)], 512, ["OB", "OBN", "OQ", "KQ"], ["bLP0"], "LD")
+        vts(T.FI[:], T.bMI[:, 0:256], col("sc"), None, A.mult, None, ["sc"], ["FI", "bMI"], "fi")
+        vts(T.LF[:], T.bLP0[:, 256:512], 0.0, None, A.is_equal, None, [], ["LF", "bLP0"], "lf")
+        vts(T.FB[:], T.FI[:], 2048, None, A.bitwise_and, None, ["FI"], ["FB"], "fb")
+        vtt(T.FBI[:], T.FB[:], T.BASE[:], A.add, ["FB", "BASE"], ["FBI"], "fbi")
+        for fx, c in (("FE", "me"), ("FO", "mo")):
+            op([("s", 0.28, lambda e, fx=fx, c=c: e.activation(T[fx][:], T.FBI[:], F.Copy, scale=col(c))),
+                ("v", 0.16, lambda e, fx=fx, c=c: e.tensor_scalar(T[fx][:], T.FBI[:], col(c), None, A.mult))], ["FBI", c], [fx], "fx")
+        for gr in range(8):
+            p0, fk, bn = 32 * (gr // 2), "FO" if gr % 2 else "FE", ("bTP1", "bSP", "bTP0", "bMI")[gr % 4]
+
+            def fn(e, p0=p0, fk=fk, bn=bn):
+                fx, fb = T[fk], T.FBI
+                return [e.matmul(T[bn][:, 0:128], fx[p0:p0 + 32, 0:128], fb[p0:p0 + 32, 0:128], True, True),
+                        e.matmul(T[bn][:, 128:384], fx[p0:p0 + 32, 128:256], fb[p0:p0 + 32, :], True, True)]
+            PE(fn, 384, [fk, "FBI"], [bn], "dot")
+
+            def fs(e, bn=bn, gr=gr):
+                return [e.activation(T.JK[:, 512 * (gr % 2) + a:512 * (gr % 2) + b], T[bn][:, a:b], F.Relu, bias=col("q%db" % hf),
+                                     accum_out=T.DM[:, 8 * hf + gr:8 * hf + gr + 1]) for hf, a, b in ((0, 0, 128), (1, 128, 384))]
+            op([("s", 0.5, fs)], ["q0b", "q1b"], ["JK%d" % (gr % 2), "DM%d" % gr, bn], "red")
+        vts(T.DUP[:], T.DM[:], 0.0, None, A.is_gt, None, ["DM%d" % b for b in range(8)], ["DUP"], "dup")
+        PE(lambda e: e.matmul(T.bLP1[0:16, 0:128], T.DUP[:], T.IDB[:], True, True), 128, ["DUP", "IDB"], ["bLP1"], "dupT")
+        op([("s", 0.17, lambda e: e.activation(T.DUT[:], T.bLP1[0:16, 0:128], F.Copy)), ("v", 0.16, lambda e: e.tensor_copy(T.DUT[:], T.bLP1[0:16, 0:128]))],
+           [], ["DUT", "bLP1"], "dut")
+        PE(lambda e: [e.matmul(T.bSP[:, 0:256], T.IDB[:], T.SS0[:, 0:S], True, False), e.matmul(T.bSP[:, 0:256], T.IDB[:], T.MM0[:, 0:S], False, True)],
+           512, ["IDB", "SS0", "MM0"], ["bSP"], "vv")
+        vtt(T.DR[:], T.RF[:], T.bSP[:, 0:256], A.subtract, ["RF"], ["DR", "bSP"], "dr", two=False)
+        vtt(T.RS1[:], T.RF[:], T.bSP[:, 0:256], A.add, ["RF", "bSP"], ["RS1"], "rs1", two=False)
+        act(T.AD[:], T.DR[:], F.Abs, ["DR"], ["AD"], "abs")
+
+        def fn3(e):
+            r = []
+            for hh in range(2):
+                o, sl = T.bMI[:, 128 * hh:128 * hh + 128], slice(128 * hh, 128 * hh + 128)
+                r.append(e.matmul(o, T.BLK[:], T.AD[:, sl], True, False))
+                r.append(e.matmul(o, T.I8K[:], T.LF[:, sl], False, False))
+                r.append(e.matmul(o, T.EH[:, sl], T.DUT[:], False, True))
+            return r
+        PE(fn3, 768, ["BLK", "AD", "I8K", "LF", "EH", "DUT"], ["bMI"], "far")
+        vts(T.SP[:], T.bMI[:, 0:256], T.THC[:], None, A.is_ge, None, ["THC"], ["SP", "bMI"], "sp")
+        RN, rn, c0 = (T.YR1, "YR1", 0) if t else (T.RW, "RT", 2048)
+        vts(T.RS2[:], T.RS1[:], 1, None, A.arith_shift_right, None, ["RS1"], ["RS2"], "rs2")
+        vtt(RN[:, c0:c0 + 512:2], T.RF[:], T.SP[:], A.mult, ["RF", "SP"], [rn + "a"], "rna")
+        vtt(RN[:, c0 + 1:c0 + 512:2], T.RS2[:], T.SP[:], A.mult, ["RS2", "SP"], [rn + "b"], "rnb")
+        wrap(T.bSP, 0, T.WQP, T.SP, 0, 16, ["SP", "WQP"], ["bSP"], "wsp")
+        vcopy(T.TG[:, 0:16], LI(4, 0, 16), ["L4_0"], ["TG0"])
+        vtt(T.TG[:, 16:32], T.TG[:, 0:16], T.DW[:], A.subtract, ["TG0", "DW"], ["TG1"])
+        vts(T.TG[:, 32:48], T.bSP[:, 0:16], 1.0, None, A.is_ge, None, [], ["TG2", "bSP"])
+        vtt(T.TG[:, 48:64], T.TG[:, 16:32], T.TG[:, 32:48], A.mult, ["TG1", "TG2"], ["TG3"])
+        vtt(T.TG[:, 64:80], T.TG[:, 48:64], T.DW[:], A.add, ["TG3", "DW"], ["TG4"])
+        vcopy(LI(11, 0, 16), T.TG[:, 64:80], ["TG4"], ["TGL"])
+
+        def scat(win_, val, R, W, nm):
+            op([("v", 0.05 + S * 3.5 * CYC, lambda e: e.tensor_copy(win_.indirect(LI(11, 0, 16)), val))], R + ["TGL"], W, nm)
+        if not t:
+            scat(T.KW[:], T.NK[:], ["NK"], KWK + KTK, "scK")
+            scat(T.ZW[:], T.XF[:], ["XF"], ["ZW", "ZT"], "scZ")
+        scat(T.KF[:], (T.NV1 if t else T.NV0)[:], ["NV1" if t else "NV0"], ["KF0", "KF1", "KFt"], "scF")
+
+    for k in range(4):
+        for h in range(2):
+            gather(T["XS%d" % k][:, HL * h:HL * h + HL], T.XW[:], LI(5 + k, 64 * h, 64 * h + 64), HL, ["XW", "SL%d_%d" % (k, h)], ["XS%d_%d" % (k, h)], "xs")
+        for h in range(2):
+            if k < 3:
+                gather(T["PT%d" % h][:], T.PW[:], LI(5 + k, 64 * h, 64 * h + 64), HL, ["PW0", "PW1", "SL%d_%d" % (k, h)], ["PT%d" % h], "pv")
+                wrap(T.bSP, 0, T.WQP, T["PT%d" % h], 0, 64, ["WQP", "PT%d" % h], ["bSP"], "ws")
+                vcopy(LI(6 + k, 64 * h, 64 * h + 64), T.bSP[:, 0:64], [], ["SL%d_%d" % (k + 1, h), "bSP"], "slist")
+        for h in range(2):
+            step(0, k, h, T["XS%d" % k], "XS%d_%d" % (k, h))
+    gather(T.PT2[:], T.PW[:], LI(8, 0, 16), S, ["PW0", "PW1", "SL3_0"], ["PT2"], "p4")
+    wrap(T.bSP, 0, T.WQP, T.PT2, 0, 16, ["WQP", "PT2"], ["bSP"], "ws4")
+    vcopy(T.SW[:, 64:80], T.bSP[:, 0:16], [], ["SW4", "bSP"])
+    for k in range(5):
+        vcopy(T.FW[:, 16 * k:16 * k + 16], LI(k, 0, 16), ["L%d_0" % k], ["FW%d" % k])
+        if k < 4:
+            vcopy(T.SW[:, 16 * k:16 * k + 16], LI(5 + k, 0, 16), ["SL%d_0" % k], ["SW%d" % k])
+    vtt(T.SFa[:], T.FW[:, 16:80], T.FW[:, 0:64], A.not_equal, ["FW%d" % k for k in range(5)], ["SFa"])
+    vtt(T.SFb[:], T.SW[:, 16:80], T.SW[:, 0:64], A.subtract, ["SW%d" % k for k in range(5)], ["SFb"])
+    vtt(T.SFa[:], T.SFa[:], T.SFb[:], A.mult, ["SFa", "SFb"], ["SFa"])
+    vtt(T.SFb[:, 0:32], T.SFa[:, 0:32], T.SFa[:, 32:64], A.add, ["SFa"], ["SFb"])
+    vtt(T.SFa[:, 0:16], T.SFb[:, 0:16], T.SFb[:, 16:32], A.add, ["SFb"], ["SFa"])
+    vtt(T.SFb[:, 32:48], T.SFa[:, 0:16], T.SW[:, 0:16], A.add, ["SFa", "SW0"], ["SFb"])
+    vcopy(LI(11, 32, 48), T.SFb[:, 32:48], ["SFb"], ["SFL"])
+    gather(T.XF[:], T.XW[:], LI(11, 32, 48), S, ["XW", "SFL"], ["XF"], "xf")
+
+    op([("s", 1.77, lambda e: e.activation(T.EW[:], T.EW[:], F.Copy, bias=-256.0)),
+        ("v", 0.9, lambda e: e.tensor_scalar(T.EW[:], T.EW[:], -256.0, None, A.add))], ["EW"], ["EW"], "env256")
+    outcome(0, T.XS0, ["XS0_0", "XS0_1"])
+    for h in range(2):
+        hs = str(h)
+        send([T["SS" + hs][:], T["MM" + hs][:]], T.VL[:, HL * h:HL * h + HL], nxt, "aA" + hs, "lA" + hs, ["SS" + hs, "MM" + hs], ["VL%d" % h], "send" + hs, 256)
+    vcopy(T.thF[:], T.thI[:], ["thI"], ["thF"])
+    PE(lambda e: e.matmul(T.bMI[:, 0:1], T.E8[:], T.thF[:], True, True), 256, ["E8", "thF"], ["bMI"], "th")
+    vts(T.THC[:], T.bMI[:, 0:1], BIG, None, A.add, None, [], ["THC", "bMI"])
+    vcopy(T.KDf[:], T.KD[:], ["KD0", "KD1"], ["KDf"])
+    DMA(T.KF[0:128:16, 0:2048], T.KDf[:, 0:128], ["KDf"], ["KF0"], "kf0", boost=-30.0)
+    DMA(T.KF[1:128:16, 0:2048], T.KDf[:, 128:256], ["KDf"], ["KF1"], "kf1", boost=-30.0)
+    splits(0)
+    DMA(T.yr[:, 0:512], T.RW[:, 2048:MW], ["RTa", "RTb"], ["oyr0"], "oyr0")
+    vcopy(T.cuF[:], T.cuI[:], ["cuI"], ["cuF"])
+    PE(lambda e: e.matmul(T.bLP1[:, 0:128], T.cuF[:], T.IDF[:], True, True), 512, ["cuF", "IDF"], ["bLP1"], "cuT")
+    act(T.cuT[:], T.bLP1[:, 0:128], F.Copy, [], ["cuT", "bLP1"], "cuT")
+    for gr in range(8):
+        DMA(T.CF[16 * gr:16 * gr + 1, :], T.cuT[:, 16 * gr:16 * gr + 16], ["cuT", "CF"], ["CF%d" % gr], "cf", kb=8)
+    send([T.wI[:]], T.wN[:], prv, "aw", "lw", ["wI"], ["wN"], "sendw", 1)
+    vcopy(col("wn"), T.wN[:], ["wN"], ["wn"])
+    act(T.WN8[:], T.BC8[:], F.Copy, ["BC8", "wn"], ["WN8"], "wn8", scale=col("wn"))
+
+    for h in range(2):
+        hs = str(h)
+        wrap(T["bOP" + hs], 64, T.WQW, T.VL, HL * h, 64, ["WQW", "VL%d" % h], ["bOP" + hs], "wh")
+        i1, i2 = T.IT[:, 256 + 64 * h:320 + 64 * h], T.IT[:, 384 + 64 * h:448 + 64 * h]
+        vcopy(i1, T["bOP" + hs][:, 64:128], [], ["HI1" + hs, "bOP" + hs], "h1")
+        vts(i2, i1, 2047, None, A.bitwise_and, None, ["HI1" + hs], ["HI2" + hs], "h2")
+        vcopy(LI(9, 64 * h, 64 * h + 64), i2, ["HI2" + hs], ["LH" + hs], "h3")
+    for k in range(4):
+        for h in range(2):
+            if k:
+                gather(T["YS%d" % k][:, HL * h:HL * h + HL], T["XS%d" % (k - 1)][:], LI(9, 64 * h, 64 * h + 64), HL,
+                       ["XS%d_0" % (k - 1), "XS%d_1" % (k - 1), "LH%d" % h], ["YS%d_%d" % (k, h)], "ys")
+        for h in range(2):
+            step(1, k, h, T["YS%d" % k] if k else T.VL, "YS%d_%d" % (k, h) if k else "VL%d" % h)
+    for h in range(2):
+        gather(T.HG[:, HL * h:HL * h + HL], T.CF[:], LI(9, 64 * h, 64 * h + 64), HL, ["CF"] + ["CF%d" % a for a in range(8)] + ["LH%d" % h], ["HG%d" % h], "cur")
+        DMA(T.yp[:, HL * h:HL * h + HL], T.HG[0:128:16, HL * h:HL * h + HL], ["HG%d" % h], ["oyp%d" % h], "oyp", kb=32)
+    outcome(1, T.VL, ["VL0", "VL1"])
+
+    def fnh(h):
+        def fn(e):
+            r = []
+            for j in range(8):
+                for a_, src in enumerate((T["SS%d" % h], T["MM%d" % h])):
+                    r.append(e.matmul(T.bOP0[:, 200 + 8 * h + j:328:16], src[:, 128 * j:128 * j + 128], T.WN8[:], a_ == 0, a_ == 1))
+            return r
+        return fn
+    for h in range(2):
+        PE(fnh(h), 1024, ["WN8", "SS%d" % h, "MM%d" % h], ["bOP0"], "hd")
+    i1, i2 = T.IT[:, 256:384], T.IT[:, 384:512]
+    vcopy(i1, T.bOP0[:, 200:328], [], ["HI10", "HI11", "bOP0"], "H1")
+    vts(i2, i1, 2047, None, A.bitwise_and, None, ["HI10", "HI11"], ["HI20", "HI21"], "H2")
+    vts(T.HFT[:], i2, 4096.0, None, A.add, None, ["HI20", "HI21"], ["HFT"], "H3")
+    PE(lambda e: e.matmul(T.bOP1[:, 256:384], T.HFT[:], T.IDF[:], True, True), 512, ["HFT", "IDF"], ["bOP1"], "HT")
+    op([("s", 0.17, lambda e: e.activation(T.HS[:], T.bOP1[:, 256:384], F.Copy)), ("v", 0.16, lambda e: e.tensor_copy(T.HS[:], T.bOP1[:, 256:384]))],
+       [], ["HS", "bOP1"], "H4")
+    send([T.HS[:]], T.HR[:], nxt, "aH", "lH", ["HS"], ["HR"], "sendH", 64)
+    DMA(T.yp[:, 2048:4096], T.HR[:], ["HR"], ["oyp2"], "oyp2")
+    splits(1)
+    DMA(T.yr[:, 512:1024], T.YR1[:], ["YR1a", "YR1b"], ["oyr1"], "oyr1", kb=128)
+    DMA(T.yk0[:], T.KF[0:128:16, 0:3072], ["KF0", "KFt"], ["oyk0"], "oyk0", kb=96)
+    DMA(T.yk1[:], T.KF[1:128:16, 0:3072], ["KF1", "KFt"], ["oyk1"], "oyk1", "s", kb=96)
+
+    if "order" not in PLANS:
+        PLANS["order"], PLANS["score"] = make_plan(ops)
+    eng = {"v": g.vector, "s": g.scalar, "t": g.tensor, "g": g, "y": g.sync}
+    cs = {"v": "cv", "s": "cs", "t": "ct", "g": "cg"}
+    cnt = dict((s_, 0) for s_ in cs.values())
+    known = dict((q, {}) for q in eng)
+    total, token = {}, [None] * len(ops)
+    for i, j in PLANS["order"]:
+        q, d, fn = ops[i]["alts"][j]
+        if q == "arr":
+            s_, v = ops[i]["tok"]
+            token[i] = (s_, v, {s_: v})
+            total[s_] = v
+            continue
+        r = q[0]
+        kn, e = known[r], eng[r]
+        need = {}
+        for dp in ops[i]["deps"]:
+            s_, v, ck = token[dp]
+            if kn.get(s_, 0) < v and need.get(s_, (0, None))[0] < v:
+                need[s_] = (v, ck)
+        for s_ in sorted(need, key=lambda s_: (-len(need[s_][1]), s_)):
+            v, ck = need[s_]
+            if kn.get(s_, 0) >= v:
+                continue
+            e.wait_ge(T.sem[s_], v)
+            for a, b in ck.items():
+                if kn.get(a, 0) < b:
+                    kn[a] = b
+        out = fn(e)
+        if q in cs:
+            for x in (out if isinstance(out, list) else [out]):
+                x.then_inc(T.sem[cs[q]], 1)
+                cnt[cs[q]] += 1
+            s_, v = cs[q], cnt[cs[q]]
+        else:
+            s_, v = ops[i]["tok"]
+        total[s_] = v
+        ck = dict(kn)
+        ck[s_] = v
+        token[i] = (s_, v, ck)
+    for s_ in sorted(total):
+        if known["g"].get(s_, 0) < total[s_]:
+            g.wait_ge(T.sem[s_], total[s_])

@@ -1,131 +1,169 @@
 from concourse.bass import DstId, RemoteDMATransfer
 from concourse.mybir import AluOpType as A, ActivationFunctionType as F
 
-S, HL = 256, 1024
+S = 256
 MW = 2560
-DUMP, WW = 3072, 3328
-BIG = 8192.0
-BFB, FP, I4, U2 = "bfloat16", "float32", "int32", "uint16"
+DUMP = 3072
+BIG, EOFF = 8192.0, 1280
+PARTS = ((0, 64), (64, 64))
+GP = 2
+RP = 1
+ENDS = ((2, 2), (1, 2))
+EARLY = 1
+BFB, FP, I4, U2, H2 = "bfloat16", "float32", "int32", "uint16", "float16"
 SCRATCH = {}
 
 
 def _decl(where, dtype, text):
     for w in text.split():
         nm, c = w.split(":")
-        p = 128
-        if "x" in c:
-            p, c = c.split("x")
-        SCRATCH[nm] = (where, [int(p), int(c)], dtype)
+        c = [int(x) for x in c.split("x")]
+        SCRATCH[nm] = (where, c if len(c) > 1 else [128] + c, dtype)
 
 
-_decl("sbuf", BFB, "XW:4096 PW:4096 ZW:3328 KW:3328 RW:2560 EW:2048 OW:2560 HIW:2560 VL:2048 KDl:256 KDh:256 PDl:256 PDh:256 ONB:128 ZB:256 "
-      "IDB:128 I8K:128 BC8:8 BLK:128 I4B:256 BASE:256 DR:256 WN8:8 EH:16x256 RHS:24 RT:8 OB:128 OBN:128 WQ1:2048 WQP:2048 WQW:2048 LOI:256 "
-      "HII:256 NK:256 NKb:256 YR1:512 XF:256 PT2:256 RF:256 KQ:256 OQ:256 FBI:256 FE:256 FO:256 LF:256 DUP:16 DUT:16x128 JK:1024 AD:256 SP:256 "
-      "XS0:2048 XS1:2048 XS2:2048 XS3:2048 YS1:2048 YS2:2048 YS3:2048 CK0:2048 CK1:2048 CR0:1024 CR1:1024 PT0:1024 PT1:1024 SS0:1024 SS1:1024 MM0:1024 MM1:1024")
-_decl("sbuf", FP, "KF:3328 CF:2048 HG:2048 thF:8x1 THC:1 KDf:256 cuF:128 cuT:128 ONF:128 IDF:128 E8:8x128 COL:32 CT:32x16 EQ:16x128 EQ2:32x128 DW:16 NV0:256 "
-      "NV1:256 FW:80 SW:80 SFa:64 SFb:64 HR:128 HS:128 HFT:128 DM:16 TG:80 A97:128 MA0:64x128 MA1:64x128 MB0:64x128 MB1:64x128 FT0:64x128 FT1:64x128")
-_decl("sbuf", I4, "stI:128 cuI:128 KD:256 PD:256 wI:1 wN:1 thI:8x1 KDt:256 KDu:256 PDt:256 PDu:256 FI:256 FB:256 RS1:256 RS2:256 IT:512")
-_decl("sbuf", U2, "LL:1536")
-_decl("psum", FP, "bMI:512 bSP:512 bTP0:512 bTP1:512 bLP0:512 bLP1:512 bOP0:512 bOP1:512")
-SEMAPHORES = ["cv", "cs", "ct", "cg"] + ["d%d" % _k for _k in range(48)] + ["aw", "lw", "aA0", "aA1", "lA0", "lA1", "aH", "lH"]
+_decl("sbuf", BFB, "XW:4096 PW:4608 RW:2560 EW:2048 LT:2048 PT1:2048 PT2:2048 LG:2048 CR:2048 CC:2048 WZ:864 PDb:512 OWb:512 ONB:128 ZB:320 "
+      "IDB:128 NI8:128 RK:16 BLK:128 E4:128 OB:128 SB:240 I4B:256 BASE:256 LM:128 YR1:512 PT3:256 OQ:256 FBI:256 FE:256 FO:256 "
+      "LF:256 JK:3072 AD:256 SP:256 MA:128 CST:2x128")
+_decl("sbuf", H2, "XS0:2048 VL:2048 SS:2048 MM:2048 CN:2048 W16:288 RHS:24 ID16:128 NI16:128 NI4:128 PI4:128 RF:256 U:256 E0:128x17x8 E1:128x17x8")
+_decl("sbuf", FP, "NW:3456 KF:3456 KDf:256 PERM:128 OWT:128 thF:8x2 THC:2 ONF:128 IDF:128 E8:8x128 COL:16 CT:32x16 EQ:16x128 EQ2:32x128 DW:16 NV0:256 NV1:256 "
+      "NC:256 WD:128 XF:256 Q2:256 FW:80 SW:80 SFa:64 SFb:64 HR:128 HS:128 YP:128 TG:32 MB:128 BD:4")
+_decl("sbuf", I4, "stI:128 cuI:128 KD:256 PD:256 KT:320 DI:256 QI:1280 wI:1 wN:1 thI:8x1 FI:256 FB:256 D2:256 D3:256 RS2:256 WC:128 IT:256 FT:128 FU:128")
+_decl("sbuf", U2, "LL:128x15x128")
+_decl("psum", FP, " ".join("b%d:512" % _k for _k in range(8)))
+SEMAPHORES = (["cv", "cs", "ct", "cg"] + ["d%d" % _k for _k in range(40)] + ["aw", "lw", "aH", "lH"]
+              + ["%s%d" % (_a, _k) for _a in ("aA", "lA") for _k in range(8)])
 
-CYC, GAT = 0.83e-3, 1.56
-WAKE, SELF, DBW, DLAT = 0.12, 0.08, 250.0, 2.0
-PREF = {"ki": 0, "xs": 0, "pv": 1, "ys": 0, "cu": 0}
-BETA, TRIES, PCF, SEED0 = 0.03, 6000, 1.15, 7
-MODELS = ((1.2, 1.0, 0.12, 1.0, 1.0), (1.2, 0.72, 0.25, 1.5, 1.3), (1.3, 1.25, 0.1, 0.8, 1.0))
+CYC = 0.83e-3
+BETA, TRIES, MOVES, SEED0, LAG, HEAT = 0.03, 100, 110000, 11, 3.0, 0.01
+MODELS = ((1.15, 1.4, 0.18, 1.0, 1.0), (1.4, 1.1, 0.22, 1.6, 1.3), (1.1, 1.9, 0.18, 1.3, 1.2))
+DLAT, RLAT, RBW, RFIRST, RCALL = 1.3, 1.8, 120.0, 2.0, 0.6
+SELF, TCYC, FIX = 0.07, 0.65, 0.052
 PLANS = {}
 
 
 def make_plan(ops):
     n = len(ops)
-    succ = [[] for _ in range(n)]
-    for i, o in enumerate(ops):
-        for d in o["deps"]:
+    deps = [sorted(o["deps"]) for o in ops]
+    succ, anc = [[] for _ in range(n)], [0] * n
+    for i in range(n):
+        for d in deps[i]:
             succ[d].append(i)
-    rq = [[a[0][0] if a[0] in ("yd", "sd", "gr") else a[0] for a in o["alts"]] for o in ops]
-    dma = [o["alts"][0][0] in ("yd", "sd") for o in ops]
+            anc[i] |= anc[d] | 1 << d
+    QI = dict((q, k) for k, q in enumerate("vstgya"))
+    kind = [o["alts"][0][0] for o in ops]
+    rq = [[QI[a[0][0]] for a in o["alts"]] for o in ops]
+    dur = [[[a[1] * (1.0 if a[0] in ("yd", "sd", "gr") else m[0]) + a[2] * m[1] for a in o["alts"]] for o in ops] for m in MODELS]
+    chan = [1 if k in ("yd", "sd") else 2 if k == "gr" else 0 for k in kind]
+    lat = [o["lat"] for o in ops]
+    pre = [[(DLAT - 0.3) * m[4] if c == 1 else 0.0 for c in chan] for m in MODELS]
+    on = [[lat[i] * m[3] if chan[i] else 0.0 for i in range(n)] for m in MODELS]
+    post = [[0.3 if chan[i] else lat[i] * m[4] if kind[i] == "arr" else m[2] for i in range(n)] for m in MODELS]
+    norm = [m[0] * 30 + m[1] * 25 + 15 for m in MODELS]
     pri = [0.0] * n
     for i in range(n - 1, -1, -1):
-        o = ops[i]
-        pri[i] = min(a[1] for a in o["alts"]) + o["lat"] + (DLAT if dma[i] else 0.0) + max([pri[j] + WAKE for j in succ[i]] or [0.0])
+        pri[i] = min(dur[0][i]) + pre[0][i] + on[0][i] + post[0][i] + max([pri[j] for j in succ[i]] or [0.0])
 
-    def schedule(boost, pick, beta):
-        left, ready = [len(o["deps"]) for o in ops], [0.0] * n
+    def schedule(boost, pick):
+        du, left, ready = dur[0], [len(d) for d in deps], [0.0] * n
         open_ = [i for i in range(n) if not left[i]]
-        free, order, bw = {}, [], 0.0
+        free, order, alt, ch = [0.0] * 6, [], [0] * n, [0.0, 0.0, RFIRST]
+        p = [BETA * (pri[i] + boost[i]) for i in range(n)]
         while open_:
-            best = None
+            bk = 1e9
             for i in open_:
-                p = pri[i] + boost[i]
-                for j in range(len(rq[i])):
-                    if pick[i] >= 0 and pick[i] != j:
-                        continue
-                    st = ready[i] if rq[i][j] == "arr" else max(ready[i], free.get(rq[i][j], 0.0))
-                    key = (st - beta * p, -p, i, j)
-                    if best is None or key < best[0]:
-                        best = (key, i, j, st)
-            _, i, j, st = best
-            open_.remove(i)
-            q, d = rq[i][j], ops[i]["alts"][j][1] * (PCF if rq[i][j] in "vstg" else 1.0)
-            if q != "arr":
-                free[q] = st + d
-            fin = st + d + ops[i]["lat"]
-            if dma[i]:
-                bw = max(bw, st + d) + ops[i]["lat"]
-                fin = bw + DLAT
-            order.append((i, j))
-            for s_ in succ[i]:
-                ready[s_] = max(ready[s_], fin + (SELF if rq[s_] == [q] else WAKE))
+                for j, q in enumerate(rq[i]):
+                    if pick[i] < 0 or pick[i] == j:
+                        st = max(free[q], ready[i])
+                        if st - p[i] < bk:
+                            bk, bi, bj, bs = st - p[i], i, j, st
+            open_.remove(bi)
+            e = bs + du[bi][bj]
+            if rq[bi][bj] < 5:
+                free[rq[bi][bj]] = e
+            if chan[bi]:
+                e = ch[chan[bi]] = max(ch[chan[bi]], e + pre[0][bi]) + on[0][bi]
+            order.append(bi)
+            alt[bi] = bj
+            for s_ in succ[bi]:
+                ready[s_] = max(ready[s_], e + (SELF if not chan[bi] and rq[s_] == [rq[bi][bj]] else post[0][bi]))
                 left[s_] -= 1
                 if not left[s_]:
                     open_.append(s_)
-        return order
+        return order, alt
+    near = [[d for d in deps[i] if not any(anc[x] >> d & 1 for x in deps[i])] for i in range(n)]
+    NM, GAP = len(MODELS), 16
 
-    def score(order, watch):
-        tot, way = 0.0, []
-        for mi, (cf, gf, wk, bf, lf) in enumerate(MODELS):
-            fin, free, bw, mx, end = [0.0] * n, {}, 0.0, 0.0, 0
-            prev, why = {}, [None] * n
-            for i, j in order:
-                o, q = ops[i], rq[i][j]
-                d = o["alts"][j][1]
-                if q in "vstg" and not dma[i]:
-                    d *= cf * (gf if o["gat"] else 1.0)
-                t = 0.0 if q == "arr" else free.get(q, 0.0)
-                w = (prev.get(q), True)
-                for x in o["deps"]:
-                    if fin[x] + wk > t:
-                        t = fin[x] + wk
-                        w = (x, False)
-                why[i], prev[q] = w, i
-                e = t + d
-                if q != "arr":
-                    free[q] = e
-                if dma[i]:
-                    bw = max(bw, e) + o["lat"] / bf
-                    e = bw + DLAT * lf
-                else:
-                    e += o["lat"] * lf
-                fin[i] = e
-                if e > mx:
-                    mx, end = e, i
-            tot += mx / (cf * (1 + gf))
-            if mi == watch:
-                x = end
-                while x is not None:
-                    way.append((x, why[x][0] if why[x][1] else None))
-                    x = why[x][0]
-        return tot, way
-    boost, pick = [o["boost"] for o in ops], [o["pref"] for o in ops]
-    two = [i for i in range(n) if len(rq[i]) == 2]
-    order = schedule(boost, pick, BETA)
+    def length(order, alt, own, mi, old=None, at=0):
+        du, pr, o_, po, gain = dur[mi], pre[mi], on[mi], post[mi], MODELS[mi][2] - SELF
+        at //= GAP
+        if old:
+            fin, why, keep = old[1][:], old[2][:], old[3][:at + 1]
+        else:
+            fin, why, keep = [0.0] * n, [0] * n, [[0.0] * 9 + [RFIRST]]
+        free = keep[at][:]
+        for k in range(at * GAP, n, GAP):
+            for i in order[k:k + GAP]:
+                j = alt[i]
+                q = rq[i][j]
+                t = free[q]
+                w = -1
+                for x in near[i]:
+                    f = fin[x]
+                    if f > t:
+                        if own[x] == q:
+                            f -= gain
+                            if f <= t:
+                                continue
+                        t = f
+                        w = x
+                t += du[i][j]
+                if q < 5:
+                    free[q] = t
+                c = chan[i]
+                if c:
+                    t += pr[i]
+                    if c == 2:
+                        t += free[9]
+                        free[9] = 0.0
+                    if free[5 + c] > t:
+                        t = free[5 + c]
+                        w = -2
+                    t += o_[i]
+                    free[5 + c] = t
+                t += po[i]
+                fin[i] = t
+                why[i] = w
+            keep.append(free[:])
+        return max(fin) / norm[mi], fin, why, keep
+
+    def owners(alt):
+        return [-1 if chan[i] else rq[i][alt[i]] for i in range(n)]
+
+    def score(order, alt):
+        return [length(order, alt, owners(alt), mi) for mi in range(NM)]
+
+    def longest(order, alt, st):
+        before, prev = [None] * n, [None] * 9
+        for i in order:
+            q = rq[i][alt[i]]
+            before[i] = prev[q if st[2][i] == -1 else 6 + chan[i]]
+            prev[q] = prev[6 + chan[i]] = i
+        x, way = st[1].index(max(st[1])), []
+        while x is not None:
+            w = st[2][x]
+            way.append((x, before[x] if w < 0 else None))
+            x = before[x] if w < 0 else w
+        return way
     seed = [SEED0]
-    best, way = score(order, 0)
 
     def rnd():
         seed[0] = (seed[0] * 1103515245 + 12345) % 2147483648
         return seed[0] / 2147483648.0
+    boost, pick = [o["boost"] for o in ops], [o["pref"] for o in ops]
+    two = [i for i in range(n) if len(rq[i]) == 2]
+    order, alt = schedule(boost, pick)
+    st = score(order, alt)
+    best, way = sum(x[0] for x in st), longest(order, alt, st[0])
     for it in range(TRIES):
         b2, p2 = list(boost), list(pick)
         share, amp = 0.02 + 0.4 * rnd() ** 2, 1.0 + 12.0 * rnd()
@@ -133,19 +171,60 @@ def make_plan(ops):
             if before is not None and rnd() < share:
                 b2[i] += amp * rnd()
                 b2[before] -= amp * rnd()
-        if rnd() < 0.5:
-            for i in two:
-                if rnd() < 0.04:
-                    p2[i] = int(3 * rnd()) - 1
-        if rnd() < 0.3:
-            for i in range(n):
-                if rnd() < 0.04:
-                    b2[i] += amp * (2 * rnd() - 1)
-        o2 = schedule(b2, p2, BETA)
-        s2, w2 = score(o2, int(rnd() * len(MODELS)))
-        if s2 <= best:
-            best, order, boost, pick, way = s2, o2, b2, p2, w2
-    return order, best
+        for i in two:
+            if rnd() < 0.02:
+                p2[i] = int(3 * rnd()) - 1
+        o2, a2 = schedule(b2, p2)
+        s2 = score(o2, a2)
+        if sum(x[0] for x in s2) <= best:
+            best, order, alt, boost, pick, st = sum(x[0] for x in s2), o2, a2, b2, p2, s2
+            way = longest(order, alt, st[int(rnd() * NM)])
+    now, keep, own = best, (order, alt), owners(alt)
+    for it in range(MOVES):
+        r, o2, a2, w2 = rnd(), order, alt, own
+        i, b = way[int(rnd() * len(way))]
+        if r < 0.15:
+            if len(rq[i]) < 2:
+                i = two[int(rnd() * len(two))]
+            a2, w2, pb = list(alt), list(own), order.index(i)
+            a2[i] = 1 - alt[i]
+            w2[i] = -1 if chan[i] else rq[i][a2[i]]
+        else:
+            if r < 0.3 or b is None:
+                pi = int(rnd() * n)
+                i = order[pi]
+                pb = pi - 1
+                skip = int(3 * rnd())
+                while pb >= 0 and (rq[order[pb]][alt[order[pb]]] != rq[i][alt[i]] or skip):
+                    skip -= rq[order[pb]][alt[order[pb]]] == rq[i][alt[i]]
+                    pb -= 1
+                if pb < 0:
+                    continue
+                b = order[pb]
+            else:
+                pi, pb = order.index(i), order.index(b)
+            if anc[i] >> b & 1:
+                continue
+            mid = order[pb:pi + 1]
+            if rnd() < 0.5:
+                up = [x for x in mid if x == i or anc[i] >> x & 1]
+                rest = [x for x in mid if not (x == i or anc[i] >> x & 1)]
+            else:
+                rest = [x for x in mid if x == b or anc[x] >> b & 1]
+                up = [x for x in mid if not (x == b or anc[x] >> b & 1)]
+            o2 = order[:pb] + up + rest + order[pi + 1:]
+        room, s2 = HEAT * (1.0 - it / MOVES) * rnd() ** 3, []
+        for mi in range(NM):
+            s2.append(length(o2, a2, w2, mi, st[mi], pb))
+            room -= s2[mi][0] - st[mi][0]
+            if room < -0.004 * (NM - 1 - mi):
+                break
+        else:
+            now, order, alt, own, st = sum(x[0] for x in s2), o2, a2, w2, s2
+            way = longest(order, alt, st[int(rnd() * NM)])
+            if now < best:
+                best, keep = now, (order, alt)
+    return [(i, keep[1][i]) for i in keep[0]], best
 
 
 def rank_program(g, core, T, topo):
@@ -155,11 +234,19 @@ def rank_program(g, core, T, topo):
     n_ranks = len(T.cores)
     nxt, prv = T.cores[(rank + 1) % n_ranks], T.cores[(rank - 1) % n_ranks]
     ops, last, readers, fore = [], {}, {}, [0.0]
+    allp = range(len(PARTS))
+    bP, bC, bQ, bS = ["b0", "b1"], ["b2", "b3"], ["b4", "b5"], ["b6", "b7"]
 
-    def LI(k, a, b):
-        return T.LL[:, 128 * k + a:128 * k + b]
+    def LI(k, a, n):
+        return T.LL[:, k, a:a + n]
 
-    def op(alts, R, W, nm="", lat=0.0, tok=None, boost=0.0, gat=False, pref=-1):
+    def ZW(a, b):
+        return T.PW[:, a:b]
+
+    def QT(a, b, step=1):
+        return T.PW[:, 2048 + a:2048 + b:step]
+
+    def op(alts, R, W, nm="", lat=0.0, tok=None, boost=0.0, pref=-1):
         i, deps = len(ops), set()
         for k in list(R) + list(W):
             if k in last:
@@ -172,400 +259,498 @@ def rank_program(g, core, T, topo):
             last[k] = i
             readers[k] = []
         deps.discard(i)
-        ops.append(dict(alts=alts, deps=deps, nm=nm, lat=lat, tok=tok, boost=boost + (fore[0] if alts[0][0] in "vstg" else 0.0), gat=gat, pref=pref))
+        ops.append(dict(alts=alts, deps=deps, nm=nm, lat=lat, tok=tok, boost=boost + fore[0], pref=pref))
+
+    def width(ap):
+        n = 1
+        for x in ap.shape[1:]:
+            n *= x
+        return n
 
     def vc(n, half=False):
-        return 0.05 + max(64, n * (0.5 if half else 1)) * CYC
+        return FIX + max(64, n * (0.5 if half else 1)) * CYC
 
     def PE(fn, cyc, R, W, nm=""):
-        op([("t", 0.05 + cyc * CYC, fn)], R, W, nm)
+        op([("t", cyc * CYC * TCYC, 0.0, fn)], R, W, nm)
     nd = [0]
 
-    def DMA(out, in_, R, W, nm="", q="y", kb=64, boost=0.0):
+    def DMA(out, in_, R, W, nm, kb, row, boost=0.0):
         s = "d%d" % nd[0]
         nd[0] += 1
-        op([(q + "d", 0.07, lambda e: e.dma_start(out, in_).then_inc(T.sem[s], 16))], R, W, nm, lat=kb / DBW, tok=(s, 16), boost=boost)
+        us = -(-(kb * 1024 // row) // 16) * (0.02 + row / 40000.0)
+        op([(q, 0.06, 0.0, lambda e: e.dma_start(out, in_).then_inc(T.sem[s], 16)) for q in ("yd", "sd")], R, W, nm, lat=us, tok=(s, 16),
+           boost=boost - fore[0], pref=0)
 
-    def vcopy(out, in_, R, W, nm=""):
-        op([("v", vc(out.shape[1]), lambda e: e.tensor_copy(out, in_))], R, W, nm)
+    def ts(out, in0, s1, s2, o0, o1=None):
+        if o1 is None:
+            return lambda e: e.tensor_scalar(out, in0, s1, None, o0)
+        return lambda e: e.tensor_scalar(out, in0, s1, s2, o0, o1)
 
     def vts(out, in0, s1, s2, o0, o1, R, W, nm="", half=False):
-        if o1 is None:
-            op([("v", vc(out.shape[1], half), lambda e: e.tensor_scalar(out, in0, s1, None, o0))], R, W, nm)
-        else:
-            op([("v", vc(out.shape[1], half), lambda e: e.tensor_scalar(out, in0, s1, s2, o0, o1))], R, W, nm)
+        op([("v", vc(width(out), half), 0.0, ts(out, in0, s1, s2, o0, o1))], R, W, nm)
 
     def vtt(out, i0, i1, o, R, W, nm="", two=True):
-        op([("v", vc(out.shape[1] * (2 if two else 1)), lambda e: e.tensor_tensor(out, i0, i1, o))], R, W, nm)
+        op([("v", vc(width(out) * (2 if two else 1)), 0.0, lambda e: e.tensor_tensor(out, i0, i1, o))], R, W, nm)
 
-    def act(out, in_, func, R, W, nm="", **k):
-        op([("s", 0.065 + max(64, in_.shape[1]) * CYC, lambda e: e.activation(out, in_, func, **k))], R, W, nm)
+    def lin(out, in_, scale, bias, R, W, nm="", half=False):
+        n, f = width(in_), F.Copy if isinstance(bias, float) else F.Identity
+        op([("s", vc(n), 0.0, lambda e: e.activation(out, in_, f, scale=scale, bias=bias)),
+            ("v", vc(n, half), 0.0, ts(out, in_, scale, bias, A.mult, A.add))], R, W, nm)
 
-    def gather(out, win, off, n, R, W, nm):
-        d = n * GAT * CYC
-        a = [("s", 0.07 + d, lambda e: e.activation(out, win.indirect(off), F.Copy)),
-             ("v", 0.06 + d, lambda e: e.tensor_copy(out, win.indirect(off)))]
-        op(a, R, W, nm, gat=True, pref=PREF.get(nm[:2], -1))
+    def cp(out, in_, R, W, nm="", half=False):
+        n = width(in_)
+        op([("s", vc(n), 0.0, lambda e: e.activation(out, in_, F.Copy)), ("v", vc(n, half), 0.0, lambda e: e.tensor_copy(out, in_))], R, W, nm)
+
+    def gather(out, win, off, R, W, nm):
+        d = out.shape[1] * CYC
+        op([("s", 0.055, d, lambda e: e.activation(out, win.indirect(off), F.Copy)),
+            ("v", 0.042, d, lambda e: e.tensor_copy(out, win.indirect(off)))], R, W, nm, pref=0)
 
     def gatherop(out, win, off, in1, o, R, W, nm):
-        op([("v", 0.06 + HL * GAT * CYC, lambda e: e.tensor_tensor(out, win.indirect(off), in1, o))], R, W, nm, gat=True)
+        op([("v", 0.042, out.shape[1] * CYC, lambda e: e.tensor_tensor(out, win.indirect(off), in1, o))], R, W, nm)
 
     def ms(ap, c, W, half=True):
-        op([("v", vc(ap.shape[1], half), lambda e: e.memset(ap, c))], [], W, "ms")
+        op([("v", vc(width(ap), half), 0.0, lambda e: e.memset(ap, c))], [], W, "ms")
+
+    def zero(out, W):
+        n = out.shape[1]
+        op([("s", vc(n), 0.0, lambda e: e.activation(out, T.ZB[:, 0:n], F.Copy)), ("v", vc(n, True), 0.0, lambda e: e.memset(out, 0.0))], ["ZB"], W, "zero")
 
     def cnt_(pat):
         n = 1
         for a_, b_ in pat:
             n *= b_
-        return 0.15 + 2 * n * CYC
+        return 2 * n * CYC
 
     def aff(out, in_, pat, cmpo, fill, base, cm, R, W):
-        op([("g", cnt_(pat), lambda e: e.affine_select(out, in_, pat, cmpo, fill, base, cm))], R, W)
+        op([("g", 0.17 + cnt_(pat), 0.0, lambda e: e.affine_select(out, in_, pat, cmpo, fill, base, cm))], R, W, "aff")
 
-    def iota(out, pat, base, cm, W, R=()):
-        op([("g", cnt_(pat), lambda e: e.iota(out, pat, base, cm, allow_small_or_imprecise_dtypes=True))], R, W)
+    def iota(out, pat, base, cm, W, whole=False):
+        k = {} if whole else dict(allow_small_or_imprecise_dtypes=True)
+        op([("g", 0.13 + cnt_(pat), 0.0, lambda e: e.iota(out, pat, base, cm, **k))], [], W, "iota")
 
-    B, KWK, KTK = 90.0, ["KW0", "KW1", "KW2", "KW3"], ["KT0", "KT1", "KT2", "KT3"]
-    DMA(T.KD[:, 0:128], T.kid0[:], [], ["KD0"], "kid0", "y", boost=B)
-    DMA(T.PD[:], T.prev[:], [], ["PD"], "prev", "s", 128, boost=B)
-    DMA(T.KD[:, 128:256], T.kid1[:], [], ["KD1"], "kid1", "y", boost=B - 1)
-    DMA(T.cuI[:], T.cur[:], [], ["cuI"], "cur", "s", boost=B - 1)
-    DMA(T.stI[:], T.start[:], [], ["stI"], "start", "y", boost=B - 2)
-    DMA(T.XW[:], T.x[:], [], ["XW"], "x", "s", 1024, boost=B - 60)
-    DMA(T.ZW[:, 0:2048], T.z[:], [], ["ZW"], "z", "y", 512, boost=B - 70)
-    DMA(T.wI[:], T.w[:], [], ["wI"], "w", "y", 1, boost=B - 3)
-    DMA(T.thI[:], T.th[:], [], ["thI"], "th", "y", 1, boost=B - 7)
+    def put(out, step, vals, R, W):
+        n = out.shape[1]
+        src, rd = T.ZB[:, 0:n], ["ZB"] + R
+        for k, v in vals:
+            aff(out, src, [[-step, n]], A.not_equal, float(v), -k, 1, rd, [W])
+            src, rd = out, [W]
+
+    B = 90.0
+    DMA(T.KD[:, 0:128], T.kid0[:], [], ["KD0"], "kid0", 64, 512, B)
+    DMA(T.KD[:, 128:256], T.kid1[:], [], ["KD1"], "kid1", 64, 512, B)
+    DMA(ZW(0, 1024), T.z[:, 0:1024], [], ["ZW0"], "z0", 256, 2048, B - 1)
+    DMA(ZW(1024, 2048), T.z[:, 1024:2048], [], ["ZW1"], "z1", 256, 2048, B - 2)
+    DMA(T.stI[:], T.start[:], [], ["stI"], "start", 64, 512, B - 4)
+    DMA(T.cuI[:], T.cur[:], [], ["cuI"], "cur", 64, 512, B - 5)
+    DMA(T.XW[:], T.x[:], [], ["XW"], "x", 1024, 8192, B - 6)
+    DMA(T.PD[:], T.prev[:], [], ["PD"], "prev", 128, 1024, B - 20)
+    DMA(T.wI[:], T.w[:], [], ["wI"], "w", 1, 8, B - 40)
+    DMA(T.thI[:], T.th[:], [], ["thI"], "th", 1, 64, B - 60)
 
     fore[0] = 80.0
-    ms(T.ONB[:], 1.0, ["ONB"])
     ms(T.ZB[:], 0.0, ["ZB"])
-    ms(T.WQP[:], 0.0, ["WQP"])
-    fore[0] = 0.0
-    ms(T.PW[:], 0.0, ["PW0", "PW1"])
-    fore[0] = 60.0
-    act(T.KW[:, 0:2048], T.WQP[:], F.Copy, ["WQP"], KWK, "zero")
-    fore[0] = 0.0
     ms(T.ONF[:], 1.0, ["ONF"], half=False)
-    ms(T.ZW[:, 2048:MW], 0.0, ["ZT"])
-    fore[0] = 70.0
-    aff(T.BC8[:], T.ONB[:, 0:8], [[-16, 8]], A.is_ge, 0.0, 0, 1, ["ONB"], ["BC8"])
-    aff(T.BC8[:], T.BC8[:], [[16, 8]], A.is_ge, 0.0, 15, -1, ["BC8"], ["BC8"])
+    ms(T.ONB[:], 1.0, ["ONB"])
+    aff(T.PERM[:], T.ONF[:], [[-1, 16], [-16, 8]], A.is_equal, 0.0, 0, 1, ["ONF"], ["PERM"])
+    put(T.RK[:], 8, [(k, -8 ** (k + 1)) for k in range(4)], [], "RK")
+    fore[0] = 60.0
+    for k in range(4, 8):
+        zero(QT(k, MW, 8), ["QT%d_%d" % (c, k) for c in range(3)])
+    iota(T.OWT[:], [[128, 16], [0, 8]], 0, 1, ["OWT"])
+    aff(T.IDB[:], T.ONB[:], [[-1, 128]], A.is_equal, 0.0, 0, 1, ["ONB"], ["IDB"])
+    put(T.NI8[:], 1, [(0, -0.125)], [], "NI8")
+    fore[0] = 20.0
+    ms(T.WZ[:], 0.0, ["WZ"])
+    ZS = dict([(nm, (T.WZ, 144 * j)) for j, nm in enumerate(("one", "p0", "p2", "p4", "a97", "big"))]
+              + [(nm, (T.W16, 144 * j)) for j, nm in enumerate(("w", "wn"))])
+
+    def slot(nm):
+        return ZS[nm][0][:, ZS[nm][1] + 15:ZS[nm][1] + 143:16]
+    BC8 = slot("one")
+    aff(BC8, T.ONB[:, 0:8], [[-16, 8]], A.is_ge, 0.0, 0, 1, ["ONB", "WZ"], ["Zone"])
+    aff(BC8, BC8, [[16, 8]], A.is_ge, 0.0, 15, -1, ["Zone"], ["Zone"])
+    put(slot("p0"), 16, ((0, 1), (1, 1)), ["WZ"], "Zp0")
+    iota(T.OWb[:, 0:256], [[1, 256]], 0, 0, ["OWl"])
+    iota(T.OWb[:, 256:512], [[0, 256]], 0, 256, ["OWh"])
+    cp(T.RHS[:, 0:8], T.RK[:, 1:16:2], ["RK"], ["RHa"])
+    cp(T.RHS[:, 8:16], T.RK[:, 0:16:2], ["RK"], ["RHb"])
+    vtt(T.RHS[:, 16:24], T.RK[:, 1:16:2], T.RK[:, 0:16:2], A.subtract, ["RK"], ["RHc"])
+    iota(T.CST[:, 0:64], [[0, 64]], 1536 * 4096, -1536 * 4096 - EOFF, ["CSa"])
+    iota(T.CST[:, 64:128], [[0, 64]], 0, 0, ["CSb"])
+    lin(T.NI4[:], T.IDB[:], -4096.0, 0.0, ["IDB"], ["NI4"], "cst", True)
+    lin(T.PI4[:], T.IDB[:], 4096.0, 0.0, ["IDB"], ["PI4"], "cst", True)
+    cp(T.ID16[:], T.IDB[:], ["IDB"], ["ID16"], "cst", True)
+    for p in allp:
+        cp(T["E%d" % p][:], T.ZB[:, 0:136], ["ZB"], ["E%d" % p], "zero", True)
     fore[0] = 0.0
     aff(T.IDF[:], T.ONF[:], [[-1, 128]], A.is_equal, 0.0, 0, 1, ["ONF"], ["IDF"])
+    cp(T.W16[:], T.ZB[:, 0:288], ["ZB"], ["W16"], "zero", True)
+    iota(T.KT[:, 256:320], [[128, 4], [0, 16]], 2048, 1, ["KT2"], True)
+    put(slot("p2"), 16, ((2, 1), (3, 1)), ["WZ"], "Zp2")
+    put(slot("p4"), 16, ((4, 1), (5, 1)), ["WZ"], "Zp4")
+    put(slot("big"), 16, ((0, -BIG),), ["WZ"], "Zbig")
+    lin(slot("a97"), BC8, 97.0, 0.0, ["Zone", "WZ"], ["Za97"], "cst")
+    lin(T.NI16[:], T.IDB[:], -1.0, 0.0, ["IDB"], ["NI16"], "cst", True)
     aff(T.BLK[:], T.ONB[:], [[-16, 8], [0, 16]], A.is_ge, 0.0, 0, 1, ["ONB"], ["BLK"])
     aff(T.BLK[:], T.BLK[:], [[16, 8], [0, 16]], A.is_ge, 0.0, 15, -1, ["BLK"], ["BLK"])
-    iota(T.KW[:, 2048:MW], [[0, MW - 2048]], 0, 0, KTK)
-    fore[0] = -60.0
-    iota(T.OW[:], [[0, 10], [1, 256]], 0, 0, ["OW0", "OW1"])
-    iota(T.HIW[:], [[1, 10], [0, 256]], 0, 0, ["HIW"])
-    fore[0] = 0.0
-    iota(T.I4B[:], [[4, 256]], 0, 0, ["I4B"])
-    aff(T.EH[:], T.ZB[0:16, :], [[-8, 2], [-1, 8], [0, 16]], A.not_equal, -BIG, 0, 1, ["ZB"], ["EH"])
+    aff(T.E4[:], T.ZB[:, 0:128], [[-16, 8], [0, 16]], A.not_equal, -BIG / 2, -4, 1, ["ZB"], ["E4"])
+    aff(T.OB[:], T.ZB[:, 0:128], [[-16, 8], [0, 16]], A.not_equal, 1.0, -4, 1, ["ZB"], ["OB"])
+    aff(T.OB[:], T.OB[:], [[-16, 8], [0, 16]], A.not_equal, 1.0, -5, 1, ["OB"], ["OB"])
+    aff(T.SB[:], T.ZB[:, 0:240], [[1, 15], [0, 16]], A.not_equal, -BIG, -7, 0, ["ZB"], ["SB"])
+    iota(T.I4B[:], [[4, 256]], 4, 0, ["I4B"])
     aff(T.E8[:], T.ONF[0:8, :], [[-1, 8], [0, 16]], A.is_equal, 0.0, 0, 1, ["ONF"], ["E8"])
-    iota(T.DW[:], [[16, 16]], DUMP, 0, ["DW"])
+    iota(T.thF[:, 1:2], [[0, 1]], -4096, -4096, ["thG"])
+    iota(T.DW[:], [[16, 16]], DUMP, 1, ["DW"])
     iota(T.NV0[:], [[2, 256]], 2048, 0, ["NV0"])
-    iota(T.LOI[:], [[0, 2], [2, 128]], 0, 0, ["LOI"])
-    iota(T.HII[:], [[1, 2], [0, 128]], 8, 0, ["HII"])
+    iota(T.NC[:], [[2, 256]], 2048, 0, ["NC"])
+    iota(T.BD[:, 0:2], [[128, 2]], 1, 1, ["BD"])
+    ms(T.WD[:], 0.0, ["WD"], half=False)
+    for k in range(1, 4):
+        for j in range(k):
+            aff(T.WD[:, k:128:8], T.WD[:, k:128:8], [[-8, 16]], A.not_equal, float(8 ** (j + 4 - k)), -j, 1, ["WD"], ["WD"])
     fore[0] = -60.0
     iota(T.KF[:, 2048:3072], [[1, 1024]], 2048, 0, ["KFt"])
-    iota(T.CF[:], [[0, 2048]], 0, 0, ["CF"])
+    fore[0] = 0.0
 
-    TAB = {"k": (), "e1": ((1, 1),), "e2": ((2, 1),), "e02": ((0, 1), (2, 1)), "e13": ((1, 1), (3, 1)), "pc": ((0, 1), (1, 256)),
-           "pn": ((0, -1), (1, -256)), "sc": tuple((k, 2 ** (11 - k)) for k in range(12)), "e12": ((12, 1),), "c12": ()}
+    TAB = {"e1": ((1, 1),), "sc": tuple((k, 2 ** (11 - k)) for k in range(12)), "e12": ((12, 1),), "c12": (),
+           "s8": tuple((k + o, 8 ** (3 - k)) for o in (0, 8) for k in range(4)), "b8": tuple((k + 8, 8 ** (3 - k)) for k in range(4))}
     NT = len(TAB)
-    C = dict((nm, j) for j, nm in enumerate(list(TAB) + ["me", "mo", "q0b", "q1b", "p", "q0", "q1", "w", "wn"]))
+    CI = dict((nm, j) for j, nm in enumerate(list(TAB) + ["me", "mo", "w", "wn"]))
 
     def col(nm):
-        return T.COL[:, C[nm]:C[nm] + 1]
-    fore[0] = 40.0
-    ms(T.CT[:], 0.0, ["CT" + nm for nm in C], half=False)
-    fore[0] = 0.0
+        return T.COL[:, CI[nm]:CI[nm] + 1]
+    ms(T.CT[:], 0.0, ["CT" + nm for nm in CI], half=False)
     for nm in TAB:
-        c, ck = T.CT[0:16, C[nm]:C[nm] + 1], ["CT" + nm]
-        if nm == "k":
-            iota(c, [[0, 1]], 0, 1, ck)
+        c, ck = T.CT[0:16, CI[nm]:CI[nm] + 1], ["CT" + nm]
         if nm == "c12":
             aff(c, c, [[0, 1]], A.is_equal, -1024.0, -12, 1, ck, ck)
         for k, v in TAB[nm]:
             aff(c, c, [[0, 1]], A.not_equal, float(v), -k, 1, ck, ck)
     u = 2.0 ** -20
     for nm, o in (("me", 0), ("mo", 16)):
-        c, ck = T.CT[:, C[nm]:C[nm] + 1], ["CT" + nm]
-        aff(c, c, [[0, 1]], A.is_gt, u, 16 if o else -11, -1 if o else 1, ck, ck)
-        for k, v in ((12, -u), (13, -5.5 * u), (14, -5.5 * u)) + (((15, 0.0),) if o else ()):
+        c, ck = T.CT[:, CI[nm]:CI[nm] + 1], ["CT" + nm]
+        aff(c, c, [[0, 1]], A.is_gt, u, 16 if o else -12, -1 if o else 1, ck, ck)
+        for k, v in ((13, -5.5 * u), (14, -5.5 * u)) + (((15, 0.0),) if o else ()):
             aff(c, c, [[0, 1]], A.not_equal, v, -k - o, 1, ck, ck)
     aff(T.EQ[:], T.ONF[0:16, :], [[0, 8], [1, 16]], A.is_equal, 0.0, 0, -1, ["ONF"], ["EQ"])
     aff(T.EQ2[:], T.ONF[0:32, :], [[0, 4], [1, 32]], A.is_equal, 0.0, 0, -1, ["ONF"], ["EQ2"])
-    PE(lambda e: [e.matmul(T.bMI[:, 0:NT], T.EQ[:], T.CT[0:16, 0:NT], True, True), e.matmul(T.bMI[:, NT:NT + 2], T.EQ2[:], T.CT[:, NT:NT + 2], True, True)],
-       512, ["EQ", "EQ2"] + ["CT" + nm for nm in C], ["bMI"], "cols")
-    op([("s", 0.12, lambda e: e.activation(T.COL[:, 0:NT + 2], T.bMI[:, 0:NT + 2], F.Copy))], [], list(TAB) + ["me", "mo", "bMI"], "cols")
-    iota(col("p"), [[0, 1]], 0, 1, ["p"])
-    for nm, ad in (("q0", 0.0), ("q1", 128.0)):
-        act(col(nm), col("p"), F.Copy, ["p"], [nm], "q", scale=1.0 / 256, bias=ad / 256)
-        act(col(nm), col(nm), F.Square, [nm], [nm], "q")
-        act(col(nm + "b"), col(nm), F.Copy, [nm], [nm + "b"], "q", bias=-1.0)
-    act(T.BASE[:], T.I4B[:], F.Identity, ["I4B", "e12", "c12"], ["BASE"], "base", scale=col("e12"), bias=col("c12"))
 
-    def fills(out, vals, W):
-        src, rd = T.ZB[:, 0:8], "ZB"
-        for k, v in vals:
-            aff(out, src, [[-16, 8]], A.not_equal, v, -k, 1, [rd], [W])
-            src, rd = out, W
-    fore[0] = 80.0
-    fills(T.RT[:, 0:8], ((0, 1.0), (1, 256.0)), "P01")
-    fore[0] = 60.0
-    iota(T.WQ1[:], [[0, 2048]], 0, 0, ["WQ1"], ["P01"])
+    fore[0] = 30.0
+    cp(T.KDf[:], T.KD[:], ["KD0", "KD1"], ["KDf"])
+    bk = T[bS[0]]
+    PE(lambda e: [e.matmul(bk[:, j:256:2], T.KDf[:, 128 * j:128 * j + 128], T.PERM[:], True, True) for j in range(2)], 1024, ["KDf", "PERM"], [bS[0]], "kT")
+    cp(T.KT[:, 0:256], bk[:, 0:256], [], ["KT0", "KT1", bS[0]], "KT")
+    vtt(T.LM[:], bk[:, 0:256:2], T.OWT[:], A.is_equal, ["OWT"], ["LM", bS[0]], "LM", two=False)
+    lin(QT(4, 2048, 16), T.LM[:], 2560.0, 0.0, ["LM"], ["QT0_4", "QT1_4"], "LM", True)
+
+    def digits(c, a, n, src, sk, ks):
+        for k in ks:
+            qi = T.QI[:, 320 * k + a:320 * k + a + n]
+            vts(qi, src[:, a:a + n], 3 * k, 7, A.arith_shift_right, A.bitwise_and, sk, ["QI%d_%d" % (x, k) for x in c], "dig")
+            cp(QT(8 * a + k, 8 * (a + n), 8), qi, ["QI%d_%d" % (x, k) for x in c], ["QT%d_%d" % (x, k) for x in c], "dig")
+    digits((0, 1), 0, 256, T.KT, ["KT0", "KT1"], (0,))
+    NWK, nb = ["NW%d" % j for j in range(4)], bP + bC
+    for j in range(4):
+        PE(lambda e, j=j: e.matmul(T[nb[j]][:, 0:512], T.IDB[:], ZW(512 * j, 512 * j + 512), True, False), 512, ["IDB", "ZW%d" % (j // 2)], [nb[j]], "nz")
+    for c in range(2):
+        bz = (bS[1], bQ[1])[c]
+        PE(lambda e, c=c, bz=bz: [e.matmul(T[bz][:, 16 * b:16 * b + 16], ZW(1024 * c + 128 * b, 1024 * c + 128 * b + 128), T.RK[:], True, True) for b in range(8)],
+           512, ["ZW%d" % c, "RK"], [bz], "zD")
+        vtt(T.DI[:, 128 * c:128 * c + 128], T.KT[:, 128 * c:128 * c + 128], T[bz][:, 0:128], A.subtract, ["KT%d" % c], ["DI%d" % c, bz], "DI", two=False)
+        digits((c,), 128 * c, 128, T.DI, ["DI%d" % c], (1, 2, 3))
+        for j in (2 * c, 2 * c + 1):
+            PE(lambda e, j=j: [e.matmul(T[nb[j]][:, 128 * i:128 * i + 128], QT(512 * j + 128 * i, 512 * j + 128 * i + 128), T.NI8[:], False, i == 3)
+                               for i in range(4)], 512, ["NI8"] + ["QT%d_%d" % (c, k) for k in range(8)], [nb[j]], "nq")
+            cp(T.NW[:, 512 * j:512 * j + 512], T[nb[j]][:, 0:512], [], ["NW%d" % j, nb[j]], "nw")
     fore[0] = 0.0
-    fills(T.RHS[:, 8:16], ((0, 0.5), (1, 128.0), (2, 0.5), (3, 128.0)), "RHSb")
-    fills(T.RHS[:, 16:24], ((0, -1.0), (1, -256.0), (2, 1.0), (3, 256.0)), "RHSd")
-    act(T.RHS[:, 0:8], T.BC8[:], F.Copy, ["BC8"], ["RHSa"], "rhs")
-    RH = ["RHSa", "RHSb", "RHSd"]
+    ms(QT(2052, 2560, 16), 2560.0, ["QT2_4"])
+    digits((2,), 256, 64, T.KT, ["KT2"], range(4))
+    PE(lambda e: [e.matmul(bk[:, 128 * i:128 * i + 128], QT(2048 + 128 * i, 2176 + 128 * i), T.NI8[:], True, True) for i in range(4)],
+       512, ["NI8"] + ["QT2_%d" % k for k in range(8)], [bS[0]], "nq")
+    cp(T.NW[:, 2048:MW], bk[:, 0:512], [], ["NT", bS[0]], "nw")
 
-    def fillq(dst, src, R, W):
-        op([("s", 16 * (0.065 + 64 * CYC), lambda e: [e.activation(dst[:, 129 * q:128 * q + 128:16], src, F.Copy) for q in range(16)])], R + W, W, "fill")
-    fore[0] = 60.0
-    fillq(T.WQP, T.RT[:, 0:8], ["P01"], ["WQP"])
-    fore[0] = 0.0
-    fillq(T.WQ1, T.BC8[:], ["BC8"], ["WQ1"])
-    vcopy(col("w"), T.wI[:], ["wI"], ["w"])
-    op([("s", 1.77, lambda e: e.activation(T.WQW[:], T.WQ1[:], F.Copy, scale=col("w"))),
-        ("v", 0.9, lambda e: e.tensor_scalar(T.WQW[:], T.WQ1[:], col("w"), None, A.mult))], ["WQ1", "w"], ["WQW"], "WQW")
-    act(T.IDB[:], T.IDF[:], F.Copy, ["IDF"], ["IDB"], "cst")
-    act(T.I8K[:], T.IDF[:], F.Copy, ["IDF"], ["I8K"], "cst", scale=BIG)
-    act(T.OB[:], T.BLK[:], F.Copy, ["BLK", "pc"], ["OB"], "cst", scale=col("pc"))
-    act(T.OBN[:], T.BLK[:], F.Copy, ["BLK", "pn"], ["OBN"], "cst", scale=col("pn"))
-    act(T.DW[:], T.DW[:], F.Identity, ["DW", "k"], ["DW"], "cst", bias=col("k"))
-    act(T.NV0[:], T.NV0[:], F.Identity, ["NV0", "e1"], ["NV0"], "cst", bias=col("e1"))
-    act(T.NV1[:], T.NV0[:], F.Copy, ["NV0"], ["NV1"], "cst", bias=512.0)
-    act(T.NK[:], T.LOI[:], F.Identity, ["LOI", "e02", "e2"], ["NK"], "cst", scale=col("e02"), bias=col("e2"))
-    act(T.NKb[:], T.HII[:], F.Copy, ["HII", "e13"], ["NKb"], "cst", scale=col("e13"))
-    vtt(T.NK[:], T.NK[:], T.NKb[:], A.add, ["NK", "NKb"], ["NK"])
+    cp(LI(0, 0, 128), T.stI[:], ["stI"], ["L0_%d" % p for p in allp])
+    cp(LI(5, 0, 128), T.cuI[:], ["cuI"], ["L5_%d" % p for p in allp])
+    cp(T.PDb[:, 0:256], T.PD[:], ["PD"], ["PDh"])
+    vtt(T.PDb[:, 256:512], T.PD[:], T.PDb[:, 0:256], A.subtract, ["PD", "PDh"], ["PDl"])
+    op([("arr", 0.0, 0.0, None)], [], ["ZW0", "ZW1", "PWf"] + ["QT%d_%d" % (c, k) for c in range(2) for k in range(8)], "free")
+    DMA(T.PW[0:128:16, 0:4096], T.PDb[:, 0:256], ["PDh", "PWf"], ["PW0"], "pw0", 64, 512)
+    DMA(T.PW[1:128:16, 0:4096], T.PDb[:, 256:512], ["PDl", "PWf"], ["PW1"], "pw1", 64, 512)
+    DMA(T.PW[4:128:16, 0:4096], T.OWb[:, 0:256], ["OWl", "PWf"], ["PW4"], "pw4", 64, 512)
+    DMA(T.PW[5:128:16, 0:4096], T.OWb[:, 256:512], ["OWh", "PWf"], ["PW5"], "pw5", 64, 512)
+    PWK, PWIN = ["PW0", "PW1", "PW4", "PW5"], T.PW[:, 0:4096]
+    DMA(T.RW[:, 0:2048], T.rs[:], ["PWf"], ["RW"], "rs", 512, 4096, -200.0)
+    DMA(T.EW[:], T.env[:], ["PWf"], ["EW"], "env", 512, 4096, -210.0)
+    cp(col("w"), T.wI[:], ["wI"], ["w"])
+    lin(slot("w"), BC8, col("w"), 0.0, ["W16", "Zone", "w"], ["Zw"], "Zw")
 
-    vcopy(LI(0, 0, 128), T.stI[:], ["stI"], ["L0_0", "L0_1"])
-    vcopy(LI(5, 0, 128), T.cuI[:], ["cuI"], ["SL0_0", "SL0_1"])
-    vts(T.PDt[:], T.PD[:], 255, None, A.bitwise_and, None, ["PD"], ["PDt"])
-    vts(T.PDu[:], T.PD[:], 8, None, A.arith_shift_right, None, ["PD"], ["PDu"])
-    vcopy(T.PDl[:], T.PDt[:], ["PDt"], ["PDl"])
-    vcopy(T.PDh[:], T.PDu[:], ["PDu"], ["PDh"])
-    DMA(T.PW[0:128:16, :], T.PDl[:], ["PDl"], ["PW0"], "pw0")
-    DMA(T.PW[1:128:16, :], T.PDh[:], ["PDh"], ["PW1"], "pw1")
-    vts(T.KDt[:], T.KD[:], 255, None, A.bitwise_and, None, ["KD0", "KD1"], ["KDt"])
-    vts(T.KDu[:], T.KD[:], 8, None, A.arith_shift_right, None, ["KD0", "KD1"], ["KDu"])
-    vcopy(T.KDl[:], T.KDt[:], ["KDt"], ["KDl"])
-    vcopy(T.KDh[:], T.KDu[:], ["KDu"], ["KDh"])
-    DMA(T.KW[0:128:16, 0:2048], T.KDl[:, 0:128], ["KDl"], ["KW0"], "kw0", kb=32)
-    DMA(T.KW[1:128:16, 0:2048], T.KDh[:, 0:128], ["KDh"], ["KW1"], "kw1", kb=32)
-    DMA(T.KW[2:128:16, 0:2048], T.KDl[:, 128:256], ["KDl"], ["KW2"], "kw2", kb=32)
-    DMA(T.KW[3:128:16, 0:2048], T.KDh[:, 128:256], ["KDh"], ["KW3"], "kw3", kb=32)
-    DMA(T.RW[:, 0:2048], T.rs[:], ["KDl", "KDh", "PDl", "PDh"], ["RW"], "rs", "y", 512, boost=-200.0)
-    DMA(T.EW[:], T.env[:], ["KDl", "KDh", "PDl", "PDh"], ["EW"], "env", "y", 512, boost=-210.0)
-    DMA(T.OW[1:128:16, :], T.HIW[0:8, :], ["HIW", "KDh"], ["OW1"], "ow1", kb=40, boost=-220.0)
-    DMA(T.KW[0:128:16, 2048:MW], T.OW[0:128:16, 2048:MW], ["OW0"], ["KT0"], "kt0", kb=8, boost=-220.0)
-    DMA(T.KW[1:128:16, 2048:MW], T.HIW[0:8, 2048:MW], ["HIW"], ["KT1"], "kt1", kb=8, boost=-220.0)
-    DMA(T.KW[2:128:16, 2048:MW], T.OW[0:128:16, 2048:MW], ["OW0"], ["KT2"], "kt2", kb=8, boost=-220.0)
-    DMA(T.KW[3:128:16, 2048:MW], T.HIW[0:8, 2048:MW], ["HIW"], ["KT3"], "kt3", kb=8, boost=-220.0)
+    bc = T[bS[1]]
+    PE(lambda e: [e.matmul(bc[:, 0:NT], T.EQ[:], T.CT[0:16, 0:NT], True, True), e.matmul(bc[:, NT:NT + 2], T.EQ2[:], T.CT[:, NT:NT + 2], True, True)],
+       512, ["EQ", "EQ2"] + ["CT" + nm for nm in CI], [bS[1]], "cols")
+    cp(T.COL[:, 0:NT + 2], bc[:, 0:NT + 2], [], list(TAB) + ["me", "mo", bS[1]], "cols")
+    op([("s", vc(2), 0.0, lambda e: e.activation(T.BD[:, 2:4], T.BD[:, 0:2], F.Square)),
+        ("v", vc(2), 0.0, lambda e: e.tensor_tensor(T.BD[:, 2:4], T.BD[:, 0:2], T.BD[:, 0:2], A.mult))], ["BD"], ["BD2"], "bd")
+    lin(T.BD[:, 0:2], T.BD[:, 2:4], -1.0, -65536.0, ["BD2"], ["BD"], "bd")
+    lin(T.BASE[:], T.I4B[:], col("e12"), col("c12"), ["I4B", "e12", "c12"], ["BASE"], "base", True)
+    lin(T.NV0[:], T.NV0[:], 1.0, col("e1"), ["e1"], ["NV0"], "cst")
+    lin(T.NV1[:], T.NV0[:], 1.0, 512.0, ["NV0"], ["NV1"], "cst")
+    lin(T.NC[:], T.NC[:], col("s8"), col("b8"), ["s8", "b8"], ["NC"], "cst")
+    cp(T.thF[:, 0:1], T.thI[:], ["thI"], ["thF"])
+    PE(lambda e: e.matmul(bc[:, 0:2], T.E8[:], T.thF[:], True, True), 256, ["E8", "thF", "thG"], [bS[1]], "th")
+    lin(T.THC[:], bc[:, 0:2], 1.0, BIG / 2, [], ["THC", bS[1]])
+    GOFF = T.THC[:, 1:2]
 
-    def wrap(bank, c0, wq, src, s0, n, R, W, nm):
-        PE(lambda e: [e.matmul(bank[:, c0:c0 + n], wq[:, 128 * q:128 * q + 128], src[:, s0 + q:s0 + 16 * n:16], q == 0, q == 15) for q in range(16)],
-           16 * max(64, n), R, W, nm)
+    def wrap(bank, o, z, src, c0, C, R, nm, first=True, end=True, more=()):
+        wz, z0 = ZS[z]
+        PE(lambda e: [f(e) for f in more] + [e.matmul(T[bank][:, o:o + C], wz[:, z0 + 15 - q:z0 + 143 - q], src[:, 16 * c0 + q:16 * (c0 + C):16],
+                                                      first and q == 0, end and q == 15) for q in range(16)],
+           1024 + 256 * len(more), ["Z" + z] + R, [bank], nm)
 
-    def step(t, k, h, X, xk):
-        hs, win = str(h), (MW if t else 2048)
-        ck, tp, lp, tk = T["CK" + hs], T["bTP" + hs], T["bLP" + hs], "bTP" + hs
-        off, lk = LI(k, 64 * h, 64 * h + 64), ["L%d_%d" % (k, h)]
-        gather(ck[:, 0:HL], T.KW[:, 0:win], off, HL, lk + KWK + (KTK if t else []), ["CKk" + hs], "kid")
-        gatherop(ck[:, HL:2 * HL], T.ZW[:, 0:win], off, X[:, HL * h:HL * h + HL], A.is_le, lk + ["ZW", xk] + (["ZT"] if t else []), ["CKz" + hs], "z")
-        PE(lambda e: [e.matmul(tp[:, q:384:16], ck[:, q:2 * HL:16], T.RHS[:], True, True) for q in range(16)], 1024, ["CKk" + hs, "CKz" + hs] + RH, [tk], "T")
-        ma, mb_, ft = T["MA" + hs], T["MB" + hs], T["FT" + hs]
-        vts(ma[:], tp[64:128, 0:128], 8.5, 0.5, A.is_ge, A.subtract, [], ["MA" + hs, tk], "m")
-        vtt(mb_[:], ma[:], tp[0:64, 256:384], A.mult, ["MA" + hs, tk], ["MB" + hs], "t", two=False)
-        vtt(ft[:], mb_[:], tp[0:64, 128:256], A.add, ["MB" + hs, tk], ["FT" + hs], "f", two=False)
-        PE(lambda e: e.matmul(lp[:, 0:64], ft[:, 0:128], T.IDF[0:64, 0:64], True, True), 256, ["FT" + hs, "IDF"], ["bLP" + hs], "tr")
-        vcopy(LI(k + 1, 64 * h, 64 * h + 64), lp[:, 0:64], [], ["L%d_%d" % (k + 1, h), "bLP" + hs], "list")
+    def rows(bank, z, src, m0, m1, first, end, R, nm):
+        wz, z0 = ZS[z]
+        PE(lambda e: [e.matmul(T[bank][:, 0:128], wz[:, z0 + 15 - m:z0 + 143 - m], src[:, 128 * m:128 * m + 128], first and m == m0, end and m == m1 - 1)
+                      for m in range(m0, m1)], 128 * (m1 - m0), R + ["Z" + z], [bank], nm)
 
-    def outcome(t, X, xk):
-        win = MW if t else 2048
-        for h in range(2):
-            wrap(T["bOP%d" % h], 0, T.WQW, X, HL * h, 64, ["WQW", xk[h]], ["bOP%d" % h], "wc")
-        for h in range(2):
-            hs = str(h)
-            bo, cr, ss, mm = T["bOP" + hs], T["CR" + hs], T["SS" + hs], T["MM" + hs]
-            xh, a97 = X[:, HL * h:HL * h + HL], T.A97[:, 64 * h:64 * h + 64]
-            gatherop(cr[:], T.RW[:, 0:win], LI(4, 64 * h, 64 * h + 64), xh, A.is_gt, ["L4_%d" % h, "RW", xk[h]] + (["RTa", "RTb"] if t else []), ["CR" + hs], "R")
-            wrap(bo, 128, T.WQ1, cr, 0, 64, ["WQ1", "CR" + hs], ["bOP" + hs], "a")
-            i1, i2, ix = T.IT[:, 64 * h:64 * h + 64], T.IT[:, 128 + 64 * h:192 + 64 * h], LI(10, 64 * h, 64 * h + 64)
-            act(a97, bo[:, 128:192], F.Copy, [], ["A97" + hs, "bOP" + hs], "a97", scale=97.0)
-            vtt(i1, a97, bo[:, 0:64], A.add, ["A97" + hs], ["XI1" + hs, "bOP" + hs], "i1", two=False)
-            vts(i2, i1, 2047, None, A.bitwise_and, None, ["XI1" + hs], ["XI2" + hs], "i2")
-            vcopy(ix, i2, ["XI2" + hs], ["IX" + hs], "ix")
-            gatherop(ss[:], T.EW[:], ix, xh, A.add, ["IX" + hs, "EW", xk[h]], ["SS" + hs], "env")
-            vts(mm[:], ss[:], 0.0, 256.0, A.is_lt, A.mult, ["SS" + hs], ["MM" + hs], "mm", half=True)
+    def sums(e, bank, src, c0, C, wts, alone):
+        return [e.matmul(T[bank][0:2 * C, r:8 * wts.shape[1]:8], src[:, 16 * c0 + r:16 * (c0 + C):8], wts, alone, alone) for r in range(8)]
+
+    def lanes(X, c0, C):
+        return X[:, 16 * c0:16 * (c0 + C)]
+
+    def cut(c0, C, n):
+        at = [c0 + 8 * (C // 8 * j // n) for j in range(n)] + [c0 + C]
+        return [("_%d" % j, at[j], at[j + 1] - at[j]) for j in range(n)]
+    came = []
+
+    def vl(a, n):
+        return [nm for nm, c0, C in came if c0 < a + n and a < c0 + C]
+
+    def step(t, k, p):
+        c0, C = PARTS[p]
+        ps, win, nr = str(p), (MW if t else 2048), 2 * C
+        tp, tc, nk = T[bP[p]], T[bC[p]], NWK + (["NT"] if t else [])
+        lk, pcs = ["L%d_%d" % (k, p)], cut(c0, C, GP)
+        for nm, a, n in pcs:
+            nt, ct, nm = lanes(T.CN, a, n), lanes(T.CC, a, n), ps + nm
+            gather(nt, T.NW[:, 0:win], LI(k, a, n), lk + nk, ["CN" + nm], "node")
+            if k or not t:
+                sl = (11 if t else 5) + k
+                gatherop(ct, T.XW[:], LI(sl, a, n), nt, A.is_ge, ["XW", "L%d_%d" % (sl, p), "CN" + nm], ["CC" + nm], "cmp")
+            else:
+                gatherop(ct, T.NW[:, 0:win], LI(k, a, n), lanes(T.VL, a, n), A.is_le, lk + nk + vl(a, n), ["CC" + nm], "cmp")
+        cn = ["CN" + ps + x[0] for x in pcs]
+        if not EARLY:
+            PE(lambda e: sums(e, bP[p], T.CN, c0, C, T.RHS[:, 8:24], True), 512, ["RHb", "RHc"] + cn, [bP[p]], "kid")
+            PE(lambda e: sums(e, bC[p], T.CC, c0, C, BC8, True), 512, ["Zone"] + ["CC" + ps + x[0] for x in pcs], [bC[p]], "count")
+            ma, mb_, ft, fu = (T[x][0:nr, 64 * p:64 * p + 64] for x in ("MA", "MB", "FT", "FU"))
+            vts(ma, tc[0:nr, 0:64], 8.5, None, A.is_ge, None, [], ["MA" + ps, bC[p]], "m")
+            vtt(mb_, ma, tp[0:nr, 64:128], A.mult, ["MA" + ps], ["MB" + ps, bP[p]], "t", two=False)
+            vtt(ft, mb_, tp[0:nr, 0:64], A.add, ["MB" + ps], ["FT" + ps, bP[p]], "f", two=False)
+            vts(fu, ft, 4095, None, A.bitwise_and, None, ["FT" + ps], ["FU" + ps], "and")
+            lin(T["E" + ps][0:nr, 1:17:2, :], fu, 1.0, -float(EOFF), ["FU" + ps], ["E" + ps], "e")
+            PE(lambda e: [e.matmul(tc[:, 64:64 + C], T["E" + ps][0:nr, 1 - h:17 - h, :], T.ID16[0:nr, h:nr:2], h == 0, h == 1) for h in range(2)],
+               128, ["ID16", "E" + ps], [bC[p]], "turn")
+            lin(LI(k + 1, c0, C), tc[:, 64:64 + C], 1.0, float(EOFF), [], ["L%d_%d" % (k + 1, p), bC[p]], "list")
+            return
+        PE(lambda e: sums(e, bC[p], T.CN, c0, C, T.RHS[:, 0:16], True), 512, ["RHa", "RHb"] + cn, [bC[p]], "kid")
+        PE(lambda e: [e.matmul(tp[0:nr, 0:128], T.ONB[0:2, 0:nr], T.CST[:], True, False)] + sums(e, bP[p], T.CN, c0, C, T.RHS[:, 8:24], False),
+           640, ["ONB", "CSa", "CSb", "RHb", "RHc"] + cn, [bP[p]], "kid")
+        lin(T.U[0:nr, 128 * p:128 * p + 128], tc[0:nr, 0:128], 1.0 / 4096, 1536 - EOFF / 4096.0, [], ["U" + ps, bC[p]], "u")
+        PE(lambda e: [e.matmul(tp[0:nr, o:o + 64], w[0:nr, 0:nr], T.U[0:nr, 128 * p + a:128 * p + a + 64], False, w is T.PI4)
+                      for o, w, a in ((0, T.NI4, 64), (64, T.NI4, 0), (64, T.PI4, 64))], 192, ["NI4", "PI4", "U" + ps], [bP[p]], "fix")
+        PE(lambda e: sums(e, bC[p], T.CC, c0, C, BC8, True), 512, ["Zone"] + ["CC" + ps + x[0] for x in pcs], [bC[p]], "count")
+        ma, mb_ = T.MA[0:nr, 64 * p:64 * p + 64], T.MB[0:nr, 64 * p:64 * p + 64]
+        vts(ma, tc[0:nr, 0:64], 8.5, None, A.is_ge, None, [], ["MA" + ps, bC[p]], "m")
+        vtt(mb_, ma, tp[0:nr, 64:128], A.mult, ["MA" + ps], ["MB" + ps, bP[p]], "t", two=False)
+        vtt(T["E" + ps][0:nr, 1:17:2, :], mb_, tp[0:nr, 0:64], A.add, ["MB" + ps], ["E" + ps, bP[p]], "f", two=False)
+        PE(lambda e: [e.matmul(tc[:, 64:64 + C], T["E" + ps][0:nr, 1 - h:17 - h, :], T.ID16[0:nr, h:nr:2], h == 0, h == 1) for h in range(2)],
+           128, ["ID16", "E" + ps], [bC[p]], "turn")
+        lin(LI(k + 1, c0, C), tc[:, 64:64 + C], 1.0, float(EOFF), [], ["L%d_%d" % (k + 1, p), bC[p]], "list")
+
+    def low(p, num, nk, out, W):
+        c0, C = PARTS[p]
+        fu = T.FU[:, c0:c0 + C]
+        vts(fu, num, 2047, None, A.bitwise_and, None, [nk], ["FU%d" % p], "and")
+        cp(out, fu, ["FU%d" % p], W, "list")
+
+    def outcome(t, p, after):
+        win, X, (c0, C) = (MW if t else 2048), (T.VL if t else T.XS0), PARTS[p]
+        nm, again, rk = str(t) + str(p), ["o%d" % p] if t else [], []
+        for n2, a, n in cut(c0, C, RP):
+            gatherop(lanes(T.CR, a, n), T.RW[:, 0:win], LI(4, a, n), lanes(X, a, n), A.is_gt,
+                     ["L4_%d" % p, "RW"] + (vl(a, n) + ["RTa", "RTb"] if t else ["XS%d" % p]) + again, ["CR" + nm + n2], "R")
+            rk.append("CR" + nm + n2)
+        i1, acc = T.FT[:, c0:c0 + C], T[bP[p]][:, 0:C]
+        if t:
+            wrap(bP[p], 0, "a97", T.CR, c0, C, rk, "a")
+            vtt(i1, T.WC[:, c0:c0 + C], acc, A.add, ["WC%d" % p], ["FT%d" % p, bP[p]], "i1", two=False)
+        else:
+            wrap(bP[p], 0, "w", T.XS0, c0, C, ["XS%d" % p], "wc", end=False)
+            wrap(bP[p], 0, "a97", T.CR, c0, C, rk, "a", first=False)
+            cp(i1, acc, [], ["FT%d" % p, bP[p]], "i1")
+        low(p, i1, "FT%d" % p, LI(10, c0, C), ["IX" + nm])
+        for n2, a, n in cut(c0, C, ENDS[t][p]):
+            n2 = nm + n2
+            gatherop(lanes(T.SS, a, n), T.EW[:], LI(10, a, n), lanes(X, a, n), A.add, ["IX" + nm, "EW"] + (vl(a, n) if t else ["XS%d" % p]) + again, ["SS" + n2], "env")
+            vts(lanes(T.MM, a, n), lanes(T.SS, a, n), 256.0, -256.0, A.is_ge, A.mult, ["SS" + n2], ["MM" + n2], "mm", half=True)
+            after(n2, a, n)
 
     def send(srcs, out, dst, rs, ls, R, W, nm, kb):
         rid, pid = topo.addr(dst)[0], topo.addr(dst)[1]
         k = dict(dst_ids=[DstId(rid=rid, pnc=pid)], dma_engine_mask=topo.mask(core, dst), remote_sem=T.sem[rs])
         tr = RemoteDMATransfer(srcs=srcs, dsts=[out], alu_op=1, **k) if len(srcs) > 1 else RemoteDMATransfer(src=srcs[0], dst=out, **k)
-        op([("gr", 1.0, lambda e: e.remote_dma_fused([tr], local_sem=T.sem[ls]))], R, [nm], nm, lat=kb / 60.0, tok=(ls, len(topo.engines(core, dst))))
-        op([("arr", 0.0, None)], [nm], W, nm + "arr", lat=2.5, tok=(rs, len(topo.engines(prv if dst == nxt else nxt, core))))
+        op([("gr", RCALL, 0.0, lambda e: e.remote_dma_fused([tr], local_sem=T.sem[ls]))], R, [nm], nm, lat=max(0.35, kb / RBW), tok=(ls, len(topo.engines(core, dst))))
+        op([("arr", 0.0, 0.0, None)], [nm], W, nm + "arr", lat=RLAT - 0.3, tok=(rs, len(topo.engines(prv if dst == nxt else nxt, core))))
 
     def splits(t):
-        win, off = (MW if t else 2048), LI(4, 0, 16)
-        gather(T.OQ[:], T.OW[:, 0:win], off, S, ["L4_0", "OW0", "OW1"], ["OQ"], "oq")
-        gather(T.KQ[:], T.KW[:, 0:win], off, S, ["L4_0"] + KWK + (KTK if t else []), ["KQ"], "kq")
-        gather(T.RF[:], T.RW[:, 0:win], off, S, ["L4_0", "RW"] + (["RTa", "RTb"] if t else []), ["RF"], "rf")
-        PE(lambda e: [e.matmul(T.bMI[:, 0:256], T.OB[:], T.OQ[:], True, True)], 256, ["OB", "OQ"], ["bMI"], "FR")
-        PE(lambda e: [e.matmul(T.bLP0[:, 256:512], T.OB[:], T.KQ[:], True, False),
-                      e.matmul(T.bLP0[:, 256:512], T.OBN[:], T.OQ[:], False, True)], 512, ["OB", "OBN", "OQ", "KQ"], ["bLP0"], "LD")
-        vts(T.FI[:], T.bMI[:, 0:256], col("sc"), None, A.mult, None, ["sc"], ["FI", "bMI"], "fi")
-        vts(T.LF[:], T.bLP0[:, 256:512], 0.0, None, A.is_equal, None, [], ["LF", "bLP0"], "lf")
+        win, off, nk = (MW if t else 2048), LI(4, 0, 16), NWK + (["NT"] if t else [])
+        vk, far = ["SS%d0_0" % t, "MM%d0_0" % t], T[bC[0]]
+        gather(T.OQ[:], PWIN, off, ["L4_0"] + PWK, ["OQ"], "oq")
+        op([("s", 0.055, S * CYC, lambda e: e.activation(T.LF[:], T.NW[:, 0:win].indirect(off), F.Sign, bias=1.5))], ["L4_0"] + nk, ["LF"], "lf")
+        gather(T.RF[:], T.RW[:, 0:win], off, ["L4_0", "RW"] + (["RTa", "RTb"] if t else []), ["RF"], "rf")
+        PE(lambda e: e.matmul(T[bS[0]][:, 0:S], T.OB[:], T.OQ[:], True, True), S, ["OB", "OQ"], [bS[0]], "FR")
+        lin(T.FI[:], T[bS[0]][:, 0:S], col("sc"), 0.0, ["sc"], ["FI", bS[0]], "fi")
         vts(T.FB[:], T.FI[:], 2048, None, A.bitwise_and, None, ["FI"], ["FB"], "fb")
         vtt(T.FBI[:], T.FB[:], T.BASE[:], A.add, ["FB", "BASE"], ["FBI"], "fbi")
         for fx, c in (("FE", "me"), ("FO", "mo")):
-            op([("s", 0.28, lambda e, fx=fx, c=c: e.activation(T[fx][:], T.FBI[:], F.Copy, scale=col(c))),
-                ("v", 0.16, lambda e, fx=fx, c=c: e.tensor_scalar(T[fx][:], T.FBI[:], col(c), None, A.mult))], ["FBI", c], [fx], "fx")
-        for gr in range(8):
-            p0, fk, bn = 32 * (gr // 2), "FO" if gr % 2 else "FE", ("bTP1", "bSP", "bTP0", "bMI")[gr % 4]
-
-            def fn(e, p0=p0, fk=fk, bn=bn):
-                fx, fb = T[fk], T.FBI
-                return [e.matmul(T[bn][:, 0:128], fx[p0:p0 + 32, 0:128], fb[p0:p0 + 32, 0:128], True, True),
-                        e.matmul(T[bn][:, 128:384], fx[p0:p0 + 32, 128:256], fb[p0:p0 + 32, :], True, True)]
-            PE(fn, 384, [fk, "FBI"], [bn], "dot")
-
-            def fs(e, bn=bn, gr=gr):
-                return [e.activation(T.JK[:, 512 * (gr % 2) + a:512 * (gr % 2) + b], T[bn][:, a:b], F.Relu, bias=col("q%db" % hf),
-                                     accum_out=T.DM[:, 8 * hf + gr:8 * hf + gr + 1]) for hf, a, b in ((0, 0, 128), (1, 128, 384))]
-            op([("s", 0.5, fs)], ["q0b", "q1b"], ["JK%d" % (gr % 2), "DM%d" % gr, bn], "red")
-        vts(T.DUP[:], T.DM[:], 0.0, None, A.is_gt, None, ["DM%d" % b for b in range(8)], ["DUP"], "dup")
-        PE(lambda e: e.matmul(T.bLP1[0:16, 0:128], T.DUP[:], T.IDB[:], True, True), 128, ["DUP", "IDB"], ["bLP1"], "dupT")
-        op([("s", 0.17, lambda e: e.activation(T.DUT[:], T.bLP1[0:16, 0:128], F.Copy)), ("v", 0.16, lambda e: e.tensor_copy(T.DUT[:], T.bLP1[0:16, 0:128]))],
-           [], ["DUT", "bLP1"], "dut")
-        PE(lambda e: [e.matmul(T.bSP[:, 0:256], T.IDB[:], T.SS0[:, 0:S], True, False), e.matmul(T.bSP[:, 0:256], T.IDB[:], T.MM0[:, 0:S], False, True)],
-           512, ["IDB", "SS0", "MM0"], ["bSP"], "vv")
-        vtt(T.DR[:], T.RF[:], T.bSP[:, 0:256], A.subtract, ["RF"], ["DR", "bSP"], "dr", two=False)
-        vtt(T.RS1[:], T.RF[:], T.bSP[:, 0:256], A.add, ["RF", "bSP"], ["RS1"], "rs1", two=False)
-        act(T.AD[:], T.DR[:], F.Abs, ["DR"], ["AD"], "abs")
-
-        def fn3(e):
-            r = []
-            for hh in range(2):
-                o, sl = T.bMI[:, 128 * hh:128 * hh + 128], slice(128 * hh, 128 * hh + 128)
-                r.append(e.matmul(o, T.BLK[:], T.AD[:, sl], True, False))
-                r.append(e.matmul(o, T.I8K[:], T.LF[:, sl], False, False))
-                r.append(e.matmul(o, T.EH[:, sl], T.DUT[:], False, True))
-            return r
-        PE(fn3, 768, ["BLK", "AD", "I8K", "LF", "EH", "DUT"], ["bMI"], "far")
-        vts(T.SP[:], T.bMI[:, 0:256], T.THC[:], None, A.is_ge, None, ["THC"], ["SP", "bMI"], "sp")
+            lin(T[fx][:], T.FBI[:], col(c), 0.0, ["FBI", c], [fx], "fx", True)
+        PE(lambda e: e.matmul(far[:, 0:S], T.E4[:], T.LF[:], True, False), S, ["E4", "LF"], [bC[0]], "leaf")
+        for m, (hf, gs) in enumerate([(0, (2 * m, 2 * m + 1)) for m in range(4)] + [(1, range(4 * m, 4 * m + 4)) for m in range(2)]):
+            bn, lo, jk = bS[(m + 1) % 2], 128 * hf, T.JK[:, 512 * m:512 * m + 512]
+            n = S - lo
+            for j in range(0, len(gs), 2):
+                PE(lambda e, bn=bn, lo=lo, j=j, n=n, p0=16 * gs[j]: [e.matmul(T[bn][:, n * (j + a):n * (j + a + 1)], fx[p0:p0 + 32, lo:lo + 128],
+                                                                              T.FBI[p0:p0 + 32, lo:S], True, True) for a, fx in enumerate((T.FE, T.FO))],
+                   2 * n, ["FE", "FO", "FBI"], [bn], "dot")
+            op([("s", vc(512), 0.0, lambda e, bn=bn, hf=hf, jk=jk: e.activation(jk, T[bn][:], F.Relu, scale=65536.0, bias=T.BD[:, hf:hf + 1]))],
+               ["BD"], ["JK%d" % m, bn], "red")
+            PE(lambda e, m=m, lo=lo, gs=gs, n=n: [e.matmul(far[:, lo:S], T.SB[:, 112 - 16 * gr:240 - 16 * gr], T.JK[:, 512 * m + n * j:512 * m + n * j + n], False, False)
+                                                  for j, gr in enumerate(gs)], 512, ["SB", "JK%d" % m], [bC[0]], "dup")
+        bv = T[bP[0]]
+        PE(lambda e: [e.matmul(bv[:, a:a + S], w[:], x[:, 0:S], x is T.RF, x is T.MM)
+                      for a, sg in ((0, T.NI16), (S, T.ID16)) for w, x in ((T.ID16, T.RF), (sg, T.SS), (sg, T.MM))],
+           6 * S, ["ID16", "NI16", "RF"] + vk, [bP[0]], "vv")
+        op([("s", vc(S), 0.0, lambda e: e.activation(T.AD[:], bv[:, 0:S], F.Abs))], [], ["AD", bP[0]], "abs")
+        lin(T.RS2[:], bv[:, S:2 * S], 0.5, -0.25, [], ["RS2", bP[0]], "rs2")
+        PE(lambda e: e.matmul(far[:, 0:S], T.BLK[:], T.AD[:], False, True), S, ["BLK", "AD"], [bC[0]], "far")
+        vts(T.SP[:], far[:, 0:S], T.THC[:, 0:1], None, A.is_ge, None, ["THC"], ["SP", bC[0]], "sp")
         RN, rn, c0 = (T.YR1, "YR1", 0) if t else (T.RW, "RT", 2048)
-        vts(T.RS2[:], T.RS1[:], 1, None, A.arith_shift_right, None, ["RS1"], ["RS2"], "rs2")
         vtt(RN[:, c0:c0 + 512:2], T.RF[:], T.SP[:], A.mult, ["RF", "SP"], [rn + "a"], "rna")
         vtt(RN[:, c0 + 1:c0 + 512:2], T.RS2[:], T.SP[:], A.mult, ["RS2", "SP"], [rn + "b"], "rnb")
-        wrap(T.bSP, 0, T.WQP, T.SP, 0, 16, ["SP", "WQP"], ["bSP"], "wsp")
-        vcopy(T.TG[:, 0:16], LI(4, 0, 16), ["L4_0"], ["TG0"])
-        vtt(T.TG[:, 16:32], T.TG[:, 0:16], T.DW[:], A.subtract, ["TG0", "DW"], ["TG1"])
-        vts(T.TG[:, 32:48], T.bSP[:, 0:16], 1.0, None, A.is_ge, None, [], ["TG2", "bSP"])
-        vtt(T.TG[:, 48:64], T.TG[:, 16:32], T.TG[:, 32:48], A.mult, ["TG1", "TG2"], ["TG3"])
-        vtt(T.TG[:, 64:80], T.TG[:, 48:64], T.DW[:], A.add, ["TG3", "DW"], ["TG4"])
-        vcopy(LI(11, 0, 16), T.TG[:, 64:80], ["TG4"], ["TGL"])
-
-        def scat(win_, val, R, W, nm):
-            op([("v", 0.05 + S * 3.5 * CYC, lambda e: e.tensor_copy(win_.indirect(LI(11, 0, 16)), val))], R + ["TGL"], W, nm)
+        s2 = bS[1]
+        wrap(s2, 0, "big", T.SP, 0, 16, ["IDF", "DW", "SP"], "wsp", False, True, [lambda e: e.matmul(T[s2][:, 0:16], T.IDF[:], T.DW[:], True, False)])
+        if t:
+            cp(T.FW[:, 64:80], off, ["L4_0"], ["FW"])
+        vtt(T.TG[:, 0:16], T.FW[:, 64:80], T[s2][:, 0:16], A.max, ["FW"], ["TG1", s2], two=False)
+        tg = LI(11, 0, 16)
+        cp(tg, T.TG[:, 0:16], ["TG1"], ["TGL"])
         if not t:
-            scat(T.KW[:], T.NK[:], ["NK"], KWK + KTK, "scK")
-            scat(T.ZW[:], T.XF[:], ["XF"], ["ZW", "ZT"], "scZ")
-        scat(T.KF[:], (T.NV1 if t else T.NV0)[:], ["NV1" if t else "NV0"], ["KF0", "KF1", "KFt"], "scF")
+            op([("v", 0.042, 2.3 * S * CYC, lambda e: e.tensor_tensor(T.NW[:].indirect(tg), T.XF[:], T.Q2[:], A.add))], ["TGL", "XF", "Q2"], NWK + ["NT"], "scN")
+        nv = "NV1" if t else "NV0"
+        op([("v", 0.042, 2.3 * S * CYC, lambda e: e.tensor_copy(T.KF[:].indirect(tg), T[nv][:]))], ["TGL", nv], ["KF0", "KF1", "KFt"], "scF")
 
+    nq = [0]
+
+    def chain(src, c0, C, z, out, W, R):
+        bq = bQ[nq[0] % 2]
+        nq[0] += 1
+        wrap(bq, 0, z, src, c0, C, R, "ws")
+        if z == "p4":
+            lin(out, T[bq][:, 0:C], 1.0, GOFF, ["THC"], W + [bq], "slist")
+        else:
+            cp(out, T[bq][:, 0:C], [], W + [bq], "slist")
+
+    for p, (c0, C) in enumerate(PARTS):
+        fore[0] = -LAG * p
+        gather(lanes(T.XS0, c0, C), T.XW[:], LI(5, c0, C), ["XW", "L5_%d" % p], ["XS%d" % p], "xs")
+    for k, pt in enumerate(("LT", "PT1", "PT2")):
+        for p, (c0, C) in enumerate(PARTS):
+            fore[0] = -LAG * p
+            gather(lanes(T[pt], c0, C), PWIN, LI(5 + k, c0, C), PWK + ["L%d_%d" % (5 + k, p)], [pt + str(p)], "pv")
+            chain(T[pt], c0, C, "p0", LI(6 + k, c0, C), ["L%d_%d" % (6 + k, p)], [pt + str(p)])
+    fore[0] = 0.0
+    LTK = ["LT%d" % p for p in allp]
+    for j in range(2):
+        DMA(T.LT[2 + j:128:16, :], T.PT1[j:128:16, :], ["PT1%d" % p for p in allp] + ["L6_%d" % p for p in allp], ["LTr%d" % j], "lt", 32, 2048)
     for k in range(4):
-        for h in range(2):
-            gather(T["XS%d" % k][:, HL * h:HL * h + HL], T.XW[:], LI(5 + k, 64 * h, 64 * h + 64), HL, ["XW", "SL%d_%d" % (k, h)], ["XS%d_%d" % (k, h)], "xs")
-        for h in range(2):
-            if k < 3:
-                gather(T["PT%d" % h][:], T.PW[:], LI(5 + k, 64 * h, 64 * h + 64), HL, ["PW0", "PW1", "SL%d_%d" % (k, h)], ["PT%d" % h], "pv")
-                wrap(T.bSP, 0, T.WQP, T["PT%d" % h], 0, 64, ["WQP", "PT%d" % h], ["bSP"], "ws")
-                vcopy(LI(6 + k, 64 * h, 64 * h + 64), T.bSP[:, 0:64], [], ["SL%d_%d" % (k + 1, h), "bSP"], "slist")
-        for h in range(2):
-            step(0, k, h, T["XS%d" % k], "XS%d_%d" % (k, h))
-    gather(T.PT2[:], T.PW[:], LI(8, 0, 16), S, ["PW0", "PW1", "SL3_0"], ["PT2"], "p4")
-    wrap(T.bSP, 0, T.WQP, T.PT2, 0, 16, ["WQP", "PT2"], ["bSP"], "ws4")
-    vcopy(T.SW[:, 64:80], T.bSP[:, 0:16], [], ["SW4", "bSP"])
-    for k in range(5):
-        vcopy(T.FW[:, 16 * k:16 * k + 16], LI(k, 0, 16), ["L%d_0" % k], ["FW%d" % k])
-        if k < 4:
-            vcopy(T.SW[:, 16 * k:16 * k + 16], LI(5 + k, 0, 16), ["SL%d_0" % k], ["SW%d" % k])
-    vtt(T.SFa[:], T.FW[:, 16:80], T.FW[:, 0:64], A.not_equal, ["FW%d" % k for k in range(5)], ["SFa"])
-    vtt(T.SFb[:], T.SW[:, 16:80], T.SW[:, 0:64], A.subtract, ["SW%d" % k for k in range(5)], ["SFb"])
+        for p in allp:
+            fore[0] = -LAG * p
+            step(0, k, p)
+    fore[0] = 0.0
+    gather(T.PT3[:], PWIN, LI(8, 0, 16), PWK + ["L8_0"], ["PT3"], "p4")
+    chain(T.PT3, 0, 16, "p0", T.SW[:, 64:80], ["SW4"], ["PT3"])
+    cp(T.FW[:], T.LL[:, 0:5, 0:16], ["L%d_0" % k for k in range(5)], ["FW"])
+    cp(T.SW[:, 0:64], T.LL[:, 5:9, 0:16], ["L%d_0" % k for k in range(5, 9)], ["SW"])
+    vtt(T.SFb[:], T.SW[:, 16:80], T.SW[:, 0:64], A.subtract, ["SW", "SW4"], ["SFb"])
+    vtt(T.SFa[:], T.FW[:, 16:80], T.FW[:, 0:64], A.not_equal, ["FW"], ["SFa"])
     vtt(T.SFa[:], T.SFa[:], T.SFb[:], A.mult, ["SFa", "SFb"], ["SFa"])
     vtt(T.SFb[:, 0:32], T.SFa[:, 0:32], T.SFa[:, 32:64], A.add, ["SFa"], ["SFb"])
     vtt(T.SFa[:, 0:16], T.SFb[:, 0:16], T.SFb[:, 16:32], A.add, ["SFb"], ["SFa"])
-    vtt(T.SFb[:, 32:48], T.SFa[:, 0:16], T.SW[:, 0:16], A.add, ["SFa", "SW0"], ["SFb"])
-    vcopy(LI(11, 32, 48), T.SFb[:, 32:48], ["SFb"], ["SFL"])
-    gather(T.XF[:], T.XW[:], LI(11, 32, 48), S, ["XW", "SFL"], ["XF"], "xf")
+    vtt(T.SFb[:, 32:48], T.SFa[:, 0:16], T.SW[:, 0:16], A.add, ["SFa", "SW"], ["SFb"])
+    cp(LI(11, 32, 16), T.SFb[:, 32:48], ["SFb"], ["SFL"])
+    gather(T.XF[:], T.XW[:], LI(11, 32, 16), ["XW", "SFL"], ["XF"], "xf")
+    bq = bQ[0]
+    PE(lambda e: e.matmul(T[bq][:, 0:S], T.WD[:], T.XF[:], True, True), 4 * S, ["WD", "XF"], [bq], "xD")
+    vtt(T.D2[:], T.NC[:], T[bq][:, 0:S], A.add, ["NC"], ["D2", bq], "d2", two=False)
+    vts(T.D3[:], T.D2[:], 7 * 512, None, A.bitwise_and, None, ["D2"], ["D3"], "d3")
+    lin(T.Q2[:], T.D3[:], -1.0 / 4096, 0.0, ["D3"], ["Q2"], "q2")
 
-    op([("s", 1.77, lambda e: e.activation(T.EW[:], T.EW[:], F.Copy, bias=-256.0)),
-        ("v", 0.9, lambda e: e.tensor_scalar(T.EW[:], T.EW[:], -256.0, None, A.add))], ["EW"], ["EW"], "env256")
-    outcome(0, T.XS0, ["XS0_0", "XS0_1"])
-    for h in range(2):
-        hs = str(h)
-        send([T["SS" + hs][:], T["MM" + hs][:]], T.VL[:, HL * h:HL * h + HL], nxt, "aA" + hs, "lA" + hs, ["SS" + hs, "MM" + hs], ["VL%d" % h], "send" + hs, 256)
-    vcopy(T.thF[:], T.thI[:], ["thI"], ["thF"])
-    PE(lambda e: e.matmul(T.bMI[:, 0:1], T.E8[:], T.thF[:], True, True), 256, ["E8", "thF"], ["bMI"], "th")
-    vts(T.THC[:], T.bMI[:, 0:1], BIG, None, A.add, None, [], ["THC", "bMI"])
-    vcopy(T.KDf[:], T.KD[:], ["KD0", "KD1"], ["KDf"])
-    DMA(T.KF[0:128:16, 0:2048], T.KDf[:, 0:128], ["KDf"], ["KF0"], "kf0", boost=-30.0)
-    DMA(T.KF[1:128:16, 0:2048], T.KDf[:, 128:256], ["KDf"], ["KF1"], "kf1", boost=-30.0)
+    ns, sent = [0], [[] for p in allp]
+    for p in allp:
+        fore[0] = -LAG * p
+
+        def hand(nm, c0, C, p=p):
+            send([lanes(T.SS, c0, C), lanes(T.MM, c0, C)], lanes(T.VL, c0, C), nxt, "aA%d" % ns[0], "lA%d" % ns[0],
+                 ["SS" + nm, "MM" + nm], ["VL" + nm], "send" + nm, 4 * C)
+            ns[0] += 1
+            came.append(("VL" + nm, c0, C))
+            sent[p].append("send" + nm)
+        outcome(0, p, hand)
+    fore[0] = 0.0
+    DMA(T.KF[0:128:16, 0:2048], T.KDf[:, 0:128], ["KDf", "PWf"], ["KF0"], "kf0", 64, 512, -300.0)
+    DMA(T.KF[1:128:16, 0:2048], T.KDf[:, 128:256], ["KDf", "PWf"], ["KF1"], "kf1", 64, 512, -300.0)
     splits(0)
-    DMA(T.yr[:, 0:512], T.RW[:, 2048:MW], ["RTa", "RTb"], ["oyr0"], "oyr0")
-    vcopy(T.cuF[:], T.cuI[:], ["cuI"], ["cuF"])
-    PE(lambda e: e.matmul(T.bLP1[:, 0:128], T.cuF[:], T.IDF[:], True, True), 512, ["cuF", "IDF"], ["bLP1"], "cuT")
-    act(T.cuT[:], T.bLP1[:, 0:128], F.Copy, [], ["cuT", "bLP1"], "cuT")
-    for gr in range(8):
-        DMA(T.CF[16 * gr:16 * gr + 1, :], T.cuT[:, 16 * gr:16 * gr + 16], ["cuT", "CF"], ["CF%d" % gr], "cf", kb=8)
+    DMA(T.yr[:, 0:512], T.RW[:, 2048:MW], ["RTa", "RTb"], ["oyr0"], "oyr0", 128, 1024)
     send([T.wI[:]], T.wN[:], prv, "aw", "lw", ["wI"], ["wN"], "sendw", 1)
-    vcopy(col("wn"), T.wN[:], ["wN"], ["wn"])
-    act(T.WN8[:], T.BC8[:], F.Copy, ["BC8", "wn"], ["WN8"], "wn8", scale=col("wn"))
+    cp(col("wn"), T.wN[:], ["wN"], ["wn"])
+    lin(slot("wn"), BC8, col("wn"), 0.0, ["W16", "Zone", "wn"], ["Zwn"], "Zn")
 
-    for h in range(2):
-        hs = str(h)
-        wrap(T["bOP" + hs], 64, T.WQW, T.VL, HL * h, 64, ["WQW", "VL%d" % h], ["bOP" + hs], "wh")
-        i1, i2 = T.IT[:, 256 + 64 * h:320 + 64 * h], T.IT[:, 384 + 64 * h:448 + 64 * h]
-        vcopy(i1, T["bOP" + hs][:, 64:128], [], ["HI1" + hs, "bOP" + hs], "h1")
-        vts(i2, i1, 2047, None, A.bitwise_and, None, ["HI1" + hs], ["HI2" + hs], "h2")
-        vcopy(LI(9, 64 * h, 64 * h + 64), i2, ["HI2" + hs], ["LH" + hs], "h3")
+    for p, (c0, C) in enumerate(PARTS):
+        fore[0] = -LAG * p
+        wrap(bP[p], 0, "w", T.VL, c0, C, vl(c0, C), "wc")
+        cp(T.WC[:, c0:c0 + C], T[bP[p]][:, 0:C], [], ["WC%d" % p, bP[p]], "wc")
+        low(p, T.WC[:, c0:c0 + C], "WC%d" % p, LI(9, c0, C), ["L9_%d" % p])
+        gather(lanes(T.LG, c0, C), T.LT[:], LI(9, c0, C), LTK + ["LTr0", "LTr1", "L9_%d" % p], ["LG%d" % p], "lg")
+        for k, z in ((12, "p4"), (13, "p0"), (14, "p2")):
+            chain(T.LG, c0, C, z, LI(k, c0, C), ["L%d_%d" % (k, p)], ["LG%d" % p])
+    fore[0] = -30.0
+    rows(bQ[0], "p4", T.LG, 0, 16, True, True, ["LG%d" % p for p in allp], "cur")
+    lin(T.YP[:], T[bQ[0]][:, 0:128], 1.0, GOFF, ["THC"], ["YP", bQ[0]], "yp")
+    DMA(T.yp[:, 0:2048], T.YP[:], ["YP"], ["oyp0"], "oyp", 64, 512)
     for k in range(4):
-        for h in range(2):
-            if k:
-                gather(T["YS%d" % k][:, HL * h:HL * h + HL], T["XS%d" % (k - 1)][:], LI(9, 64 * h, 64 * h + 64), HL,
-                       ["XS%d_0" % (k - 1), "XS%d_1" % (k - 1), "LH%d" % h], ["YS%d_%d" % (k, h)], "ys")
-        for h in range(2):
-            step(1, k, h, T["YS%d" % k] if k else T.VL, "YS%d_%d" % (k, h) if k else "VL%d" % h)
-    for h in range(2):
-        gather(T.HG[:, HL * h:HL * h + HL], T.CF[:], LI(9, 64 * h, 64 * h + 64), HL, ["CF"] + ["CF%d" % a for a in range(8)] + ["LH%d" % h], ["HG%d" % h], "cur")
-        DMA(T.yp[:, HL * h:HL * h + HL], T.HG[0:128:16, HL * h:HL * h + HL], ["HG%d" % h], ["oyp%d" % h], "oyp", kb=32)
-    outcome(1, T.VL, ["VL0", "VL1"])
+        for p in allp:
+            fore[0] = -LAG * p
+            step(1, k, p)
+    for p in allp:
+        fore[0] = -LAG * p
 
-    def fnh(h):
-        def fn(e):
-            r = []
-            for j in range(8):
-                for a_, src in enumerate((T["SS%d" % h], T["MM%d" % h])):
-                    r.append(e.matmul(T.bOP0[:, 200 + 8 * h + j:328:16], src[:, 128 * j:128 * j + 128], T.WN8[:], a_ == 0, a_ == 1))
-            return r
-        return fn
-    for h in range(2):
-        PE(fnh(h), 1024, ["WN8", "SS%d" % h, "MM%d" % h], ["bOP0"], "hd")
-    i1, i2 = T.IT[:, 256:384], T.IT[:, 384:512]
-    vcopy(i1, T.bOP0[:, 200:328], [], ["HI10", "HI11", "bOP0"], "H1")
-    vts(i2, i1, 2047, None, A.bitwise_and, None, ["HI10", "HI11"], ["HI20", "HI21"], "H2")
-    vts(T.HFT[:], i2, 4096.0, None, A.add, None, ["HI20", "HI21"], ["HFT"], "H3")
-    PE(lambda e: e.matmul(T.bOP1[:, 256:384], T.HFT[:], T.IDF[:], True, True), 512, ["HFT", "IDF"], ["bOP1"], "HT")
-    op([("s", 0.17, lambda e: e.activation(T.HS[:], T.bOP1[:, 256:384], F.Copy)), ("v", 0.16, lambda e: e.tensor_copy(T.HS[:], T.bOP1[:, 256:384]))],
-       [], ["HS", "bOP1"], "H4")
+        def handsum(nm, c0, C):
+            rows(bQ[1], "wn", T.SS, c0 // 8, (c0 + C) // 8, c0 == 0, False, ["SS" + nm], "hs")
+            rows(bQ[1], "wn", T.MM, c0 // 8, (c0 + C) // 8, False, c0 + C == 128, ["MM" + nm], "hm")
+        op([("arr", 0.0, 0.0, None)], sent[p] + (["RS2", "AD"] if p == 0 else []), ["o%d" % p], "free")
+        outcome(1, p, handsum)
+    fore[0] = 0.0
+    i1, i2 = T.IT[:, 0:128], T.IT[:, 128:256]
+    cp(i1, T[bQ[1]][:, 0:128], [], ["H1", bQ[1]], "H1")
+    vts(i2, i1, 2047, None, A.bitwise_and, None, ["H1"], ["H2"], "H2")
+    lin(T.HS[:], i2, 1.0, 4096.0, ["H2"], ["HS"], "H3")
     send([T.HS[:]], T.HR[:], nxt, "aH", "lH", ["HS"], ["HR"], "sendH", 64)
-    DMA(T.yp[:, 2048:4096], T.HR[:], ["HR"], ["oyp2"], "oyp2")
+    DMA(T.yp[:, 2048:4096], T.HR[:], ["HR"], ["oyp2"], "oyp2", 64, 512)
     splits(1)
-    DMA(T.yr[:, 512:1024], T.YR1[:], ["YR1a", "YR1b"], ["oyr1"], "oyr1", kb=128)
-    DMA(T.yk0[:], T.KF[0:128:16, 0:3072], ["KF0", "KFt"], ["oyk0"], "oyk0", kb=96)
-    DMA(T.yk1[:], T.KF[1:128:16, 0:3072], ["KF1", "KFt"], ["oyk1"], "oyk1", "s", kb=96)
+    DMA(T.yr[:, 512:1024], T.YR1[:], ["YR1a", "YR1b"], ["oyr1"], "oyr1", 128, 1024)
+    DMA(T.yk0[:], T.KF[0:128:16, 0:3072], ["KF0", "KFt"], ["oyk0"], "oyk0", 96, 6144)
+    DMA(T.yk1[:], T.KF[1:128:16, 0:3072], ["KF1", "KFt"], ["oyk1"], "oyk1", 96, 6144)
 
     if "order" not in PLANS:
         PLANS["order"], PLANS["score"] = make_plan(ops)
@@ -575,19 +760,22 @@ def rank_program(g, core, T, topo):
     known = dict((q, {}) for q in eng)
     total, token = {}, [None] * len(ops)
     for i, j in PLANS["order"]:
-        q, d, fn = ops[i]["alts"][j]
+        q, fn = ops[i]["alts"][j][0], ops[i]["alts"][j][3]
+        if ops[i]["nm"] == "free":
+            token[i] = [x for dp in ops[i]["deps"] for x in token[dp]]
+            continue
         if q == "arr":
             s_, v = ops[i]["tok"]
-            token[i] = (s_, v, {s_: v})
+            token[i] = [(s_, v, {s_: v})]
             total[s_] = v
             continue
         r = q[0]
         kn, e = known[r], eng[r]
         need = {}
         for dp in ops[i]["deps"]:
-            s_, v, ck = token[dp]
-            if kn.get(s_, 0) < v and need.get(s_, (0, None))[0] < v:
-                need[s_] = (v, ck)
+            for s_, v, ck in token[dp]:
+                if kn.get(s_, 0) < v and need.get(s_, (0, None))[0] < v:
+                    need[s_] = (v, ck)
         for s_ in sorted(need, key=lambda s_: (-len(need[s_][1]), s_)):
             v, ck = need[s_]
             if kn.get(s_, 0) >= v:
@@ -607,7 +795,7 @@ def rank_program(g, core, T, topo):
         total[s_] = v
         ck = dict(kn)
         ck[s_] = v
-        token[i] = (s_, v, ck)
+        token[i] = [(s_, v, ck)]
     for s_ in sorted(total):
         if known["g"].get(s_, 0) < total[s_]:
             g.wait_ge(T.sem[s_], total[s_])

@@ -8,8 +8,9 @@ BIG, EOFF = 8192.0, 1280
 PARTS = ((0, 64), (64, 64))
 GP = 2
 RP = 1
-ENDS = ((2, 2), (1, 2))
-EARLY = 1
+ACC, RNP = 1, (0, 0)
+ENDS = (((32, 32), (32, 32)), ((64,), (32, 32)))
+LEAST = 32
 BFB, FP, I4, U2, H2 = "bfloat16", "float32", "int32", "uint16", "float16"
 SCRATCH = {}
 
@@ -21,23 +22,24 @@ def _decl(where, dtype, text):
         SCRATCH[nm] = (where, c if len(c) > 1 else [128] + c, dtype)
 
 
-_decl("sbuf", BFB, "XW:4096 PW:4608 RW:2560 EW:2048 LT:2048 PT1:2048 PT2:2048 LG:2048 CR:2048 CC:2048 WZ:864 PDb:512 OWb:512 ONB:128 ZB:320 "
-      "IDB:128 NI8:128 RK:16 BLK:128 E4:128 OB:128 SB:240 I4B:256 BASE:256 LM:128 YR1:512 PT3:256 OQ:256 FBI:256 FE:256 FO:256 "
-      "LF:256 JK:3072 AD:256 SP:256 MA:128 CST:2x128")
-_decl("sbuf", H2, "XS0:2048 VL:2048 SS:2048 MM:2048 CN:2048 W16:288 RHS:24 ID16:128 NI16:128 NI4:128 PI4:128 RF:256 U:256 E0:128x17x8 E1:128x17x8")
-_decl("sbuf", FP, "NW:3456 KF:3456 KDf:256 PERM:128 OWT:128 thF:8x2 THC:2 ONF:128 IDF:128 E8:8x128 COL:16 CT:32x16 EQ:16x128 EQ2:32x128 DW:16 NV0:256 NV1:256 "
-      "NC:256 WD:128 XF:256 Q2:256 FW:80 SW:80 SFa:64 SFb:64 HR:128 HS:128 YP:128 TG:32 MB:128 BD:4")
-_decl("sbuf", I4, "stI:128 cuI:128 KD:256 PD:256 KT:320 DI:256 QI:1280 wI:1 wN:1 thI:8x1 FI:256 FB:256 D2:256 D3:256 RS2:256 WC:128 IT:256 FT:128 FU:128")
+_decl("sbuf", BFB, "XW:4096 PW:4096 RW:2560 EW:2048 LT:2048 PT1:2048 PT2:2048 LG:2048 CR:2048 CC:2048 XS0:2048 WZ:1008 PDb:512 OWb:512 ONB:128 ZB:320 "
+      "IDB:128 NI8:128 RK:16 BLK:128 E4:128 SB:240 BW:2560 BK:320 LM:128 YR1:512 PT3:256 FBI:256 FE:256 FO:256 "
+      "LF:256 JK:3072 AD:256 SP:256 MA:128 I15:128 I05:128 EH:16x256 DUT:16x128 CST:2x128")
+_decl("sbuf", H2, "VL:2048 SS:2048 MM:2048 CN:2048 W16:288 RHS:24 ID16:128 NI16:128 NI4:128 PI4:128 RF:256 RS2:256 U:256 BASE:256 KDh:256 PERM:128 E0:128x17x8 E1:128x17x8")
+_decl("sbuf", FP, "NW:3456 KF:3456 KDf:256 OWT:128 thF:8x2 THC:2 ONF:128 IDF:128 E8:8x128 COL:16 CT:32x16 EQ:16x128 EQ2:32x128 DW:16 NV0:256 NJ:512 "
+      "NC:256 WD:128 XF:256 Q2:256 FW:80 SW:80 SFa:64 SFb:64 HR:128 HS:128 YP:128 TG:16 MB:128 BD:2 DM:16 I4B:256 BI:320 EQ8:16x128")
+_decl("sbuf", I4, "stI:128 cuI:128 KD:256 PD:256 KT:320 DI:256 QI:1280 wI:1 wN:1 thI:8x1 FI:320 FB:320 D2:256 D3:256 RSI:256 WC:128 IT:256 FT:128 FU:128")
 _decl("sbuf", U2, "LL:128x15x128")
 _decl("psum", FP, " ".join("b%d:512" % _k for _k in range(8)))
-SEMAPHORES = (["cv", "cs", "ct", "cg"] + ["d%d" % _k for _k in range(40)] + ["aw", "lw", "aH", "lH"]
+SEMAPHORES = (["cv", "cs", "ct", "cg"] + ["d%d" % _k for _k in range(40)] + ["aw", "lw", "aH0", "lH0", "aH1", "lH1"]
               + ["%s%d" % (_a, _k) for _a in ("aA", "lA") for _k in range(8)])
 
 CYC = 0.83e-3
-BETA, TRIES, MOVES, SEED0, LAG, HEAT = 0.03, 100, 110000, 11, 3.0, 0.01
-MODELS = ((1.15, 1.4, 0.18, 1.0, 1.0), (1.4, 1.1, 0.22, 1.6, 1.3), (1.1, 1.9, 0.18, 1.3, 1.2))
-DLAT, RLAT, RBW, RFIRST, RCALL = 1.3, 1.8, 120.0, 2.0, 0.6
-SELF, TCYC, FIX = 0.07, 0.65, 0.052
+BETA, TRIES, MOVES, SEED0, LAG, HEAT = 0.03, 100, 42000, 3, 0.0, 0.01
+MODELS = ((1.15, 1.4, 0.2, 1.0, 1.0, 0.02, 1.0), (1.02, 1.08, 0.22, 1.6, 1.6, 0.06, 2.5), (1.35, 1.9, 0.18, 1.4, 1.2, 0.05, 1.5))
+DLAT, RLAT, RBW, RFIRST, RCALL = 1.3, 2.3, 170.0, 2.0, 0.6
+SELF, TCYC, FIX = 0.07, 0.71, 0.052
+MEAN, PACK, PHEAT, MORE, AGAIN, REHEAT = 0.0, 500, 3.0, 0, 30000, 0.006
 PLANS = {}
 
 
@@ -52,11 +54,11 @@ def make_plan(ops):
     QI = dict((q, k) for k, q in enumerate("vstgya"))
     kind = [o["alts"][0][0] for o in ops]
     rq = [[QI[a[0][0]] for a in o["alts"]] for o in ops]
-    dur = [[[a[1] * (1.0 if a[0] in ("yd", "sd", "gr") else m[0]) + a[2] * m[1] for a in o["alts"]] for o in ops] for m in MODELS]
+    dur = [[[a[1] * (1.0 if a[0] in ("yd", "sd") else m[6] if a[0] == "gr" else m[0]) + a[2] * m[1] for a in o["alts"]] for o in ops] for m in MODELS]
     chan = [1 if k in ("yd", "sd") else 2 if k == "gr" else 0 for k in kind]
     lat = [o["lat"] for o in ops]
     pre = [[(DLAT - 0.3) * m[4] if c == 1 else 0.0 for c in chan] for m in MODELS]
-    on = [[lat[i] * m[3] if chan[i] else 0.0 for i in range(n)] for m in MODELS]
+    on = [[lat[i] * m[3] + ops[i]["rows"] * m[5] if chan[i] else 0.0 for i in range(n)] for m in MODELS]
     post = [[0.3 if chan[i] else lat[i] * m[4] if kind[i] == "arr" else m[2] for i in range(n)] for m in MODELS]
     norm = [m[0] * 30 + m[1] * 25 + 15 for m in MODELS]
     pri = [0.0] * n
@@ -134,7 +136,7 @@ def make_plan(ops):
                 fin[i] = t
                 why[i] = w
             keep.append(free[:])
-        return max(fin) / norm[mi], fin, why, keep
+        return (max(fin) + MEAN * sum(fin) / n) / norm[mi], fin, why, keep
 
     def owners(alt):
         return [-1 if chan[i] else rq[i][alt[i]] for i in range(n)]
@@ -179,8 +181,53 @@ def make_plan(ops):
         if sum(x[0] for x in s2) <= best:
             best, order, alt, boost, pick, st = sum(x[0] for x in s2), o2, a2, b2, p2, s2
             way = longest(order, alt, st[int(rnd() * NM)])
+    def packed(order, alt, own, mi):
+        du, gain = dur[mi], MODELS[mi][2] - SELF
+        lag = [pre[mi][i] + on[mi][i] + post[mi][i] for i in range(n)]
+        link = [[], []]
+        for c in (1, 2):
+            line = [i for i in order if chan[i] == c]
+            link[0] += list(zip(line[1:], line))
+            link[1] += list(zip(line, line[1:]))
+        for back in (1, 0):
+            at, busy, seq = [0.0] * n, [[] for _ in range(6)], order[::-1] if back else order
+            other = dict(link[back])
+            for i in seq:
+                q, d = rq[i][alt[i]], du[i][alt[i]]
+                if back:
+                    t = max([lag[i]] + [at[x] + du[x][alt[x]] + lag[i] - (gain if own[i] == rq[x][alt[x]] else 0.0) for x in succ[i]])
+                    if i in other:
+                        t = max(t, at[other[i]] + on[mi][i])
+                else:
+                    t = max([0.0] + [at[x] + du[x][alt[x]] + lag[x] - (gain if own[x] == q else 0.0) for x in near[i]])
+                    if i in other:
+                        t = max(t, at[other[i]] + on[mi][other[i]])
+                if q < 5:
+                    k, bq = 0, busy[q]
+                    while k < len(bq) and bq[k][0] < t + d:
+                        t = max(t, bq[k][1])
+                        k += 1
+                    bq.insert(k, (t, t + d))
+                at[i] = t
+            place = dict((x, k) for k, x in enumerate(order))
+            order = sorted(order, key=lambda x: ((-at[x] - du[x][alt[x]]) if back else at[x], place[x]))
+        return order
     now, keep, own = best, (order, alt), owners(alt)
-    for it in range(MOVES):
+    for it in range(MOVES + MORE):
+        heat = HEAT * (1.0 - it / MOVES) if it < MOVES else REHEAT * (1.0 - (it - MOVES) % AGAIN / AGAIN)
+        if it >= MOVES and (it - MOVES) % AGAIN == 0:
+            now, (order, alt) = best, keep
+            own, st = owners(alt), score(order, alt)
+            way = longest(order, alt, st[0])
+        if it % PACK == PACK - 1:
+            o2 = packed(order, alt, own, it // PACK % NM)
+            s2 = score(o2, alt)
+            if sum(x[0] for x in s2) < now + heat * PHEAT:
+                now, order, st = sum(x[0] for x in s2), o2, s2
+                way = longest(order, alt, st[0])
+                if now < best:
+                    best, keep = now, (order, alt)
+            continue
         r, o2, a2, w2 = rnd(), order, alt, own
         i, b = way[int(rnd() * len(way))]
         if r < 0.15:
@@ -213,7 +260,7 @@ def make_plan(ops):
                 rest = [x for x in mid if x == b or anc[x] >> b & 1]
                 up = [x for x in mid if not (x == b or anc[x] >> b & 1)]
             o2 = order[:pb] + up + rest + order[pi + 1:]
-        room, s2 = HEAT * (1.0 - it / MOVES) * rnd() ** 3, []
+        room, s2 = heat * rnd() ** 3, []
         for mi in range(NM):
             s2.append(length(o2, a2, w2, mi, st[mi], pb))
             room -= s2[mi][0] - st[mi][0]
@@ -246,7 +293,7 @@ def rank_program(g, core, T, topo):
     def QT(a, b, step=1):
         return T.PW[:, 2048 + a:2048 + b:step]
 
-    def op(alts, R, W, nm="", lat=0.0, tok=None, boost=0.0, pref=-1):
+    def op(alts, R, W, nm="", lat=0.0, tok=None, boost=0.0, pref=-1, rows=0):
         i, deps = len(ops), set()
         for k in list(R) + list(W):
             if k in last:
@@ -259,7 +306,7 @@ def rank_program(g, core, T, topo):
             last[k] = i
             readers[k] = []
         deps.discard(i)
-        ops.append(dict(alts=alts, deps=deps, nm=nm, lat=lat, tok=tok, boost=boost + fore[0], pref=pref))
+        ops.append(dict(alts=alts, deps=deps, nm=nm, lat=lat, tok=tok, boost=boost + fore[0], pref=pref, rows=rows))
 
     def width(ap):
         n = 1
@@ -277,8 +324,7 @@ def rank_program(g, core, T, topo):
     def DMA(out, in_, R, W, nm, kb, row, boost=0.0):
         s = "d%d" % nd[0]
         nd[0] += 1
-        us = -(-(kb * 1024 // row) // 16) * (0.02 + row / 40000.0)
-        op([(q, 0.06, 0.0, lambda e: e.dma_start(out, in_).then_inc(T.sem[s], 16)) for q in ("yd", "sd")], R, W, nm, lat=us, tok=(s, 16),
+        op([(q, 0.06, 0.0, lambda e: e.dma_start(out, in_).then_inc(T.sem[s], 16)) for q in ("yd", "sd")[0:1 + (nm[0] == "o" or nm == "kid1")]], R, W, nm, lat=kb / 640.0, tok=(s, 16), rows=-(-(kb * 1024 // row) // 16),
            boost=boost - fore[0], pref=0)
 
     def ts(out, in0, s1, s2, o0, o1=None):
@@ -352,17 +398,17 @@ def rank_program(g, core, T, topo):
     ms(T.ZB[:], 0.0, ["ZB"])
     ms(T.ONF[:], 1.0, ["ONF"], half=False)
     ms(T.ONB[:], 1.0, ["ONB"])
-    aff(T.PERM[:], T.ONF[:], [[-1, 16], [-16, 8]], A.is_equal, 0.0, 0, 1, ["ONF"], ["PERM"])
+    aff(T.PERM[:], T.ONB[:], [[-1, 16], [-16, 8]], A.is_equal, 0.0, 0, 1, ["ONB"], ["PERM"])
     put(T.RK[:], 8, [(k, -8 ** (k + 1)) for k in range(4)], [], "RK")
     fore[0] = 60.0
     for k in range(4, 8):
-        zero(QT(k, MW, 8), ["QT%d_%d" % (c, k) for c in range(3)])
+        zero(QT(k, 2048, 8), ["QT%d_%d" % (c, k) for c in range(2)])
     iota(T.OWT[:], [[128, 16], [0, 8]], 0, 1, ["OWT"])
     aff(T.IDB[:], T.ONB[:], [[-1, 128]], A.is_equal, 0.0, 0, 1, ["ONB"], ["IDB"])
     put(T.NI8[:], 1, [(0, -0.125)], [], "NI8")
     fore[0] = 20.0
     ms(T.WZ[:], 0.0, ["WZ"])
-    ZS = dict([(nm, (T.WZ, 144 * j)) for j, nm in enumerate(("one", "p0", "p2", "p4", "a97", "big"))]
+    ZS = dict([(nm, (T.WZ, 144 * j)) for j, nm in enumerate(("one", "p0", "p2", "p4", "a97", "big", "wb"))]
               + [(nm, (T.W16, 144 * j)) for j, nm in enumerate(("w", "wn"))])
 
     def slot(nm):
@@ -378,33 +424,38 @@ def rank_program(g, core, T, topo):
     vtt(T.RHS[:, 16:24], T.RK[:, 1:16:2], T.RK[:, 0:16:2], A.subtract, ["RK"], ["RHc"])
     iota(T.CST[:, 0:64], [[0, 64]], 1536 * 4096, -1536 * 4096 - EOFF, ["CSa"])
     iota(T.CST[:, 64:128], [[0, 64]], 0, 0, ["CSb"])
-    lin(T.NI4[:], T.IDB[:], -4096.0, 0.0, ["IDB"], ["NI4"], "cst", True)
-    lin(T.PI4[:], T.IDB[:], 4096.0, 0.0, ["IDB"], ["PI4"], "cst", True)
-    cp(T.ID16[:], T.IDB[:], ["IDB"], ["ID16"], "cst", True)
+    put(T.NI4[:], 1, [(0, -4096)], [], "NI4")
+    put(T.PI4[:], 1, [(0, 4096)], [], "PI4")
+    put(T.ID16[:], 1, [(0, 1)], [], "ID16")
     for p in allp:
         cp(T["E%d" % p][:], T.ZB[:, 0:136], ["ZB"], ["E%d" % p], "zero", True)
     fore[0] = 0.0
     aff(T.IDF[:], T.ONF[:], [[-1, 128]], A.is_equal, 0.0, 0, 1, ["ONF"], ["IDF"])
-    cp(T.W16[:], T.ZB[:, 0:288], ["ZB"], ["W16"], "zero", True)
-    iota(T.KT[:, 256:320], [[128, 4], [0, 16]], 2048, 1, ["KT2"], True)
+    aff(T.W16[:], T.ZB[:, 0:288], [[0, 288]], A.is_ge, 0.0, 0, 0, ["ZB"], ["W16"])
     put(slot("p2"), 16, ((2, 1), (3, 1)), ["WZ"], "Zp2")
     put(slot("p4"), 16, ((4, 1), (5, 1)), ["WZ"], "Zp4")
     put(slot("big"), 16, ((0, -BIG),), ["WZ"], "Zbig")
     lin(slot("a97"), BC8, 97.0, 0.0, ["Zone", "WZ"], ["Za97"], "cst")
-    lin(T.NI16[:], T.IDB[:], -1.0, 0.0, ["IDB"], ["NI16"], "cst", True)
+    put(T.NI16[:], 1, [(0, -1)], [], "NI16")
+    if max(RNP):
+        put(T.I15[:], 1, [(0, 1536)], [], "I15")
+        put(T.I05[:], 1, [(0, 1536 - 1040)], [], "I05")
     aff(T.BLK[:], T.ONB[:], [[-16, 8], [0, 16]], A.is_ge, 0.0, 0, 1, ["ONB"], ["BLK"])
     aff(T.BLK[:], T.BLK[:], [[16, 8], [0, 16]], A.is_ge, 0.0, 15, -1, ["BLK"], ["BLK"])
     aff(T.E4[:], T.ZB[:, 0:128], [[-16, 8], [0, 16]], A.not_equal, -BIG / 2, -4, 1, ["ZB"], ["E4"])
-    aff(T.OB[:], T.ZB[:, 0:128], [[-16, 8], [0, 16]], A.not_equal, 1.0, -4, 1, ["ZB"], ["OB"])
-    aff(T.OB[:], T.OB[:], [[-16, 8], [0, 16]], A.not_equal, 1.0, -5, 1, ["OB"], ["OB"])
-    aff(T.SB[:], T.ZB[:, 0:240], [[1, 15], [0, 16]], A.not_equal, -BIG, -7, 0, ["ZB"], ["SB"])
-    iota(T.I4B[:], [[4, 256]], 4, 0, ["I4B"])
+    if ACC:
+        aff(T.EH[:], T.ZB[0:16, 0:256], [[-8, 2], [-1, 8], [0, 16]], A.not_equal, -BIG, 0, 1, ["ZB"], ["EH"])
+    else:
+        aff(T.SB[:], T.ZB[:, 0:240], [[1, 15], [0, 16]], A.not_equal, -65536 * BIG, -7, 0, ["ZB"], ["SB"])
+    iota(T.I4B[:], [[4, 256]], 1028, 0, ["I4B"])
+    iota(T.NJ[:], [[1, 512]], 0, 0, ["NJ"])
+    iota(T.BI[:], [[1, 320]], 0, 320, ["BI"])
     aff(T.E8[:], T.ONF[0:8, :], [[-1, 8], [0, 16]], A.is_equal, 0.0, 0, 1, ["ONF"], ["E8"])
     iota(T.thF[:, 1:2], [[0, 1]], -4096, -4096, ["thG"])
     iota(T.DW[:], [[16, 16]], DUMP, 1, ["DW"])
     iota(T.NV0[:], [[2, 256]], 2048, 0, ["NV0"])
     iota(T.NC[:], [[2, 256]], 2048, 0, ["NC"])
-    iota(T.BD[:, 0:2], [[128, 2]], 1, 1, ["BD"])
+    iota(T.BD[:], [[128, 2]], 1, 1, ["BD"])
     ms(T.WD[:], 0.0, ["WD"], half=False)
     for k in range(1, 4):
         for j in range(k):
@@ -413,7 +464,8 @@ def rank_program(g, core, T, topo):
     iota(T.KF[:, 2048:3072], [[1, 1024]], 2048, 0, ["KFt"])
     fore[0] = 0.0
 
-    TAB = {"e1": ((1, 1),), "sc": tuple((k, 2 ** (11 - k)) for k in range(12)), "e12": ((12, 1),), "c12": (),
+    TAB = {"sc": tuple((k, 2 ** (11 - k)) for k in range(12)), "e1": ((1, 1),), "e12": ((12, 1),),
+           "ns": ((0, -0.125), (8, -0.125)), "nb": ((3, -0.5), (11, -0.5), (4, -320)),
            "s8": tuple((k + o, 8 ** (3 - k)) for o in (0, 8) for k in range(4)), "b8": tuple((k + 8, 8 ** (3 - k)) for k in range(4))}
     NT = len(TAB)
     CI = dict((nm, j) for j, nm in enumerate(list(TAB) + ["me", "mo", "w", "wn"]))
@@ -423,23 +475,23 @@ def rank_program(g, core, T, topo):
     ms(T.CT[:], 0.0, ["CT" + nm for nm in CI], half=False)
     for nm in TAB:
         c, ck = T.CT[0:16, CI[nm]:CI[nm] + 1], ["CT" + nm]
-        if nm == "c12":
-            aff(c, c, [[0, 1]], A.is_equal, -1024.0, -12, 1, ck, ck)
         for k, v in TAB[nm]:
             aff(c, c, [[0, 1]], A.not_equal, float(v), -k, 1, ck, ck)
-    u = 2.0 ** -20
     for nm, o in (("me", 0), ("mo", 16)):
         c, ck = T.CT[:, CI[nm]:CI[nm] + 1], ["CT" + nm]
-        aff(c, c, [[0, 1]], A.is_gt, u, 16 if o else -12, -1 if o else 1, ck, ck)
-        for k, v in ((13, -5.5 * u), (14, -5.5 * u)) + (((15, 0.0),) if o else ()):
-            aff(c, c, [[0, 1]], A.not_equal, v, -k - o, 1, ck, ck)
+        aff(c, c, [[0, 1]], A.is_ge, 2.0 ** -20, -13 - o, 1, ck, ck)
+        if o:
+            aff(c, c, [[0, 1]], A.is_ge, 0.0, -o, 1, ck, ck)
+        if ACC:
+            aff(c, c, [[0, 1]], A.not_equal, -2.0 ** -20, -12 - o, 1, ck, ck)
+    aff(T.EQ8[:], T.ONF[0:16, :], [[1, 16], [0, 8]], A.is_equal, 0.0, 0, -1, ["ONF"], ["EQ8"])
     aff(T.EQ[:], T.ONF[0:16, :], [[0, 8], [1, 16]], A.is_equal, 0.0, 0, -1, ["ONF"], ["EQ"])
     aff(T.EQ2[:], T.ONF[0:32, :], [[0, 4], [1, 32]], A.is_equal, 0.0, 0, -1, ["ONF"], ["EQ2"])
 
     fore[0] = 30.0
-    cp(T.KDf[:], T.KD[:], ["KD0", "KD1"], ["KDf"])
+    cp(T.KDh[:], T.KD[:], ["KD0", "KD1"], ["KDh"])
     bk = T[bS[0]]
-    PE(lambda e: [e.matmul(bk[:, j:256:2], T.KDf[:, 128 * j:128 * j + 128], T.PERM[:], True, True) for j in range(2)], 1024, ["KDf", "PERM"], [bS[0]], "kT")
+    PE(lambda e: [e.matmul(bk[:, j:256:2], T.KDh[:, 128 * j:128 * j + 128], T.PERM[:], True, True) for j in range(2)], 256, ["KDh", "PERM"], [bS[0]], "kT")
     cp(T.KT[:, 0:256], bk[:, 0:256], [], ["KT0", "KT1", bS[0]], "KT")
     vtt(T.LM[:], bk[:, 0:256:2], T.OWT[:], A.is_equal, ["OWT"], ["LM", bS[0]], "LM", two=False)
     lin(QT(4, 2048, 16), T.LM[:], 2560.0, 0.0, ["LM"], ["QT0_4", "QT1_4"], "LM", True)
@@ -464,11 +516,6 @@ def rank_program(g, core, T, topo):
                                for i in range(4)], 512, ["NI8"] + ["QT%d_%d" % (c, k) for k in range(8)], [nb[j]], "nq")
             cp(T.NW[:, 512 * j:512 * j + 512], T[nb[j]][:, 0:512], [], ["NW%d" % j, nb[j]], "nw")
     fore[0] = 0.0
-    ms(QT(2052, 2560, 16), 2560.0, ["QT2_4"])
-    digits((2,), 256, 64, T.KT, ["KT2"], range(4))
-    PE(lambda e: [e.matmul(bk[:, 128 * i:128 * i + 128], QT(2048 + 128 * i, 2176 + 128 * i), T.NI8[:], True, True) for i in range(4)],
-       512, ["NI8"] + ["QT2_%d" % k for k in range(8)], [bS[0]], "nq")
-    cp(T.NW[:, 2048:MW], bk[:, 0:512], [], ["NT", bS[0]], "nw")
 
     cp(LI(0, 0, 128), T.stI[:], ["stI"], ["L0_%d" % p for p in allp])
     cp(LI(5, 0, 128), T.cuI[:], ["cuI"], ["L5_%d" % p for p in allp])
@@ -484,17 +531,22 @@ def rank_program(g, core, T, topo):
     DMA(T.EW[:], T.env[:], ["PWf"], ["EW"], "env", 512, 4096, -210.0)
     cp(col("w"), T.wI[:], ["wI"], ["w"])
     lin(slot("w"), BC8, col("w"), 0.0, ["W16", "Zone", "w"], ["Zw"], "Zw")
+    lin(slot("wb"), BC8, col("w"), 0.0, ["WZ", "Zone", "w"], ["Zwb"], "Zw")
 
     bc = T[bS[1]]
-    PE(lambda e: [e.matmul(bc[:, 0:NT], T.EQ[:], T.CT[0:16, 0:NT], True, True), e.matmul(bc[:, NT:NT + 2], T.EQ2[:], T.CT[:, NT:NT + 2], True, True)],
-       512, ["EQ", "EQ2"] + ["CT" + nm for nm in CI], [bS[1]], "cols")
+    PE(lambda e: [e.matmul(bc[:, 0:1], T.EQ8[:], T.CT[0:16, 0:1], True, True), e.matmul(bc[:, 1:NT], T.EQ[:], T.CT[0:16, 1:NT], True, True),
+                  e.matmul(bc[:, NT:NT + 2], T.EQ2[:], T.CT[:, NT:NT + 2], True, True)], 768, ["EQ", "EQ2", "EQ8"] + ["CT" + nm for nm in CI], [bS[1]], "cols")
     cp(T.COL[:, 0:NT + 2], bc[:, 0:NT + 2], [], list(TAB) + ["me", "mo", bS[1]], "cols")
-    op([("s", vc(2), 0.0, lambda e: e.activation(T.BD[:, 2:4], T.BD[:, 0:2], F.Square)),
-        ("v", vc(2), 0.0, lambda e: e.tensor_tensor(T.BD[:, 2:4], T.BD[:, 0:2], T.BD[:, 0:2], A.mult))], ["BD"], ["BD2"], "bd")
-    lin(T.BD[:, 0:2], T.BD[:, 2:4], -1.0, -65536.0, ["BD2"], ["BD"], "bd")
-    lin(T.BASE[:], T.I4B[:], col("e12"), col("c12"), ["I4B", "e12", "c12"], ["BASE"], "base", True)
+    lin(T.FI[:], T.BI[:], col("sc"), 0.0, ["BI", "sc"], ["FI"], "fi")
+    vts(T.FB[:], T.FI[:], 2048, None, A.bitwise_and, None, ["FI"], ["FB"], "fb")
+    lin(T.BK[:], T.FB[:], 1.0, -1024.0, ["FB"], ["BK"], "bk")
+    for gr in range(8):
+        DMA(T.BW[16 * gr:16 * gr + 16, :], T.BK[:], ["BK"], ["BW%d" % gr], "bw", 80, 640, -100.0)
+    vtt(T.BD[:], T.BD[:], T.BD[:], A.mult, [], ["BD"], "bd")
+    lin(T.BD[:], T.BD[:], (1.0 if ACC else -1.0) / 65536, -12.0, [], ["BD"], "bd")
+    lin(T.BASE[:], T.I4B[:], col("e12"), 0.0, ["I4B", "e12"], ["BASE"], "base")
     lin(T.NV0[:], T.NV0[:], 1.0, col("e1"), ["e1"], ["NV0"], "cst")
-    lin(T.NV1[:], T.NV0[:], 1.0, 512.0, ["NV0"], ["NV1"], "cst")
+    lin(T.NW[:, 2048:MW], T.NJ[:], col("ns"), col("nb"), ["NJ", "ns", "nb"], ["NT"], "nt")
     lin(T.NC[:], T.NC[:], col("s8"), col("b8"), ["s8", "b8"], ["NC"], "cst")
     cp(T.thF[:, 0:1], T.thI[:], ["thI"], ["thF"])
     PE(lambda e: e.matmul(bc[:, 0:2], T.E8[:], T.thF[:], True, True), 256, ["E8", "thF", "thG"], [bS[1]], "th")
@@ -507,13 +559,13 @@ def rank_program(g, core, T, topo):
                                                       first and q == 0, end and q == 15) for q in range(16)],
            1024 + 256 * len(more), ["Z" + z] + R, [bank], nm)
 
-    def rows(bank, z, src, m0, m1, first, end, R, nm):
+    def rows(bank, z, src, l0, n, m0, m1, first, end, R, nm):
         wz, z0 = ZS[z]
-        PE(lambda e: [e.matmul(T[bank][:, 0:128], wz[:, z0 + 15 - m:z0 + 143 - m], src[:, 128 * m:128 * m + 128], first and m == m0, end and m == m1 - 1)
-                      for m in range(m0, m1)], 128 * (m1 - m0), R + ["Z" + z], [bank], nm)
+        PE(lambda e: [e.matmul(T[bank][:, 0:n], wz[:, z0 + 15 - m:z0 + 143 - m], src[:, l0 + n * m:l0 + n * m + n], first and m == m0, end and m == m1 - 1)
+                      for m in range(m0, m1)], max(64, n) * (m1 - m0), R + ["Z" + z], [bank], nm)
 
-    def sums(e, bank, src, c0, C, wts, alone):
-        return [e.matmul(T[bank][0:2 * C, r:8 * wts.shape[1]:8], src[:, 16 * c0 + r:16 * (c0 + C):8], wts, alone, alone) for r in range(8)]
+    def sums(e, bank, x, w, c0, C, alone):
+        return [e.matmul(T[bank][0:2 * C, r:8 * w.shape[1]:8], x[:, 16 * c0 + r:16 * (c0 + C):8], w, alone, alone) for r in range(8)]
 
     def lanes(X, c0, C):
         return X[:, 16 * c0:16 * (c0 + C)]
@@ -534,32 +586,21 @@ def rank_program(g, core, T, topo):
         for nm, a, n in pcs:
             nt, ct, nm = lanes(T.CN, a, n), lanes(T.CC, a, n), ps + nm
             gather(nt, T.NW[:, 0:win], LI(k, a, n), lk + nk, ["CN" + nm], "node")
-            if k or not t:
+            if t and k == 1:
+                gatherop(ct, T.XS0[:], LI(9, a, n), nt, A.is_ge, ["XS%d" % x for x in allp] + ["L9_%d" % p, "CN" + nm], ["CC" + nm], "cmp")
+            elif k or not t:
                 sl = (11 if t else 5) + k
                 gatherop(ct, T.XW[:], LI(sl, a, n), nt, A.is_ge, ["XW", "L%d_%d" % (sl, p), "CN" + nm], ["CC" + nm], "cmp")
             else:
                 gatherop(ct, T.NW[:, 0:win], LI(k, a, n), lanes(T.VL, a, n), A.is_le, lk + nk + vl(a, n), ["CC" + nm], "cmp")
-        cn = ["CN" + ps + x[0] for x in pcs]
-        if not EARLY:
-            PE(lambda e: sums(e, bP[p], T.CN, c0, C, T.RHS[:, 8:24], True), 512, ["RHb", "RHc"] + cn, [bP[p]], "kid")
-            PE(lambda e: sums(e, bC[p], T.CC, c0, C, BC8, True), 512, ["Zone"] + ["CC" + ps + x[0] for x in pcs], [bC[p]], "count")
-            ma, mb_, ft, fu = (T[x][0:nr, 64 * p:64 * p + 64] for x in ("MA", "MB", "FT", "FU"))
-            vts(ma, tc[0:nr, 0:64], 8.5, None, A.is_ge, None, [], ["MA" + ps, bC[p]], "m")
-            vtt(mb_, ma, tp[0:nr, 64:128], A.mult, ["MA" + ps], ["MB" + ps, bP[p]], "t", two=False)
-            vtt(ft, mb_, tp[0:nr, 0:64], A.add, ["MB" + ps], ["FT" + ps, bP[p]], "f", two=False)
-            vts(fu, ft, 4095, None, A.bitwise_and, None, ["FT" + ps], ["FU" + ps], "and")
-            lin(T["E" + ps][0:nr, 1:17:2, :], fu, 1.0, -float(EOFF), ["FU" + ps], ["E" + ps], "e")
-            PE(lambda e: [e.matmul(tc[:, 64:64 + C], T["E" + ps][0:nr, 1 - h:17 - h, :], T.ID16[0:nr, h:nr:2], h == 0, h == 1) for h in range(2)],
-               128, ["ID16", "E" + ps], [bC[p]], "turn")
-            lin(LI(k + 1, c0, C), tc[:, 64:64 + C], 1.0, float(EOFF), [], ["L%d_%d" % (k + 1, p), bC[p]], "list")
-            return
-        PE(lambda e: sums(e, bC[p], T.CN, c0, C, T.RHS[:, 0:16], True), 512, ["RHa", "RHb"] + cn, [bC[p]], "kid")
-        PE(lambda e: [e.matmul(tp[0:nr, 0:128], T.ONB[0:2, 0:nr], T.CST[:], True, False)] + sums(e, bP[p], T.CN, c0, C, T.RHS[:, 8:24], False),
-           640, ["ONB", "CSa", "CSb", "RHb", "RHc"] + cn, [bP[p]], "kid")
+        cn = ["CN" + ps + x[0] for x in pcs] + ["RHa", "RHb", "RHc"]
+        PE(lambda e: sums(e, bC[p], T.CN, T.RHS[:, 0:16], c0, C, True), 512, cn, [bC[p]], "kid")
+        PE(lambda e: [e.matmul(tp[0:nr, 0:128], T.ONB[0:2, 0:nr], T.CST[:], True, False)] + sums(e, bP[p], T.CN, T.RHS[:, 8:24], c0, C, False),
+           640, ["ONB", "CSa", "CSb"] + cn, [bP[p]], "kid")
         lin(T.U[0:nr, 128 * p:128 * p + 128], tc[0:nr, 0:128], 1.0 / 4096, 1536 - EOFF / 4096.0, [], ["U" + ps, bC[p]], "u")
         PE(lambda e: [e.matmul(tp[0:nr, o:o + 64], w[0:nr, 0:nr], T.U[0:nr, 128 * p + a:128 * p + a + 64], False, w is T.PI4)
                       for o, w, a in ((0, T.NI4, 64), (64, T.NI4, 0), (64, T.PI4, 64))], 192, ["NI4", "PI4", "U" + ps], [bP[p]], "fix")
-        PE(lambda e: sums(e, bC[p], T.CC, c0, C, BC8, True), 512, ["Zone"] + ["CC" + ps + x[0] for x in pcs], [bC[p]], "count")
+        PE(lambda e: sums(e, bC[p], T.CC, BC8, c0, C, True), 512, ["Zone"] + ["CC" + ps + x[0] for x in pcs], [bC[p]], "count")
         ma, mb_ = T.MA[0:nr, 64 * p:64 * p + 64], T.MB[0:nr, 64 * p:64 * p + 64]
         vts(ma, tc[0:nr, 0:64], 8.5, None, A.is_ge, None, [], ["MA" + ps, bC[p]], "m")
         vtt(mb_, ma, tp[0:nr, 64:128], A.mult, ["MA" + ps], ["MB" + ps, bP[p]], "t", two=False)
@@ -579,19 +620,19 @@ def rank_program(g, core, T, topo):
         nm, again, rk = str(t) + str(p), ["o%d" % p] if t else [], []
         for n2, a, n in cut(c0, C, RP):
             gatherop(lanes(T.CR, a, n), T.RW[:, 0:win], LI(4, a, n), lanes(X, a, n), A.is_gt,
-                     ["L4_%d" % p, "RW"] + (vl(a, n) + ["RTa", "RTb"] if t else ["XS%d" % p]) + again, ["CR" + nm + n2], "R")
+                     ["L4_%d" % p, "RW"] + (vl(a, n) + ["RT"] if t else ["XS%d" % p]) + again, ["CR" + nm + n2], "R")
             rk.append("CR" + nm + n2)
         i1, acc = T.FT[:, c0:c0 + C], T[bP[p]][:, 0:C]
         if t:
             wrap(bP[p], 0, "a97", T.CR, c0, C, rk, "a")
             vtt(i1, T.WC[:, c0:c0 + C], acc, A.add, ["WC%d" % p], ["FT%d" % p, bP[p]], "i1", two=False)
         else:
-            wrap(bP[p], 0, "w", T.XS0, c0, C, ["XS%d" % p], "wc", end=False)
+            wrap(bP[p], 0, "wb", T.XS0, c0, C, ["XS%d" % p], "wc", end=False)
             wrap(bP[p], 0, "a97", T.CR, c0, C, rk, "a", first=False)
             cp(i1, acc, [], ["FT%d" % p, bP[p]], "i1")
         low(p, i1, "FT%d" % p, LI(10, c0, C), ["IX" + nm])
-        for n2, a, n in cut(c0, C, ENDS[t][p]):
-            n2 = nm + n2
+        for j, n in enumerate(ENDS[t][p]):
+            n2, a = nm + "_%d" % j, c0 + sum(ENDS[t][p][:j])
             gatherop(lanes(T.SS, a, n), T.EW[:], LI(10, a, n), lanes(X, a, n), A.add, ["IX" + nm, "EW"] + (vl(a, n) if t else ["XS%d" % p]) + again, ["SS" + n2], "env")
             vts(lanes(T.MM, a, n), lanes(T.SS, a, n), 256.0, -256.0, A.is_ge, A.mult, ["SS" + n2], ["MM" + n2], "mm", half=True)
             after(n2, a, n)
@@ -600,46 +641,67 @@ def rank_program(g, core, T, topo):
         rid, pid = topo.addr(dst)[0], topo.addr(dst)[1]
         k = dict(dst_ids=[DstId(rid=rid, pnc=pid)], dma_engine_mask=topo.mask(core, dst), remote_sem=T.sem[rs])
         tr = RemoteDMATransfer(srcs=srcs, dsts=[out], alu_op=1, **k) if len(srcs) > 1 else RemoteDMATransfer(src=srcs[0], dst=out, **k)
-        op([("gr", RCALL, 0.0, lambda e: e.remote_dma_fused([tr], local_sem=T.sem[ls]))], R, [nm], nm, lat=max(0.35, kb / RBW), tok=(ls, len(topo.engines(core, dst))))
+        op([("gr", RCALL, 0.0, lambda e: e.remote_dma_fused([tr], local_sem=T.sem[ls]))], R, [nm], nm, lat=kb / RBW, rows=16, tok=(ls, len(topo.engines(core, dst))))
         op([("arr", 0.0, 0.0, None)], [nm], W, nm + "arr", lat=RLAT - 0.3, tok=(rs, len(topo.engines(prv if dst == nxt else nxt, core))))
 
     def splits(t):
         win, off, nk = (MW if t else 2048), LI(4, 0, 16), NWK + (["NT"] if t else [])
         vk, far = ["SS%d0_0" % t, "MM%d0_0" % t], T[bC[0]]
-        gather(T.OQ[:], PWIN, off, ["L4_0"] + PWK, ["OQ"], "oq")
-        op([("s", 0.055, S * CYC, lambda e: e.activation(T.LF[:], T.NW[:, 0:win].indirect(off), F.Sign, bias=1.5))], ["L4_0"] + nk, ["LF"], "lf")
-        gather(T.RF[:], T.RW[:, 0:win], off, ["L4_0", "RW"] + (["RTa", "RTb"] if t else []), ["RF"], "rf")
-        PE(lambda e: e.matmul(T[bS[0]][:, 0:S], T.OB[:], T.OQ[:], True, True), S, ["OB", "OQ"], [bS[0]], "FR")
-        lin(T.FI[:], T[bS[0]][:, 0:S], col("sc"), 0.0, ["sc"], ["FI", bS[0]], "fi")
-        vts(T.FB[:], T.FI[:], 2048, None, A.bitwise_and, None, ["FI"], ["FB"], "fb")
-        vtt(T.FBI[:], T.FB[:], T.BASE[:], A.add, ["FB", "BASE"], ["FBI"], "fbi")
+        bwk = ["L4_0"] + ["BW%d" % gr for gr in range(8)]
+        gatherop(T.FBI[:], T.BW[:], off, T.BASE[:], A.add, bwk + ["BASE"], ["FBI"], "fbi")
         for fx, c in (("FE", "me"), ("FO", "mo")):
             lin(T[fx][:], T.FBI[:], col(c), 0.0, ["FBI", c], [fx], "fx", True)
+        op([("s", 0.055, S * CYC, lambda e: e.activation(T.LF[:], T.NW[:, 0:win].indirect(off), F.Sign, bias=1.5))], ["L4_0"] + nk, ["LF"], "lf")
+        gather(T.RF[:], T.RW[:, 0:win], off, ["L4_0", "RW"] + (["RT"] if t else []), ["RF"], "rf")
         PE(lambda e: e.matmul(far[:, 0:S], T.E4[:], T.LF[:], True, False), S, ["E4", "LF"], [bC[0]], "leaf")
-        for m, (hf, gs) in enumerate([(0, (2 * m, 2 * m + 1)) for m in range(4)] + [(1, range(4 * m, 4 * m + 4)) for m in range(2)]):
-            bn, lo, jk = bS[(m + 1) % 2], 128 * hf, T.JK[:, 512 * m:512 * m + 512]
+        for gr in range(8 if ACC else 0):
+            bn, fx, p0 = (bS + bQ)[gr % 3], (T.FE, T.FO)[gr % 2], 32 * (gr // 2)
+            PE(lambda e, bn=bn, fx=fx, p0=p0: [e.matmul(T[bn][:, 128 * hf:128 + S * hf], fx[p0:p0 + 32, 128 * hf:128 * hf + 128], T.FBI[p0:p0 + 32, 0:128 + 128 * hf], True, True)
+                                               for hf in range(2)], 384, ["FE", "FO", "FBI"], [bn], "dot")
+            op([("s", vc(128) + vc(S) + 0.04, 0.0,
+                 lambda e, bn=bn, gr=gr: [e.activation(T.JK[:, 384 * gr + 128 * hf:384 * gr + 128 + S * hf], T[bn][:, 128 * hf:128 + S * hf], F.Relu, bias=T.BD[:, hf:hf + 1],
+                                                       accum_out=T.DM[:, 8 * hf + gr:8 * hf + gr + 1]) for hf in range(2)])], ["BD"], ["DM%d" % gr, bn], "red")
+        if ACC:
+            bd = T[bS[1]]
+            PE(lambda e: e.matmul(bd[0:16, 0:128], T.DM[:], T.IDF[:], True, True), 512, ["IDF"] + ["DM%d" % gr for gr in range(8)], [bS[1]], "dupT")
+            op([("s", vc(128), 0.0, lambda e: e.activation(T.DUT[:], bd[0:16, 0:128], F.Sign)),
+                ("v", vc(128), 0.0, ts(T.DUT[:], bd[0:16, 0:128], 0.0, None, A.is_gt))], [], ["DUT", bS[1]], "dut")
+            PE(lambda e: [e.matmul(far[:, 128 * hf:128 * hf + 128], T.EH[:, 128 * hf:128 * hf + 128], T.DUT[:], False, False) for hf in range(2)],
+               S, ["EH", "DUT"], [bC[0]], "dup")
+        for m, (hf, gs) in enumerate([] if ACC else [(0, (2 * m, 2 * m + 1)) for m in range(4)] + [(1, range(4 * m, 4 * m + 4)) for m in range(2)]):
+            bn, lo, jk = (bS + bQ)[m % 3], 128 * hf, T.JK[:, 512 * m:512 * m + 512]
             n = S - lo
             for j in range(0, len(gs), 2):
                 PE(lambda e, bn=bn, lo=lo, j=j, n=n, p0=16 * gs[j]: [e.matmul(T[bn][:, n * (j + a):n * (j + a + 1)], fx[p0:p0 + 32, lo:lo + 128],
                                                                               T.FBI[p0:p0 + 32, lo:S], True, True) for a, fx in enumerate((T.FE, T.FO))],
                    2 * n, ["FE", "FO", "FBI"], [bn], "dot")
-            op([("s", vc(512), 0.0, lambda e, bn=bn, hf=hf, jk=jk: e.activation(jk, T[bn][:], F.Relu, scale=65536.0, bias=T.BD[:, hf:hf + 1]))],
-               ["BD"], ["JK%d" % m, bn], "red")
+            op([("s", vc(512), 0.0, lambda e, bn=bn, hf=hf, jk=jk: e.activation(jk, T[bn][:], F.Relu, bias=T.BD[:, hf:hf + 1])),
+                ("v", vc(512), 0.0, ts(jk, T[bn][:], T.BD[:, hf:hf + 1], 0.0, A.add, A.max))], ["BD"], ["JK%d" % m, bn], "red", pref=0)
             PE(lambda e, m=m, lo=lo, gs=gs, n=n: [e.matmul(far[:, lo:S], T.SB[:, 112 - 16 * gr:240 - 16 * gr], T.JK[:, 512 * m + n * j:512 * m + n * j + n], False, False)
                                                   for j, gr in enumerate(gs)], 512, ["SB", "JK%d" % m], [bC[0]], "dup")
         bv = T[bP[0]]
-        PE(lambda e: [e.matmul(bv[:, a:a + S], w[:], x[:, 0:S], x is T.RF, x is T.MM)
-                      for a, sg in ((0, T.NI16), (S, T.ID16)) for w, x in ((T.ID16, T.RF), (sg, T.SS), (sg, T.MM))],
-           6 * S, ["ID16", "NI16", "RF"] + vk, [bP[0]], "vv")
+        PE(lambda e: [e.matmul(bv[:, 0:S], w[:], x[:, 0:S], x is T.RF, x is T.MM) for w, x in ((T.ID16, T.RF), (T.NI16, T.SS), (T.NI16, T.MM))],
+           3 * S, ["ID16", "NI16", "RF"] + vk, [bP[0]], "vv")
         op([("s", vc(S), 0.0, lambda e: e.activation(T.AD[:], bv[:, 0:S], F.Abs))], [], ["AD", bP[0]], "abs")
-        lin(T.RS2[:], bv[:, S:2 * S], 0.5, -0.25, [], ["RS2", bP[0]], "rs2")
+        PE(lambda e: [e.matmul(T[bS[0]][:, 0:S], T.ID16[:], x[:, 0:S], x is T.RF, x is T.MM) for x in (T.RF, T.SS, T.MM)], 3 * S, ["ID16", "RF"] + vk, [bS[0]], "vv")
+        lin((T.RS2 if RNP[t] else T.RSI)[:], T[bS[0]][:, 0:S], 0.5, 1039.75 if RNP[t] else -0.25, [], ["RS2", bS[0]], "rs2")
         PE(lambda e: e.matmul(far[:, 0:S], T.BLK[:], T.AD[:], False, True), S, ["BLK", "AD"], [bC[0]], "far")
         vts(T.SP[:], far[:, 0:S], T.THC[:, 0:1], None, A.is_ge, None, ["THC"], ["SP", bC[0]], "sp")
         RN, rn, c0 = (T.YR1, "YR1", 0) if t else (T.RW, "RT", 2048)
-        vtt(RN[:, c0:c0 + 512:2], T.RF[:], T.SP[:], A.mult, ["RF", "SP"], [rn + "a"], "rna")
-        vtt(RN[:, c0 + 1:c0 + 512:2], T.RS2[:], T.SP[:], A.mult, ["RS2", "SP"], [rn + "b"], "rnb")
+        b0 = T[bS[0]]
+        if RNP[t]:
+            PE(lambda e: [e.matmul(b0[:, 0:512:2], T.ID16[:], T.RF[:], True, False), e.matmul(b0[:, 0:512:2], T.I15[:], T.SP[:], False, True),
+                          e.matmul(b0[:, 1:512:2], T.ID16[:], T.RS2[:], True, False), e.matmul(b0[:, 1:512:2], T.I05[:], T.SP[:], False, True)],
+               4 * S, ["ID16", "I15", "I05", "RF", "RS2", "SP"], [bS[0]], "rn")
+            op([("s", vc(512), 0.0, lambda e: e.activation(RN[:, c0:c0 + 512], b0[:], F.Relu, bias=-1536.0)),
+                ("v", vc(512), 0.0, ts(RN[:, c0:c0 + 512], b0[:], -1536.0, 0.0, A.add, A.max))], [], [rn, bS[0]], "rn")
+        else:
+            vtt(RN[:, c0:c0 + 512:2], T.RF[:], T.SP[:], A.mult, ["RF", "SP"], [rn + "a"], "rna")
+            vtt(RN[:, c0 + 1:c0 + 512:2], T.RSI[:], T.SP[:], A.mult, ["RS2", "SP"], [rn + "b"], "rnb")
+            op([("arr", 0.0, 0.0, None)], [rn + "a", rn + "b"], [rn], "free")
         s2 = bS[1]
-        wrap(s2, 0, "big", T.SP, 0, 16, ["IDF", "DW", "SP"], "wsp", False, True, [lambda e: e.matmul(T[s2][:, 0:16], T.IDF[:], T.DW[:], True, False)])
+        PE(lambda e: e.matmul(T[s2][:, 0:16], T.IDF[:], T.DW[:], True, False), 256, ["IDF", "DW"], [s2], "dump")
+        wrap(s2, 0, "big", T.SP, 0, 16, ["SP"], "wsp", False, True)
         if t:
             cp(T.FW[:, 64:80], off, ["L4_0"], ["FW"])
         vtt(T.TG[:, 0:16], T.FW[:, 64:80], T[s2][:, 0:16], A.max, ["FW"], ["TG1", s2], two=False)
@@ -647,8 +709,7 @@ def rank_program(g, core, T, topo):
         cp(tg, T.TG[:, 0:16], ["TG1"], ["TGL"])
         if not t:
             op([("v", 0.042, 2.3 * S * CYC, lambda e: e.tensor_tensor(T.NW[:].indirect(tg), T.XF[:], T.Q2[:], A.add))], ["TGL", "XF", "Q2"], NWK + ["NT"], "scN")
-        nv = "NV1" if t else "NV0"
-        op([("v", 0.042, 2.3 * S * CYC, lambda e: e.tensor_copy(T.KF[:].indirect(tg), T[nv][:]))], ["TGL", nv], ["KF0", "KF1", "KFt"], "scF")
+        op([("v", 0.042, 2.3 * S * CYC, ts(T.KF[:].indirect(tg), T.NV0[:], 1.0, 512.0 * t, A.mult, A.add))], ["TGL", "NV0"], ["KF0", "KF1", "KFt"], "scF")
 
     nq = [0]
 
@@ -656,10 +717,7 @@ def rank_program(g, core, T, topo):
         bq = bQ[nq[0] % 2]
         nq[0] += 1
         wrap(bq, 0, z, src, c0, C, R, "ws")
-        if z == "p4":
-            lin(out, T[bq][:, 0:C], 1.0, GOFF, ["THC"], W + [bq], "slist")
-        else:
-            cp(out, T[bq][:, 0:C], [], W + [bq], "slist")
+        cp(out, T[bq][:, 0:C], [], W + [bq], "slist")
 
     for p, (c0, C) in enumerate(PARTS):
         fore[0] = -LAG * p
@@ -696,22 +754,29 @@ def rank_program(g, core, T, topo):
     vts(T.D3[:], T.D2[:], 7 * 512, None, A.bitwise_and, None, ["D2"], ["D3"], "d3")
     lin(T.Q2[:], T.D3[:], -1.0 / 4096, 0.0, ["D3"], ["Q2"], "q2")
 
-    ns, sent = [0], [[] for p in allp]
+    ns, sent, held = [0], [[] for p in allp], []
     for p in allp:
         fore[0] = -LAG * p
 
         def hand(nm, c0, C, p=p):
+            held.append((nm, C))
+            C = sum(x[1] for x in held)
+            if C < LEAST:
+                return
+            c0 -= C - held[-1][1]
             send([lanes(T.SS, c0, C), lanes(T.MM, c0, C)], lanes(T.VL, c0, C), nxt, "aA%d" % ns[0], "lA%d" % ns[0],
-                 ["SS" + nm, "MM" + nm], ["VL" + nm], "send" + nm, 4 * C)
+                 [x + y[0] for x in ("SS", "MM") for y in held], ["VL" + nm], "send" + nm, 4 * C)
+            del held[:]
             ns[0] += 1
             came.append(("VL" + nm, c0, C))
             sent[p].append("send" + nm)
         outcome(0, p, hand)
     fore[0] = 0.0
+    cp(T.KDf[:], T.KD[:], ["KD0", "KD1"], ["KDf"])
     DMA(T.KF[0:128:16, 0:2048], T.KDf[:, 0:128], ["KDf", "PWf"], ["KF0"], "kf0", 64, 512, -300.0)
     DMA(T.KF[1:128:16, 0:2048], T.KDf[:, 128:256], ["KDf", "PWf"], ["KF1"], "kf1", 64, 512, -300.0)
     splits(0)
-    DMA(T.yr[:, 0:512], T.RW[:, 2048:MW], ["RTa", "RTb"], ["oyr0"], "oyr0", 128, 1024)
+    DMA(T.yr[:, 0:512], T.RW[:, 2048:MW], ["RT"], ["oyr0"], "oyr0", 128, 1024)
     send([T.wI[:]], T.wN[:], prv, "aw", "lw", ["wI"], ["wN"], "sendw", 1)
     cp(col("wn"), T.wN[:], ["wN"], ["wn"])
     lin(slot("wn"), BC8, col("wn"), 0.0, ["W16", "Zone", "wn"], ["Zwn"], "Zn")
@@ -722,10 +787,10 @@ def rank_program(g, core, T, topo):
         cp(T.WC[:, c0:c0 + C], T[bP[p]][:, 0:C], [], ["WC%d" % p, bP[p]], "wc")
         low(p, T.WC[:, c0:c0 + C], "WC%d" % p, LI(9, c0, C), ["L9_%d" % p])
         gather(lanes(T.LG, c0, C), T.LT[:], LI(9, c0, C), LTK + ["LTr0", "LTr1", "L9_%d" % p], ["LG%d" % p], "lg")
-        for k, z in ((12, "p4"), (13, "p0"), (14, "p2")):
+        for k, z in ((13, "p0"), (14, "p2")):
             chain(T.LG, c0, C, z, LI(k, c0, C), ["L%d_%d" % (k, p)], ["LG%d" % p])
     fore[0] = -30.0
-    rows(bQ[0], "p4", T.LG, 0, 16, True, True, ["LG%d" % p for p in allp], "cur")
+    rows(bQ[0], "p4", T.LG, 0, 128, 0, 16, True, True, ["LG%d" % p for p in allp], "cur")
     lin(T.YP[:], T[bQ[0]][:, 0:128], 1.0, GOFF, ["THC"], ["YP", bQ[0]], "yp")
     DMA(T.yp[:, 0:2048], T.YP[:], ["YP"], ["oyp0"], "oyp", 64, 512)
     for k in range(4):
@@ -735,20 +800,24 @@ def rank_program(g, core, T, topo):
     for p in allp:
         fore[0] = -LAG * p
 
-        def handsum(nm, c0, C):
-            rows(bQ[1], "wn", T.SS, c0 // 8, (c0 + C) // 8, c0 == 0, False, ["SS" + nm], "hs")
-            rows(bQ[1], "wn", T.MM, c0 // 8, (c0 + C) // 8, False, c0 + C == 128, ["MM" + nm], "hm")
+        a0, n0 = PARTS[p]
+        hb = bC[p] if p else bQ[1]
+
+        def handsum(nm, c0, C, a0=a0, n0=n0, hb=hb):
+            m0, m1 = 16 * (c0 - a0) // n0, 16 * (c0 + C - a0) // n0
+            rows(hb, "wn", T.SS, 16 * a0, n0, m0, m1, m0 == 0, False, ["SS" + nm], "hs")
+            rows(hb, "wn", T.MM, 16 * a0, n0, m0, m1, False, m1 == 16, ["MM" + nm], "hm")
         op([("arr", 0.0, 0.0, None)], sent[p] + (["RS2", "AD"] if p == 0 else []), ["o%d" % p], "free")
         outcome(1, p, handsum)
+        i1, i2, hs, hr = T.IT[:, a0:a0 + n0], T.IT[:, 128 + a0:128 + a0 + n0], T.HS[:, a0:a0 + n0], T.HR[:, a0:a0 + n0]
+        cp(i1, T[hb][:, 0:n0], [], ["H1%d" % p, hb], "H1")
+        vts(i2, i1, 2047, None, A.bitwise_and, None, ["H1%d" % p], ["H2%d" % p], "H2")
+        lin(hs, i2, 1.0, 4096.0, ["H2%d" % p], ["HS%d" % p], "H3")
+        send([hs], hr, nxt, "aH%d" % p, "lH%d" % p, ["HS%d" % p], ["HR%d" % p], "sendH%d" % p, n0 // 2)
+        DMA(T.yp[:, 2048 + 16 * a0:2048 + 16 * (a0 + n0)], hr, ["HR%d" % p], ["oyp2%d" % p], "oyp2", n0 // 2, 4 * n0)
     fore[0] = 0.0
-    i1, i2 = T.IT[:, 0:128], T.IT[:, 128:256]
-    cp(i1, T[bQ[1]][:, 0:128], [], ["H1", bQ[1]], "H1")
-    vts(i2, i1, 2047, None, A.bitwise_and, None, ["H1"], ["H2"], "H2")
-    lin(T.HS[:], i2, 1.0, 4096.0, ["H2"], ["HS"], "H3")
-    send([T.HS[:]], T.HR[:], nxt, "aH", "lH", ["HS"], ["HR"], "sendH", 64)
-    DMA(T.yp[:, 2048:4096], T.HR[:], ["HR"], ["oyp2"], "oyp2", 64, 512)
     splits(1)
-    DMA(T.yr[:, 512:1024], T.YR1[:], ["YR1a", "YR1b"], ["oyr1"], "oyr1", 128, 1024)
+    DMA(T.yr[:, 512:1024], T.YR1[:], ["YR1"], ["oyr1"], "oyr1", 128, 1024)
     DMA(T.yk0[:], T.KF[0:128:16, 0:3072], ["KF0", "KFt"], ["oyk0"], "oyk0", 96, 6144)
     DMA(T.yk1[:], T.KF[1:128:16, 0:3072], ["KF1", "KFt"], ["oyk1"], "oyk1", 96, 6144)
 

from concourse.bass import DstId, RemoteDMATransfer
from concourse.mybir import AluOpType as A, ActivationFunctionType as F

S = 256
MW = 2560
DUMP = 3072
BIG, EOFF = 8192.0, 1280
PARTS = ((0, 64), (64, 64))
GP = 2
RP = 1
ACC, RNP = 1, (0, 0)
ENDS = (((32, 32), (32, 32)), ((64,), (32, 32)))
LEAST = 32
BFB, FP, I4, U2, H2 = "bfloat16", "float32", "int32", "uint16", "float16"
SCRATCH = {}


def _decl(where, dtype, text):
    for w in text.split():
        nm, c = w.split(":")
        c = [int(x) for x in c.split("x")]
        SCRATCH[nm] = (where, c if len(c) > 1 else [128] + c, dtype)


_decl("sbuf", BFB, "XW:4096 PW:4096 RW:2560 EW:2048 LT:2048 PT1:2048 PT2:2048 LG:2048 CR:2048 CC:2048 XS0:2048 WZ:1008 PDb:512 OWb:512 ONB:128 ZB:320 "
      "IDB:128 NI8:128 RK:16 BLK:128 E4:128 SB:240 BW:2560 BK:320 LM:128 YR1:512 PT3:256 FBI:256 FE:256 FO:256 "
      "LF:256 JK:3072 AD:256 SP:256 MA:128 I15:128 I05:128 EH:16x256 DUT:16x128 CST:2x128")
_decl("sbuf", H2, "VL:2048 SS:2048 MM:2048 CN:2048 W16:288 RHS:24 ID16:128 NI16:128 NI4:128 PI4:128 RF:256 RS2:256 U:256 BASE:256 KDh:256 PERM:128 E0:128x17x8 E1:128x17x8")
_decl("sbuf", FP, "NW:3456 KF:3456 KDf:256 OWT:128 thF:8x2 THC:2 ONF:128 IDF:128 E8:8x128 COL:16 CT:32x16 EQ:16x128 EQ2:32x128 DW:16 NV0:256 NJ:512 "
      "NC:256 WD:128 XF:256 Q2:256 FW:80 SW:80 SFa:64 SFb:64 HR:128 HS:128 YP:128 TG:16 MB:128 BD:2 DM:16 I4B:256 BI:320 EQ8:16x128")
_decl("sbuf", I4, "stI:128 cuI:128 KD:256 PD:256 KT:320 DI:256 QI:1280 wI:1 wN:1 thI:8x1 FI:320 FB:320 D2:256 D3:256 RSI:256 WC:128 IT:256 FT:128 FU:128")
_decl("sbuf", U2, "LL:128x15x128")
_decl("psum", FP, " ".join("b%d:512" % _k for _k in range(8)))
SEMAPHORES = (["cv", "cs", "ct", "cg"] + ["d%d" % _k for _k in range(40)] + ["aw", "lw", "aH0", "lH0", "aH1", "lH1"]
              + ["%s%d" % (_a, _k) for _a in ("aA", "lA") for _k in range(8)])

CYC = 0.83e-3
BETA, TRIES, MOVES, SEED0, LAG, HEAT = 0.03, 100, 42000, 3, 0.0, 0.01
MODELS = ((1.15, 1.4, 0.2, 1.0, 1.0, 0.02, 1.0), (1.02, 1.08, 0.22, 1.6, 1.6, 0.06, 2.5), (1.35, 1.9, 0.18, 1.4, 1.2, 0.05, 1.5))
DLAT, RLAT, RBW, RFIRST, RCALL = 1.3, 2.3, 170.0, 2.0, 0.6
SELF, TCYC, FIX = 0.07, 0.71, 0.052
MEAN, PACK, PHEAT, MORE, AGAIN, REHEAT = 0.0, 500, 3.0, 0, 30000, 0.006
PLANS = {}


def make_plan(ops):
    n = len(ops)
    deps = [sorted(o["deps"]) for o in ops]
    succ, anc = [[] for _ in range(n)], [0] * n
    for i in range(n):
        for d in deps[i]:
            succ[d].append(i)
            anc[i] |= anc[d] | 1 << d
    QI = dict((q, k) for k, q in enumerate("vstgya"))
    kind = [o["alts"][0][0] for o in ops]
    rq = [[QI[a[0][0]] for a in o["alts"]] for o in ops]
    dur = [[[a[1] * (1.0 if a[0] in ("yd", "sd") else m[6] if a[0] == "gr" else m[0]) + a[2] * m[1] for a in o["alts"]] for o in ops] for m in MODELS]
    chan = [1 if k in ("yd", "sd") else 2 if k == "gr" else 0 for k in kind]
    lat = [o["lat"] for o in ops]
    pre = [[(DLAT - 0.3) * m[4] if c == 1 else 0.0 for c in chan] for m in MODELS]
    on = [[lat[i] * m[3] + ops[i]["rows"] * m[5] if chan[i] else 0.0 for i in range(n)] for m in MODELS]
    post = [[0.3 if chan[i] else lat[i] * m[4] if kind[i] == "arr" else m[2] for i in range(n)] for m in MODELS]
    norm = [m[0] * 30 + m[1] * 25 + 15 for m in MODELS]
    pri = [0.0] * n
    for i in range(n - 1, -1, -1):
        pri[i] = min(dur[0][i]) + pre[0][i] + on[0][i] + post[0][i] + max([pri[j] for j in succ[i]] or [0.0])

    def schedule(boost, pick):
        du, left, ready = dur[0], [len(d) for d in deps], [0.0] * n
        open_ = [i for i in range(n) if not left[i]]
        free, order, alt, ch = [0.0] * 6, [], [0] * n, [0.0, 0.0, RFIRST]
        p = [BETA * (pri[i] + boost[i]) for i in range(n)]
        while open_:
            bk = 1e9
            for i in open_:
                for j, q in enumerate(rq[i]):
                    if pick[i] < 0 or pick[i] == j:
                        st = max(free[q], ready[i])
                        if st - p[i] < bk:
                            bk, bi, bj, bs = st - p[i], i, j, st
            open_.remove(bi)
            e = bs + du[bi][bj]
            if rq[bi][bj] < 5:
                free[rq[bi][bj]] = e
            if chan[bi]:
                e = ch[chan[bi]] = max(ch[chan[bi]], e + pre[0][bi]) + on[0][bi]
            order.append(bi)
            alt[bi] = bj
            for s_ in succ[bi]:
                ready[s_] = max(ready[s_], e + (SELF if not chan[bi] and rq[s_] == [rq[bi][bj]] else post[0][bi]))
                left[s_] -= 1
                if not left[s_]:
                    open_.append(s_)
        return order, alt
    near = [[d for d in deps[i] if not any(anc[x] >> d & 1 for x in deps[i])] for i in range(n)]
    NM, GAP = len(MODELS), 16

    def length(order, alt, own, mi, old=None, at=0):
        du, pr, o_, po, gain = dur[mi], pre[mi], on[mi], post[mi], MODELS[mi][2] - SELF
        at //= GAP
        if old:
            fin, why, keep = old[1][:], old[2][:], old[3][:at + 1]
        else:
            fin, why, keep = [0.0] * n, [0] * n, [[0.0] * 9 + [RFIRST]]
        free = keep[at][:]
        for k in range(at * GAP, n, GAP):
            for i in order[k:k + GAP]:
                j = alt[i]
                q = rq[i][j]
                t = free[q]
                w = -1
                for x in near[i]:
                    f = fin[x]
                    if f > t:
                        if own[x] == q:
                            f -= gain
                            if f <= t:
                                continue
                        t = f
                        w = x
                t += du[i][j]
                if q < 5:
                    free[q] = t
                c = chan[i]
                if c:
                    t += pr[i]
                    if c == 2:
                        t += free[9]
                        free[9] = 0.0
                    if free[5 + c] > t:
                        t = free[5 + c]
                        w = -2
                    t += o_[i]
                    free[5 + c] = t
                t += po[i]
                fin[i] = t
                why[i] = w
            keep.append(free[:])
        return (max(fin) + MEAN * sum(fin) / n) / norm[mi], fin, why, keep

    def owners(alt):
        return [-1 if chan[i] else rq[i][alt[i]] for i in range(n)]

    def score(order, alt):
        return [length(order, alt, owners(alt), mi) for mi in range(NM)]

    def longest(order, alt, st):
        before, prev = [None] * n, [None] * 9
        for i in order:
            q = rq[i][alt[i]]
            before[i] = prev[q if st[2][i] == -1 else 6 + chan[i]]
            prev[q] = prev[6 + chan[i]] = i
        x, way = st[1].index(max(st[1])), []
        while x is not None:
            w = st[2][x]
            way.append((x, before[x] if w < 0 else None))
            x = before[x] if w < 0 else w
        return way
    seed = [SEED0]

    def rnd():
        seed[0] = (seed[0] * 1103515245 + 12345) % 2147483648
        return seed[0] / 2147483648.0
    boost, pick = [o["boost"] for o in ops], [o["pref"] for o in ops]
    two = [i for i in range(n) if len(rq[i]) == 2]
    order, alt = schedule(boost, pick)
    st = score(order, alt)
    best, way = sum(x[0] for x in st), longest(order, alt, st[0])
    for it in range(TRIES):
        b2, p2 = list(boost), list(pick)
        share, amp = 0.02 + 0.4 * rnd() ** 2, 1.0 + 12.0 * rnd()
        for i, before in way:
            if before is not None and rnd() < share:
                b2[i] += amp * rnd()
                b2[before] -= amp * rnd()
        for i in two:
            if rnd() < 0.02:
                p2[i] = int(3 * rnd()) - 1
        o2, a2 = schedule(b2, p2)
        s2 = score(o2, a2)
        if sum(x[0] for x in s2) <= best:
            best, order, alt, boost, pick, st = sum(x[0] for x in s2), o2, a2, b2, p2, s2
            way = longest(order, alt, st[int(rnd() * NM)])
    def packed(order, alt, own, mi):
        du, gain = dur[mi], MODELS[mi][2] - SELF
        lag = [pre[mi][i] + on[mi][i] + post[mi][i] for i in range(n)]
        link = [[], []]
        for c in (1, 2):
            line = [i for i in order if chan[i] == c]
            link[0] += list(zip(line[1:], line))
            link[1] += list(zip(line, line[1:]))
        for back in (1, 0):
            at, busy, seq = [0.0] * n, [[] for _ in range(6)], order[::-1] if back else order
            other = dict(link[back])
            for i in seq:
                q, d = rq[i][alt[i]], du[i][alt[i]]
                if back:
                    t = max([lag[i]] + [at[x] + du[x][alt[x]] + lag[i] - (gain if own[i] == rq[x][alt[x]] else 0.0) for x in succ[i]])
                    if i in other:
                        t = max(t, at[other[i]] + on[mi][i])
                else:
                    t = max([0.0] + [at[x] + du[x][alt[x]] + lag[x] - (gain if own[x] == q else 0.0) for x in near[i]])
                    if i in other:
                        t = max(t, at[other[i]] + on[mi][other[i]])
                if q < 5:
                    k, bq = 0, busy[q]
                    while k < len(bq) and bq[k][0] < t + d:
                        t = max(t, bq[k][1])
                        k += 1
                    bq.insert(k, (t, t + d))
                at[i] = t
            place = dict((x, k) for k, x in enumerate(order))
            order = sorted(order, key=lambda x: ((-at[x] - du[x][alt[x]]) if back else at[x], place[x]))
        return order
    now, keep, own = best, (order, alt), owners(alt)
    for it in range(MOVES + MORE):
        heat = HEAT * (1.0 - it / MOVES) if it < MOVES else REHEAT * (1.0 - (it - MOVES) % AGAIN / AGAIN)
        if it >= MOVES and (it - MOVES) % AGAIN == 0:
            now, (order, alt) = best, keep
            own, st = owners(alt), score(order, alt)
            way = longest(order, alt, st[0])
        if it % PACK == PACK - 1:
            o2 = packed(order, alt, own, it // PACK % NM)
            s2 = score(o2, alt)
            if sum(x[0] for x in s2) < now + heat * PHEAT:
                now, order, st = sum(x[0] for x in s2), o2, s2
                way = longest(order, alt, st[0])
                if now < best:
                    best, keep = now, (order, alt)
            continue
        r, o2, a2, w2 = rnd(), order, alt, own
        i, b = way[int(rnd() * len(way))]
        if r < 0.15:
            if len(rq[i]) < 2:
                i = two[int(rnd() * len(two))]
            a2, w2, pb = list(alt), list(own), order.index(i)
            a2[i] = 1 - alt[i]
            w2[i] = -1 if chan[i] else rq[i][a2[i]]
        else:
            if r < 0.3 or b is None:
                pi = int(rnd() * n)
                i = order[pi]
                pb = pi - 1
                skip = int(3 * rnd())
                while pb >= 0 and (rq[order[pb]][alt[order[pb]]] != rq[i][alt[i]] or skip):
                    skip -= rq[order[pb]][alt[order[pb]]] == rq[i][alt[i]]
                    pb -= 1
                if pb < 0:
                    continue
                b = order[pb]
            else:
                pi, pb = order.index(i), order.index(b)
            if anc[i] >> b & 1:
                continue
            mid = order[pb:pi + 1]
            if rnd() < 0.5:
                up = [x for x in mid if x == i or anc[i] >> x & 1]
                rest = [x for x in mid if not (x == i or anc[i] >> x & 1)]
            else:
                rest = [x for x in mid if x == b or anc[x] >> b & 1]
                up = [x for x in mid if not (x == b or anc[x] >> b & 1)]
            o2 = order[:pb] + up + rest + order[pi + 1:]
        room, s2 = heat * rnd() ** 3, []
        for mi in range(NM):
            s2.append(length(o2, a2, w2, mi, st[mi], pb))
            room -= s2[mi][0] - st[mi][0]
            if room < -0.004 * (NM - 1 - mi):
                break
        else:
            now, order, alt, own, st = sum(x[0] for x in s2), o2, a2, w2, s2
            way = longest(order, alt, st[int(rnd() * NM)])
            if now < best:
                best, keep = now, (order, alt)
    return [(i, keep[1][i]) for i in keep[0]], best


def rank_program(g, core, T, topo):
    rank = T.rank_of(core)
    if rank is None:
        return
    n_ranks = len(T.cores)
    nxt, prv = T.cores[(rank + 1) % n_ranks], T.cores[(rank - 1) % n_ranks]
    ops, last, readers, fore = [], {}, {}, [0.0]
    allp = range(len(PARTS))
    bP, bC, bQ, bS = ["b0", "b1"], ["b2", "b3"], ["b4", "b5"], ["b6", "b7"]

    def LI(k, a, n):
        return T.LL[:, k, a:a + n]

    def ZW(a, b):
        return T.PW[:, a:b]

    def QT(a, b, step=1):
        return T.PW[:, 2048 + a:2048 + b:step]

    def op(alts, R, W, nm="", lat=0.0, tok=None, boost=0.0, pref=-1, rows=0):
        i, deps = len(ops), set()
        for k in list(R) + list(W):
            if k in last:
                deps.add(last[k])
        for k in W:
            deps.update(readers.get(k, ()))
        for k in R:
            readers.setdefault(k, []).append(i)
        for k in W:
            last[k] = i
            readers[k] = []
        deps.discard(i)
        ops.append(dict(alts=alts, deps=deps, nm=nm, lat=lat, tok=tok, boost=boost + fore[0], pref=pref, rows=rows))

    def width(ap):
        n = 1
        for x in ap.shape[1:]:
            n *= x
        return n

    def vc(n, half=False):
        return FIX + max(64, n * (0.5 if half else 1)) * CYC

    def PE(fn, cyc, R, W, nm=""):
        op([("t", cyc * CYC * TCYC, 0.0, fn)], R, W, nm)
    nd = [0]

    def DMA(out, in_, R, W, nm, kb, row, boost=0.0):
        s = "d%d" % nd[0]
        nd[0] += 1
        op([(q, 0.06, 0.0, lambda e: e.dma_start(out, in_).then_inc(T.sem[s], 16)) for q in ("yd", "sd")[0:1 + (nm[0] == "o" or nm == "kid1")]], R, W, nm, lat=kb / 640.0, tok=(s, 16), rows=-(-(kb * 1024 // row) // 16),
           boost=boost - fore[0], pref=0)

    def ts(out, in0, s1, s2, o0, o1=None):
        if o1 is None:
            return lambda e: e.tensor_scalar(out, in0, s1, None, o0)
        return lambda e: e.tensor_scalar(out, in0, s1, s2, o0, o1)

    def vts(out, in0, s1, s2, o0, o1, R, W, nm="", half=False):
        op([("v", vc(width(out), half), 0.0, ts(out, in0, s1, s2, o0, o1))], R, W, nm)

    def vtt(out, i0, i1, o, R, W, nm="", two=True):
        op([("v", vc(width(out) * (2 if two else 1)), 0.0, lambda e: e.tensor_tensor(out, i0, i1, o))], R, W, nm)

    def lin(out, in_, scale, bias, R, W, nm="", half=False):
        n, f = width(in_), F.Copy if isinstance(bias, float) else F.Identity
        op([("s", vc(n), 0.0, lambda e: e.activation(out, in_, f, scale=scale, bias=bias)),
            ("v", vc(n, half), 0.0, ts(out, in_, scale, bias, A.mult, A.add))], R, W, nm)

    def cp(out, in_, R, W, nm="", half=False):
        n = width(in_)
        op([("s", vc(n), 0.0, lambda e: e.activation(out, in_, F.Copy)), ("v", vc(n, half), 0.0, lambda e: e.tensor_copy(out, in_))], R, W, nm)

    def gather(out, win, off, R, W, nm):
        d = out.shape[1] * CYC
        op([("s", 0.055, d, lambda e: e.activation(out, win.indirect(off), F.Copy)),
            ("v", 0.042, d, lambda e: e.tensor_copy(out, win.indirect(off)))], R, W, nm, pref=0)

    def gatherop(out, win, off, in1, o, R, W, nm):
        op([("v", 0.042, out.shape[1] * CYC, lambda e: e.tensor_tensor(out, win.indirect(off), in1, o))], R, W, nm)

    def ms(ap, c, W, half=True):
        op([("v", vc(width(ap), half), 0.0, lambda e: e.memset(ap, c))], [], W, "ms")

    def zero(out, W):
        n = out.shape[1]
        op([("s", vc(n), 0.0, lambda e: e.activation(out, T.ZB[:, 0:n], F.Copy)), ("v", vc(n, True), 0.0, lambda e: e.memset(out, 0.0))], ["ZB"], W, "zero")

    def cnt_(pat):
        n = 1
        for a_, b_ in pat:
            n *= b_
        return 2 * n * CYC

    def aff(out, in_, pat, cmpo, fill, base, cm, R, W):
        op([("g", 0.17 + cnt_(pat), 0.0, lambda e: e.affine_select(out, in_, pat, cmpo, fill, base, cm))], R, W, "aff")

    def iota(out, pat, base, cm, W, whole=False):
        k = {} if whole else dict(allow_small_or_imprecise_dtypes=True)
        op([("g", 0.13 + cnt_(pat), 0.0, lambda e: e.iota(out, pat, base, cm, **k))], [], W, "iota")

    def put(out, step, vals, R, W):
        n = out.shape[1]
        src, rd = T.ZB[:, 0:n], ["ZB"] + R
        for k, v in vals:
            aff(out, src, [[-step, n]], A.not_equal, float(v), -k, 1, rd, [W])
            src, rd = out, [W]

    B = 90.0
    DMA(T.KD[:, 0:128], T.kid0[:], [], ["KD0"], "kid0", 64, 512, B)
    DMA(T.KD[:, 128:256], T.kid1[:], [], ["KD1"], "kid1", 64, 512, B)
    DMA(ZW(0, 1024), T.z[:, 0:1024], [], ["ZW0"], "z0", 256, 2048, B - 1)
    DMA(ZW(1024, 2048), T.z[:, 1024:2048], [], ["ZW1"], "z1", 256, 2048, B - 2)
    DMA(T.stI[:], T.start[:], [], ["stI"], "start", 64, 512, B - 4)
    DMA(T.cuI[:], T.cur[:], [], ["cuI"], "cur", 64, 512, B - 5)
    DMA(T.XW[:], T.x[:], [], ["XW"], "x", 1024, 8192, B - 6)
    DMA(T.PD[:], T.prev[:], [], ["PD"], "prev", 128, 1024, B - 20)
    DMA(T.wI[:], T.w[:], [], ["wI"], "w", 1, 8, B - 40)
    DMA(T.thI[:], T.th[:], [], ["thI"], "th", 1, 64, B - 60)

    fore[0] = 80.0
    ms(T.ZB[:], 0.0, ["ZB"])
    ms(T.ONF[:], 1.0, ["ONF"], half=False)
    ms(T.ONB[:], 1.0, ["ONB"])
    aff(T.PERM[:], T.ONB[:], [[-1, 16], [-16, 8]], A.is_equal, 0.0, 0, 1, ["ONB"], ["PERM"])
    put(T.RK[:], 8, [(k, -8 ** (k + 1)) for k in range(4)], [], "RK")
    fore[0] = 60.0
    for k in range(4, 8):
        zero(QT(k, 2048, 8), ["QT%d_%d" % (c, k) for c in range(2)])
    iota(T.OWT[:], [[128, 16], [0, 8]], 0, 1, ["OWT"])
    aff(T.IDB[:], T.ONB[:], [[-1, 128]], A.is_equal, 0.0, 0, 1, ["ONB"], ["IDB"])
    put(T.NI8[:], 1, [(0, -0.125)], [], "NI8")
    fore[0] = 20.0
    ms(T.WZ[:], 0.0, ["WZ"])
    ZS = dict([(nm, (T.WZ, 144 * j)) for j, nm in enumerate(("one", "p0", "p2", "p4", "a97", "big", "wb"))]
              + [(nm, (T.W16, 144 * j)) for j, nm in enumerate(("w", "wn"))])

    def slot(nm):
        return ZS[nm][0][:, ZS[nm][1] + 15:ZS[nm][1] + 143:16]
    BC8 = slot("one")
    aff(BC8, T.ONB[:, 0:8], [[-16, 8]], A.is_ge, 0.0, 0, 1, ["ONB", "WZ"], ["Zone"])
    aff(BC8, BC8, [[16, 8]], A.is_ge, 0.0, 15, -1, ["Zone"], ["Zone"])
    put(slot("p0"), 16, ((0, 1), (1, 1)), ["WZ"], "Zp0")
    iota(T.OWb[:, 0:256], [[1, 256]], 0, 0, ["OWl"])
    iota(T.OWb[:, 256:512], [[0, 256]], 0, 256, ["OWh"])
    cp(T.RHS[:, 0:8], T.RK[:, 1:16:2], ["RK"], ["RHa"])
    cp(T.RHS[:, 8:16], T.RK[:, 0:16:2], ["RK"], ["RHb"])
    vtt(T.RHS[:, 16:24], T.RK[:, 1:16:2], T.RK[:, 0:16:2], A.subtract, ["RK"], ["RHc"])
    iota(T.CST[:, 0:64], [[0, 64]], 1536 * 4096, -1536 * 4096 - EOFF, ["CSa"])
    iota(T.CST[:, 64:128], [[0, 64]], 0, 0, ["CSb"])
    put(T.NI4[:], 1, [(0, -4096)], [], "NI4")
    put(T.PI4[:], 1, [(0, 4096)], [], "PI4")
    put(T.ID16[:], 1, [(0, 1)], [], "ID16")
    for p in allp:
        cp(T["E%d" % p][:], T.ZB[:, 0:136], ["ZB"], ["E%d" % p], "zero", True)
    fore[0] = 0.0
    aff(T.IDF[:], T.ONF[:], [[-1, 128]], A.is_equal, 0.0, 0, 1, ["ONF"], ["IDF"])
    aff(T.W16[:], T.ZB[:, 0:288], [[0, 288]], A.is_ge, 0.0, 0, 0, ["ZB"], ["W16"])
    put(slot("p2"), 16, ((2, 1), (3, 1)), ["WZ"], "Zp2")
    put(slot("p4"), 16, ((4, 1), (5, 1)), ["WZ"], "Zp4")
    put(slot("big"), 16, ((0, -BIG),), ["WZ"], "Zbig")
    lin(slot("a97"), BC8, 97.0, 0.0, ["Zone", "WZ"], ["Za97"], "cst")
    put(T.NI16[:], 1, [(0, -1)], [], "NI16")
    if max(RNP):
        put(T.I15[:], 1, [(0, 1536)], [], "I15")
        put(T.I05[:], 1, [(0, 1536 - 1040)], [], "I05")
    aff(T.BLK[:], T.ONB[:], [[-16, 8], [0, 16]], A.is_ge, 0.0, 0, 1, ["ONB"], ["BLK"])
    aff(T.BLK[:], T.BLK[:], [[16, 8], [0, 16]], A.is_ge, 0.0, 15, -1, ["BLK"], ["BLK"])
    aff(T.E4[:], T.ZB[:, 0:128], [[-16, 8], [0, 16]], A.not_equal, -BIG / 2, -4, 1, ["ZB"], ["E4"])
    if ACC:
        aff(T.EH[:], T.ZB[0:16, 0:256], [[-8, 2], [-1, 8], [0, 16]], A.not_equal, -BIG, 0, 1, ["ZB"], ["EH"])
    else:
        aff(T.SB[:], T.ZB[:, 0:240], [[1, 15], [0, 16]], A.not_equal, -65536 * BIG, -7, 0, ["ZB"], ["SB"])
    iota(T.I4B[:], [[4, 256]], 1028, 0, ["I4B"])
    iota(T.NJ[:], [[1, 512]], 0, 0, ["NJ"])
    iota(T.BI[:], [[1, 320]], 0, 320, ["BI"])
    aff(T.E8[:], T.ONF[0:8, :], [[-1, 8], [0, 16]], A.is_equal, 0.0, 0, 1, ["ONF"], ["E8"])
    iota(T.thF[:, 1:2], [[0, 1]], -4096, -4096, ["thG"])
    iota(T.DW[:], [[16, 16]], DUMP, 1, ["DW"])
    iota(T.NV0[:], [[2, 256]], 2048, 0, ["NV0"])
    iota(T.NC[:], [[2, 256]], 2048, 0, ["NC"])
    iota(T.BD[:], [[128, 2]], 1, 1, ["BD"])
    ms(T.WD[:], 0.0, ["WD"], half=False)
    for k in range(1, 4):
        for j in range(k):
            aff(T.WD[:, k:128:8], T.WD[:, k:128:8], [[-8, 16]], A.not_equal, float(8 ** (j + 4 - k)), -j, 1, ["WD"], ["WD"])
    fore[0] = -60.0
    iota(T.KF[:, 2048:3072], [[1, 1024]], 2048, 0, ["KFt"])
    fore[0] = 0.0

    TAB = {"sc": tuple((k, 2 ** (11 - k)) for k in range(12)), "e1": ((1, 1),), "e12": ((12, 1),),
           "ns": ((0, -0.125), (8, -0.125)), "nb": ((3, -0.5), (11, -0.5), (4, -320)),
           "s8": tuple((k + o, 8 ** (3 - k)) for o in (0, 8) for k in range(4)), "b8": tuple((k + 8, 8 ** (3 - k)) for k in range(4))}
    NT = len(TAB)
    CI = dict((nm, j) for j, nm in enumerate(list(TAB) + ["me", "mo", "w", "wn"]))

    def col(nm):
        return T.COL[:, CI[nm]:CI[nm] + 1]
    ms(T.CT[:], 0.0, ["CT" + nm for nm in CI], half=False)
    for nm in TAB:
        c, ck = T.CT[0:16, CI[nm]:CI[nm] + 1], ["CT" + nm]
        for k, v in TAB[nm]:
            aff(c, c, [[0, 1]], A.not_equal, float(v), -k, 1, ck, ck)
    for nm, o in (("me", 0), ("mo", 16)):
        c, ck = T.CT[:, CI[nm]:CI[nm] + 1], ["CT" + nm]
        aff(c, c, [[0, 1]], A.is_ge, 2.0 ** -20, -13 - o, 1, ck, ck)
        if o:
            aff(c, c, [[0, 1]], A.is_ge, 0.0, -o, 1, ck, ck)
        if ACC:
            aff(c, c, [[0, 1]], A.not_equal, -2.0 ** -20, -12 - o, 1, ck, ck)
    aff(T.EQ8[:], T.ONF[0:16, :], [[1, 16], [0, 8]], A.is_equal, 0.0, 0, -1, ["ONF"], ["EQ8"])
    aff(T.EQ[:], T.ONF[0:16, :], [[0, 8], [1, 16]], A.is_equal, 0.0, 0, -1, ["ONF"], ["EQ"])
    aff(T.EQ2[:], T.ONF[0:32, :], [[0, 4], [1, 32]], A.is_equal, 0.0, 0, -1, ["ONF"], ["EQ2"])

    fore[0] = 30.0
    cp(T.KDh[:], T.KD[:], ["KD0", "KD1"], ["KDh"])
    bk = T[bS[0]]
    PE(lambda e: [e.matmul(bk[:, j:256:2], T.KDh[:, 128 * j:128 * j + 128], T.PERM[:], True, True) for j in range(2)], 256, ["KDh", "PERM"], [bS[0]], "kT")
    cp(T.KT[:, 0:256], bk[:, 0:256], [], ["KT0", "KT1", bS[0]], "KT")
    vtt(T.LM[:], bk[:, 0:256:2], T.OWT[:], A.is_equal, ["OWT"], ["LM", bS[0]], "LM", two=False)
    lin(QT(4, 2048, 16), T.LM[:], 2560.0, 0.0, ["LM"], ["QT0_4", "QT1_4"], "LM", True)

    def digits(c, a, n, src, sk, ks):
        for k in ks:
            qi = T.QI[:, 320 * k + a:320 * k + a + n]
            vts(qi, src[:, a:a + n], 3 * k, 7, A.arith_shift_right, A.bitwise_and, sk, ["QI%d_%d" % (x, k) for x in c], "dig")
            cp(QT(8 * a + k, 8 * (a + n), 8), qi, ["QI%d_%d" % (x, k) for x in c], ["QT%d_%d" % (x, k) for x in c], "dig")
    digits((0, 1), 0, 256, T.KT, ["KT0", "KT1"], (0,))
    NWK, nb = ["NW%d" % j for j in range(4)], bP + bC
    for j in range(4):
        PE(lambda e, j=j: e.matmul(T[nb[j]][:, 0:512], T.IDB[:], ZW(512 * j, 512 * j + 512), True, False), 512, ["IDB", "ZW%d" % (j // 2)], [nb[j]], "nz")
    for c in range(2):
        bz = (bS[1], bQ[1])[c]
        PE(lambda e, c=c, bz=bz: [e.matmul(T[bz][:, 16 * b:16 * b + 16], ZW(1024 * c + 128 * b, 1024 * c + 128 * b + 128), T.RK[:], True, True) for b in range(8)],
           512, ["ZW%d" % c, "RK"], [bz], "zD")
        vtt(T.DI[:, 128 * c:128 * c + 128], T.KT[:, 128 * c:128 * c + 128], T[bz][:, 0:128], A.subtract, ["KT%d" % c], ["DI%d" % c, bz], "DI", two=False)
        digits((c,), 128 * c, 128, T.DI, ["DI%d" % c], (1, 2, 3))
        for j in (2 * c, 2 * c + 1):
            PE(lambda e, j=j: [e.matmul(T[nb[j]][:, 128 * i:128 * i + 128], QT(512 * j + 128 * i, 512 * j + 128 * i + 128), T.NI8[:], False, i == 3)
                               for i in range(4)], 512, ["NI8"] + ["QT%d_%d" % (c, k) for k in range(8)], [nb[j]], "nq")
            cp(T.NW[:, 512 * j:512 * j + 512], T[nb[j]][:, 0:512], [], ["NW%d" % j, nb[j]], "nw")
    fore[0] = 0.0

    cp(LI(0, 0, 128), T.stI[:], ["stI"], ["L0_%d" % p for p in allp])
    cp(LI(5, 0, 128), T.cuI[:], ["cuI"], ["L5_%d" % p for p in allp])
    cp(T.PDb[:, 0:256], T.PD[:], ["PD"], ["PDh"])
    vtt(T.PDb[:, 256:512], T.PD[:], T.PDb[:, 0:256], A.subtract, ["PD", "PDh"], ["PDl"])
    op([("arr", 0.0, 0.0, None)], [], ["ZW0", "ZW1", "PWf"] + ["QT%d_%d" % (c, k) for c in range(2) for k in range(8)], "free")
    DMA(T.PW[0:128:16, 0:4096], T.PDb[:, 0:256], ["PDh", "PWf"], ["PW0"], "pw0", 64, 512)
    DMA(T.PW[1:128:16, 0:4096], T.PDb[:, 256:512], ["PDl", "PWf"], ["PW1"], "pw1", 64, 512)
    DMA(T.PW[4:128:16, 0:4096], T.OWb[:, 0:256], ["OWl", "PWf"], ["PW4"], "pw4", 64, 512)
    DMA(T.PW[5:128:16, 0:4096], T.OWb[:, 256:512], ["OWh", "PWf"], ["PW5"], "pw5", 64, 512)
    PWK, PWIN = ["PW0", "PW1", "PW4", "PW5"], T.PW[:, 0:4096]
    DMA(T.RW[:, 0:2048], T.rs[:], ["PWf"], ["RW"], "rs", 512, 4096, -200.0)
    DMA(T.EW[:], T.env[:], ["PWf"], ["EW"], "env", 512, 4096, -210.0)
    cp(col("w"), T.wI[:], ["wI"], ["w"])
    lin(slot("w"), BC8, col("w"), 0.0, ["W16", "Zone", "w"], ["Zw"], "Zw")
    lin(slot("wb"), BC8, col("w"), 0.0, ["WZ", "Zone", "w"], ["Zwb"], "Zw")

    bc = T[bS[1]]
    PE(lambda e: [e.matmul(bc[:, 0:1], T.EQ8[:], T.CT[0:16, 0:1], True, True), e.matmul(bc[:, 1:NT], T.EQ[:], T.CT[0:16, 1:NT], True, True),
                  e.matmul(bc[:, NT:NT + 2], T.EQ2[:], T.CT[:, NT:NT + 2], True, True)], 768, ["EQ", "EQ2", "EQ8"] + ["CT" + nm for nm in CI], [bS[1]], "cols")
    cp(T.COL[:, 0:NT + 2], bc[:, 0:NT + 2], [], list(TAB) + ["me", "mo", bS[1]], "cols")
    lin(T.FI[:], T.BI[:], col("sc"), 0.0, ["BI", "sc"], ["FI"], "fi")
    vts(T.FB[:], T.FI[:], 2048, None, A.bitwise_and, None, ["FI"], ["FB"], "fb")
    lin(T.BK[:], T.FB[:], 1.0, -1024.0, ["FB"], ["BK"], "bk")
    for gr in range(8):
        DMA(T.BW[16 * gr:16 * gr + 16, :], T.BK[:], ["BK"], ["BW%d" % gr], "bw", 80, 640, -100.0)
    vtt(T.BD[:], T.BD[:], T.BD[:], A.mult, [], ["BD"], "bd")
    lin(T.BD[:], T.BD[:], (1.0 if ACC else -1.0) / 65536, -12.0, [], ["BD"], "bd")
    lin(T.BASE[:], T.I4B[:], col("e12"), 0.0, ["I4B", "e12"], ["BASE"], "base")
    lin(T.NV0[:], T.NV0[:], 1.0, col("e1"), ["e1"], ["NV0"], "cst")
    lin(T.NW[:, 2048:MW], T.NJ[:], col("ns"), col("nb"), ["NJ", "ns", "nb"], ["NT"], "nt")
    lin(T.NC[:], T.NC[:], col("s8"), col("b8"), ["s8", "b8"], ["NC"], "cst")
    cp(T.thF[:, 0:1], T.thI[:], ["thI"], ["thF"])
    PE(lambda e: e.matmul(bc[:, 0:2], T.E8[:], T.thF[:], True, True), 256, ["E8", "thF", "thG"], [bS[1]], "th")
    lin(T.THC[:], bc[:, 0:2], 1.0, BIG / 2, [], ["THC", bS[1]])
    GOFF = T.THC[:, 1:2]

    def wrap(bank, o, z, src, c0, C, R, nm, first=True, end=True, more=()):
        wz, z0 = ZS[z]
        PE(lambda e: [f(e) for f in more] + [e.matmul(T[bank][:, o:o + C], wz[:, z0 + 15 - q:z0 + 143 - q], src[:, 16 * c0 + q:16 * (c0 + C):16],
                                                      first and q == 0, end and q == 15) for q in range(16)],
           1024 + 256 * len(more), ["Z" + z] + R, [bank], nm)

    def rows(bank, z, src, l0, n, m0, m1, first, end, R, nm):
        wz, z0 = ZS[z]
        PE(lambda e: [e.matmul(T[bank][:, 0:n], wz[:, z0 + 15 - m:z0 + 143 - m], src[:, l0 + n * m:l0 + n * m + n], first and m == m0, end and m == m1 - 1)
                      for m in range(m0, m1)], max(64, n) * (m1 - m0), R + ["Z" + z], [bank], nm)

    def sums(e, bank, x, w, c0, C, alone):
        return [e.matmul(T[bank][0:2 * C, r:8 * w.shape[1]:8], x[:, 16 * c0 + r:16 * (c0 + C):8], w, alone, alone) for r in range(8)]

    def lanes(X, c0, C):
        return X[:, 16 * c0:16 * (c0 + C)]

    def cut(c0, C, n):
        at = [c0 + 8 * (C // 8 * j // n) for j in range(n)] + [c0 + C]
        return [("_%d" % j, at[j], at[j + 1] - at[j]) for j in range(n)]
    came = []

    def vl(a, n):
        return [nm for nm, c0, C in came if c0 < a + n and a < c0 + C]

    def step(t, k, p):
        c0, C = PARTS[p]
        ps, win, nr = str(p), (MW if t else 2048), 2 * C
        tp, tc, nk = T[bP[p]], T[bC[p]], NWK + (["NT"] if t else [])
        lk, pcs = ["L%d_%d" % (k, p)], cut(c0, C, GP)
        for nm, a, n in pcs:
            nt, ct, nm = lanes(T.CN, a, n), lanes(T.CC, a, n), ps + nm
            gather(nt, T.NW[:, 0:win], LI(k, a, n), lk + nk, ["CN" + nm], "node")
            if t and k == 1:
                gatherop(ct, T.XS0[:], LI(9, a, n), nt, A.is_ge, ["XS%d" % x for x in allp] + ["L9_%d" % p, "CN" + nm], ["CC" + nm], "cmp")
            elif k or not t:
                sl = (11 if t else 5) + k
                gatherop(ct, T.XW[:], LI(sl, a, n), nt, A.is_ge, ["XW", "L%d_%d" % (sl, p), "CN" + nm], ["CC" + nm], "cmp")
            else:
                gatherop(ct, T.NW[:, 0:win], LI(k, a, n), lanes(T.VL, a, n), A.is_le, lk + nk + vl(a, n), ["CC" + nm], "cmp")
        cn = ["CN" + ps + x[0] for x in pcs] + ["RHa", "RHb", "RHc"]
        PE(lambda e: sums(e, bC[p], T.CN, T.RHS[:, 0:16], c0, C, True), 512, cn, [bC[p]], "kid")
        PE(lambda e: [e.matmul(tp[0:nr, 0:128], T.ONB[0:2, 0:nr], T.CST[:], True, False)] + sums(e, bP[p], T.CN, T.RHS[:, 8:24], c0, C, False),
           640, ["ONB", "CSa", "CSb"] + cn, [bP[p]], "kid")
        lin(T.U[0:nr, 128 * p:128 * p + 128], tc[0:nr, 0:128], 1.0 / 4096, 1536 - EOFF / 4096.0, [], ["U" + ps, bC[p]], "u")
        PE(lambda e: [e.matmul(tp[0:nr, o:o + 64], w[0:nr, 0:nr], T.U[0:nr, 128 * p + a:128 * p + a + 64], False, w is T.PI4)
                      for o, w, a in ((0, T.NI4, 64), (64, T.NI4, 0), (64, T.PI4, 64))], 192, ["NI4", "PI4", "U" + ps], [bP[p]], "fix")
        PE(lambda e: sums(e, bC[p], T.CC, BC8, c0, C, True), 512, ["Zone"] + ["CC" + ps + x[0] for x in pcs], [bC[p]], "count")
        ma, mb_ = T.MA[0:nr, 64 * p:64 * p + 64], T.MB[0:nr, 64 * p:64 * p + 64]
        vts(ma, tc[0:nr, 0:64], 8.5, None, A.is_ge, None, [], ["MA" + ps, bC[p]], "m")
        vtt(mb_, ma, tp[0:nr, 64:128], A.mult, ["MA" + ps], ["MB" + ps, bP[p]], "t", two=False)
        vtt(T["E" + ps][0:nr, 1:17:2, :], mb_, tp[0:nr, 0:64], A.add, ["MB" + ps], ["E" + ps, bP[p]], "f", two=False)
        PE(lambda e: [e.matmul(tc[:, 64:64 + C], T["E" + ps][0:nr, 1 - h:17 - h, :], T.ID16[0:nr, h:nr:2], h == 0, h == 1) for h in range(2)],
           128, ["ID16", "E" + ps], [bC[p]], "turn")
        lin(LI(k + 1, c0, C), tc[:, 64:64 + C], 1.0, float(EOFF), [], ["L%d_%d" % (k + 1, p), bC[p]], "list")

    def low(p, num, nk, out, W):
        c0, C = PARTS[p]
        fu = T.FU[:, c0:c0 + C]
        vts(fu, num, 2047, None, A.bitwise_and, None, [nk], ["FU%d" % p], "and")
        cp(out, fu, ["FU%d" % p], W, "list")

    def outcome(t, p, after):
        win, X, (c0, C) = (MW if t else 2048), (T.VL if t else T.XS0), PARTS[p]
        nm, again, rk = str(t) + str(p), ["o%d" % p] if t else [], []
        for n2, a, n in cut(c0, C, RP):
            gatherop(lanes(T.CR, a, n), T.RW[:, 0:win], LI(4, a, n), lanes(X, a, n), A.is_gt,
                     ["L4_%d" % p, "RW"] + (vl(a, n) + ["RT"] if t else ["XS%d" % p]) + again, ["CR" + nm + n2], "R")
            rk.append("CR" + nm + n2)
        i1, acc = T.FT[:, c0:c0 + C], T[bP[p]][:, 0:C]
        if t:
            wrap(bP[p], 0, "a97", T.CR, c0, C, rk, "a")
            vtt(i1, T.WC[:, c0:c0 + C], acc, A.add, ["WC%d" % p], ["FT%d" % p, bP[p]], "i1", two=False)
        else:
            wrap(bP[p], 0, "wb", T.XS0, c0, C, ["XS%d" % p], "wc", end=False)
            wrap(bP[p], 0, "a97", T.CR, c0, C, rk, "a", first=False)
            cp(i1, acc, [], ["FT%d" % p, bP[p]], "i1")
        low(p, i1, "FT%d" % p, LI(10, c0, C), ["IX" + nm])
        for j, n in enumerate(ENDS[t][p]):
            n2, a = nm + "_%d" % j, c0 + sum(ENDS[t][p][:j])
            gatherop(lanes(T.SS, a, n), T.EW[:], LI(10, a, n), lanes(X, a, n), A.add, ["IX" + nm, "EW"] + (vl(a, n) if t else ["XS%d" % p]) + again, ["SS" + n2], "env")
            vts(lanes(T.MM, a, n), lanes(T.SS, a, n), 256.0, -256.0, A.is_ge, A.mult, ["SS" + n2], ["MM" + n2], "mm", half=True)
            after(n2, a, n)

    def send(srcs, out, dst, rs, ls, R, W, nm, kb):
        rid, pid = topo.addr(dst)[0], topo.addr(dst)[1]
        k = dict(dst_ids=[DstId(rid=rid, pnc=pid)], dma_engine_mask=topo.mask(core, dst), remote_sem=T.sem[rs])
        tr = RemoteDMATransfer(srcs=srcs, dsts=[out], alu_op=1, **k) if len(srcs) > 1 else RemoteDMATransfer(src=srcs[0], dst=out, **k)
        op([("gr", RCALL, 0.0, lambda e: e.remote_dma_fused([tr], local_sem=T.sem[ls]))], R, [nm], nm, lat=kb / RBW, rows=16, tok=(ls, len(topo.engines(core, dst))))
        op([("arr", 0.0, 0.0, None)], [nm], W, nm + "arr", lat=RLAT - 0.3, tok=(rs, len(topo.engines(prv if dst == nxt else nxt, core))))

    def splits(t):
        win, off, nk = (MW if t else 2048), LI(4, 0, 16), NWK + (["NT"] if t else [])
        vk, far = ["SS%d0_0" % t, "MM%d0_0" % t], T[bC[0]]
        bwk = ["L4_0"] + ["BW%d" % gr for gr in range(8)]
        gatherop(T.FBI[:], T.BW[:], off, T.BASE[:], A.add, bwk + ["BASE"], ["FBI"], "fbi")
        for fx, c in (("FE", "me"), ("FO", "mo")):
            lin(T[fx][:], T.FBI[:], col(c), 0.0, ["FBI", c], [fx], "fx", True)
        op([("s", 0.055, S * CYC, lambda e: e.activation(T.LF[:], T.NW[:, 0:win].indirect(off), F.Sign, bias=1.5))], ["L4_0"] + nk, ["LF"], "lf")
        gather(T.RF[:], T.RW[:, 0:win], off, ["L4_0", "RW"] + (["RT"] if t else []), ["RF"], "rf")
        PE(lambda e: e.matmul(far[:, 0:S], T.E4[:], T.LF[:], True, False), S, ["E4", "LF"], [bC[0]], "leaf")
        for gr in range(8 if ACC else 0):
            bn, fx, p0 = (bS + bQ)[gr % 3], (T.FE, T.FO)[gr % 2], 32 * (gr // 2)
            PE(lambda e, bn=bn, fx=fx, p0=p0: [e.matmul(T[bn][:, 128 * hf:128 + S * hf], fx[p0:p0 + 32, 128 * hf:128 * hf + 128], T.FBI[p0:p0 + 32, 0:128 + 128 * hf], True, True)
                                               for hf in range(2)], 384, ["FE", "FO", "FBI"], [bn], "dot")
            op([("s", vc(128) + vc(S) + 0.04, 0.0,
                 lambda e, bn=bn, gr=gr: [e.activation(T.JK[:, 384 * gr + 128 * hf:384 * gr + 128 + S * hf], T[bn][:, 128 * hf:128 + S * hf], F.Relu, bias=T.BD[:, hf:hf + 1],
                                                       accum_out=T.DM[:, 8 * hf + gr:8 * hf + gr + 1]) for hf in range(2)])], ["BD"], ["DM%d" % gr, bn], "red")
        if ACC:
            bd = T[bS[1]]
            PE(lambda e: e.matmul(bd[0:16, 0:128], T.DM[:], T.IDF[:], True, True), 512, ["IDF"] + ["DM%d" % gr for gr in range(8)], [bS[1]], "dupT")
            op([("s", vc(128), 0.0, lambda e: e.activation(T.DUT[:], bd[0:16, 0:128], F.Sign)),
                ("v", vc(128), 0.0, ts(T.DUT[:], bd[0:16, 0:128], 0.0, None, A.is_gt))], [], ["DUT", bS[1]], "dut")
            PE(lambda e: [e.matmul(far[:, 128 * hf:128 * hf + 128], T.EH[:, 128 * hf:128 * hf + 128], T.DUT[:], False, False) for hf in range(2)],
               S, ["EH", "DUT"], [bC[0]], "dup")
        for m, (hf, gs) in enumerate([] if ACC else [(0, (2 * m, 2 * m + 1)) for m in range(4)] + [(1, range(4 * m, 4 * m + 4)) for m in range(2)]):
            bn, lo, jk = (bS + bQ)[m % 3], 128 * hf, T.JK[:, 512 * m:512 * m + 512]
            n = S - lo
            for j in range(0, len(gs), 2):
                PE(lambda e, bn=bn, lo=lo, j=j, n=n, p0=16 * gs[j]: [e.matmul(T[bn][:, n * (j + a):n * (j + a + 1)], fx[p0:p0 + 32, lo:lo + 128],
                                                                              T.FBI[p0:p0 + 32, lo:S], True, True) for a, fx in enumerate((T.FE, T.FO))],
                   2 * n, ["FE", "FO", "FBI"], [bn], "dot")
            op([("s", vc(512), 0.0, lambda e, bn=bn, hf=hf, jk=jk: e.activation(jk, T[bn][:], F.Relu, bias=T.BD[:, hf:hf + 1])),
                ("v", vc(512), 0.0, ts(jk, T[bn][:], T.BD[:, hf:hf + 1], 0.0, A.add, A.max))], ["BD"], ["JK%d" % m, bn], "red", pref=0)
            PE(lambda e, m=m, lo=lo, gs=gs, n=n: [e.matmul(far[:, lo:S], T.SB[:, 112 - 16 * gr:240 - 16 * gr], T.JK[:, 512 * m + n * j:512 * m + n * j + n], False, False)
                                                  for j, gr in enumerate(gs)], 512, ["SB", "JK%d" % m], [bC[0]], "dup")
        bv = T[bP[0]]
        PE(lambda e: [e.matmul(bv[:, 0:S], w[:], x[:, 0:S], x is T.RF, x is T.MM) for w, x in ((T.ID16, T.RF), (T.NI16, T.SS), (T.NI16, T.MM))],
           3 * S, ["ID16", "NI16", "RF"] + vk, [bP[0]], "vv")
        op([("s", vc(S), 0.0, lambda e: e.activation(T.AD[:], bv[:, 0:S], F.Abs))], [], ["AD", bP[0]], "abs")
        PE(lambda e: [e.matmul(T[bS[0]][:, 0:S], T.ID16[:], x[:, 0:S], x is T.RF, x is T.MM) for x in (T.RF, T.SS, T.MM)], 3 * S, ["ID16", "RF"] + vk, [bS[0]], "vv")
        lin((T.RS2 if RNP[t] else T.RSI)[:], T[bS[0]][:, 0:S], 0.5, 1039.75 if RNP[t] else -0.25, [], ["RS2", bS[0]], "rs2")
        PE(lambda e: e.matmul(far[:, 0:S], T.BLK[:], T.AD[:], False, True), S, ["BLK", "AD"], [bC[0]], "far")
        vts(T.SP[:], far[:, 0:S], T.THC[:, 0:1], None, A.is_ge, None, ["THC"], ["SP", bC[0]], "sp")
        RN, rn, c0 = (T.YR1, "YR1", 0) if t else (T.RW, "RT", 2048)
        b0 = T[bS[0]]
        if RNP[t]:
            PE(lambda e: [e.matmul(b0[:, 0:512:2], T.ID16[:], T.RF[:], True, False), e.matmul(b0[:, 0:512:2], T.I15[:], T.SP[:], False, True),
                          e.matmul(b0[:, 1:512:2], T.ID16[:], T.RS2[:], True, False), e.matmul(b0[:, 1:512:2], T.I05[:], T.SP[:], False, True)],
               4 * S, ["ID16", "I15", "I05", "RF", "RS2", "SP"], [bS[0]], "rn")
            op([("s", vc(512), 0.0, lambda e: e.activation(RN[:, c0:c0 + 512], b0[:], F.Relu, bias=-1536.0)),
                ("v", vc(512), 0.0, ts(RN[:, c0:c0 + 512], b0[:], -1536.0, 0.0, A.add, A.max))], [], [rn, bS[0]], "rn")
        else:
            vtt(RN[:, c0:c0 + 512:2], T.RF[:], T.SP[:], A.mult, ["RF", "SP"], [rn + "a"], "rna")
            vtt(RN[:, c0 + 1:c0 + 512:2], T.RSI[:], T.SP[:], A.mult, ["RS2", "SP"], [rn + "b"], "rnb")
            op([("arr", 0.0, 0.0, None)], [rn + "a", rn + "b"], [rn], "free")
        s2 = bS[1]
        PE(lambda e: e.matmul(T[s2][:, 0:16], T.IDF[:], T.DW[:], True, False), 256, ["IDF", "DW"], [s2], "dump")
        wrap(s2, 0, "big", T.SP, 0, 16, ["SP"], "wsp", False, True)
        if t:
            cp(T.FW[:, 64:80], off, ["L4_0"], ["FW"])
        vtt(T.TG[:, 0:16], T.FW[:, 64:80], T[s2][:, 0:16], A.max, ["FW"], ["TG1", s2], two=False)
        tg = LI(11, 0, 16)
        cp(tg, T.TG[:, 0:16], ["TG1"], ["TGL"])
        if not t:
            op([("v", 0.042, 2.3 * S * CYC, lambda e: e.tensor_tensor(T.NW[:].indirect(tg), T.XF[:], T.Q2[:], A.add))], ["TGL", "XF", "Q2"], NWK + ["NT"], "scN")
        op([("v", 0.042, 2.3 * S * CYC, ts(T.KF[:].indirect(tg), T.NV0[:], 1.0, 512.0 * t, A.mult, A.add))], ["TGL", "NV0"], ["KF0", "KF1", "KFt"], "scF")

    nq = [0]

    def chain(src, c0, C, z, out, W, R):
        bq = bQ[nq[0] % 2]
        nq[0] += 1
        wrap(bq, 0, z, src, c0, C, R, "ws")
        cp(out, T[bq][:, 0:C], [], W + [bq], "slist")

    for p, (c0, C) in enumerate(PARTS):
        fore[0] = -LAG * p
        gather(lanes(T.XS0, c0, C), T.XW[:], LI(5, c0, C), ["XW", "L5_%d" % p], ["XS%d" % p], "xs")
    for k, pt in enumerate(("LT", "PT1", "PT2")):
        for p, (c0, C) in enumerate(PARTS):
            fore[0] = -LAG * p
            gather(lanes(T[pt], c0, C), PWIN, LI(5 + k, c0, C), PWK + ["L%d_%d" % (5 + k, p)], [pt + str(p)], "pv")
            chain(T[pt], c0, C, "p0", LI(6 + k, c0, C), ["L%d_%d" % (6 + k, p)], [pt + str(p)])
    fore[0] = 0.0
    LTK = ["LT%d" % p for p in allp]
    for j in range(2):
        DMA(T.LT[2 + j:128:16, :], T.PT1[j:128:16, :], ["PT1%d" % p for p in allp] + ["L6_%d" % p for p in allp], ["LTr%d" % j], "lt", 32, 2048)
    for k in range(4):
        for p in allp:
            fore[0] = -LAG * p
            step(0, k, p)
    fore[0] = 0.0
    gather(T.PT3[:], PWIN, LI(8, 0, 16), PWK + ["L8_0"], ["PT3"], "p4")
    chain(T.PT3, 0, 16, "p0", T.SW[:, 64:80], ["SW4"], ["PT3"])
    cp(T.FW[:], T.LL[:, 0:5, 0:16], ["L%d_0" % k for k in range(5)], ["FW"])
    cp(T.SW[:, 0:64], T.LL[:, 5:9, 0:16], ["L%d_0" % k for k in range(5, 9)], ["SW"])
    vtt(T.SFb[:], T.SW[:, 16:80], T.SW[:, 0:64], A.subtract, ["SW", "SW4"], ["SFb"])
    vtt(T.SFa[:], T.FW[:, 16:80], T.FW[:, 0:64], A.not_equal, ["FW"], ["SFa"])
    vtt(T.SFa[:], T.SFa[:], T.SFb[:], A.mult, ["SFa", "SFb"], ["SFa"])
    vtt(T.SFb[:, 0:32], T.SFa[:, 0:32], T.SFa[:, 32:64], A.add, ["SFa"], ["SFb"])
    vtt(T.SFa[:, 0:16], T.SFb[:, 0:16], T.SFb[:, 16:32], A.add, ["SFb"], ["SFa"])
    vtt(T.SFb[:, 32:48], T.SFa[:, 0:16], T.SW[:, 0:16], A.add, ["SFa", "SW"], ["SFb"])
    cp(LI(11, 32, 16), T.SFb[:, 32:48], ["SFb"], ["SFL"])
    gather(T.XF[:], T.XW[:], LI(11, 32, 16), ["XW", "SFL"], ["XF"], "xf")
    bq = bQ[0]
    PE(lambda e: e.matmul(T[bq][:, 0:S], T.WD[:], T.XF[:], True, True), 4 * S, ["WD", "XF"], [bq], "xD")
    vtt(T.D2[:], T.NC[:], T[bq][:, 0:S], A.add, ["NC"], ["D2", bq], "d2", two=False)
    vts(T.D3[:], T.D2[:], 7 * 512, None, A.bitwise_and, None, ["D2"], ["D3"], "d3")
    lin(T.Q2[:], T.D3[:], -1.0 / 4096, 0.0, ["D3"], ["Q2"], "q2")

    ns, sent, held = [0], [[] for p in allp], []
    for p in allp:
        fore[0] = -LAG * p

        def hand(nm, c0, C, p=p):
            held.append((nm, C))
            C = sum(x[1] for x in held)
            if C < LEAST:
                return
            c0 -= C - held[-1][1]
            send([lanes(T.SS, c0, C), lanes(T.MM, c0, C)], lanes(T.VL, c0, C), nxt, "aA%d" % ns[0], "lA%d" % ns[0],
                 [x + y[0] for x in ("SS", "MM") for y in held], ["VL" + nm], "send" + nm, 4 * C)
            del held[:]
            ns[0] += 1
            came.append(("VL" + nm, c0, C))
            sent[p].append("send" + nm)
        outcome(0, p, hand)
    fore[0] = 0.0
    cp(T.KDf[:], T.KD[:], ["KD0", "KD1"], ["KDf"])
    DMA(T.KF[0:128:16, 0:2048], T.KDf[:, 0:128], ["KDf", "PWf"], ["KF0"], "kf0", 64, 512, -300.0)
    DMA(T.KF[1:128:16, 0:2048], T.KDf[:, 128:256], ["KDf", "PWf"], ["KF1"], "kf1", 64, 512, -300.0)
    splits(0)
    DMA(T.yr[:, 0:512], T.RW[:, 2048:MW], ["RT"], ["oyr0"], "oyr0", 128, 1024)
    send([T.wI[:]], T.wN[:], prv, "aw", "lw", ["wI"], ["wN"], "sendw", 1)
    cp(col("wn"), T.wN[:], ["wN"], ["wn"])
    lin(slot("wn"), BC8, col("wn"), 0.0, ["W16", "Zone", "wn"], ["Zwn"], "Zn")

    for p, (c0, C) in enumerate(PARTS):
        fore[0] = -LAG * p
        wrap(bP[p], 0, "w", T.VL, c0, C, vl(c0, C), "wc")
        cp(T.WC[:, c0:c0 + C], T[bP[p]][:, 0:C], [], ["WC%d" % p, bP[p]], "wc")
        low(p, T.WC[:, c0:c0 + C], "WC%d" % p, LI(9, c0, C), ["L9_%d" % p])
        gather(lanes(T.LG, c0, C), T.LT[:], LI(9, c0, C), LTK + ["LTr0", "LTr1", "L9_%d" % p], ["LG%d" % p], "lg")
        for k, z in ((13, "p0"), (14, "p2")):
            chain(T.LG, c0, C, z, LI(k, c0, C), ["L%d_%d" % (k, p)], ["LG%d" % p])
    fore[0] = -30.0
    rows(bQ[0], "p4", T.LG, 0, 128, 0, 16, True, True, ["LG%d" % p for p in allp], "cur")
    lin(T.YP[:], T[bQ[0]][:, 0:128], 1.0, GOFF, ["THC"], ["YP", bQ[0]], "yp")
    DMA(T.yp[:, 0:2048], T.YP[:], ["YP"], ["oyp0"], "oyp", 64, 512)
    for k in range(4):
        for p in allp:
            fore[0] = -LAG * p
            step(1, k, p)
    for p in allp:
        fore[0] = -LAG * p

        a0, n0 = PARTS[p]
        hb = bC[p] if p else bQ[1]

        def handsum(nm, c0, C, a0=a0, n0=n0, hb=hb):
            m0, m1 = 16 * (c0 - a0) // n0, 16 * (c0 + C - a0) // n0
            rows(hb, "wn", T.SS, 16 * a0, n0, m0, m1, m0 == 0, False, ["SS" + nm], "hs")
            rows(hb, "wn", T.MM, 16 * a0, n0, m0, m1, False, m1 == 16, ["MM" + nm], "hm")
        op([("arr", 0.0, 0.0, None)], sent[p] + (["RS2", "AD"] if p == 0 else []), ["o%d" % p], "free")
        outcome(1, p, handsum)
        i1, i2, hs, hr = T.IT[:, a0:a0 + n0], T.IT[:, 128 + a0:128 + a0 + n0], T.HS[:, a0:a0 + n0], T.HR[:, a0:a0 + n0]
        cp(i1, T[hb][:, 0:n0], [], ["H1%d" % p, hb], "H1")
        vts(i2, i1, 2047, None, A.bitwise_and, None, ["H1%d" % p], ["H2%d" % p], "H2")
        lin(hs, i2, 1.0, 4096.0, ["H2%d" % p], ["HS%d" % p], "H3")
        send([hs], hr, nxt, "aH%d" % p, "lH%d" % p, ["HS%d" % p], ["HR%d" % p], "sendH%d" % p, n0 // 2)
        DMA(T.yp[:, 2048 + 16 * a0:2048 + 16 * (a0 + n0)], hr, ["HR%d" % p], ["oyp2%d" % p], "oyp2", n0 // 2, 4 * n0)
    fore[0] = 0.0
    splits(1)
    DMA(T.yr[:, 512:1024], T.YR1[:], ["YR1"], ["oyr1"], "oyr1", 128, 1024)
    DMA(T.yk0[:], T.KF[0:128:16, 0:3072], ["KF0", "KFt"], ["oyk0"], "oyk0", 96, 6144)
    DMA(T.yk1[:], T.KF[1:128:16, 0:3072], ["KF1", "KFt"], ["oyk1"], "oyk1", 96, 6144)

    if "order" not in PLANS:
        PLANS["order"], PLANS["score"] = make_plan(ops)
    eng = {"v": g.vector, "s": g.scalar, "t": g.tensor, "g": g, "y": g.sync}
    cs = {"v": "cv", "s": "cs", "t": "ct", "g": "cg"}
    cnt = dict((s_, 0) for s_ in cs.values())
    known = dict((q, {}) for q in eng)
    total, token = {}, [None] * len(ops)
    for i, j in PLANS["order"]:
        q, fn = ops[i]["alts"][j][0], ops[i]["alts"][j][3]
        if ops[i]["nm"] == "free":
            token[i] = [x for dp in ops[i]["deps"] for x in token[dp]]
            continue
        if q == "arr":
            s_, v = ops[i]["tok"]
            token[i] = [(s_, v, {s_: v})]
            total[s_] = v
            continue
        r = q[0]
        kn, e = known[r], eng[r]
        need = {}
        for dp in ops[i]["deps"]:
            for s_, v, ck in token[dp]:
                if kn.get(s_, 0) < v and need.get(s_, (0, None))[0] < v:
                    need[s_] = (v, ck)
        for s_ in sorted(need, key=lambda s_: (-len(need[s_][1]), s_)):
            v, ck = need[s_]
            if kn.get(s_, 0) >= v:
                continue
            e.wait_ge(T.sem[s_], v)
            for a, b in ck.items():
                if kn.get(a, 0) < b:
                    kn[a] = b
        out = fn(e)
        if q in cs:
            for x in (out if isinstance(out, list) else [out]):
                x.then_inc(T.sem[cs[q]], 1)
                cnt[cs[q]] += 1
            s_, v = cs[q], cnt[cs[q]]
        else:
            s_, v = ops[i]["tok"]
        total[s_] = v
        ck = dict(kn)
        ck[s_] = v
        token[i] = [(s_, v, ck)]
    for s_ in sorted(total):
        if known["g"].get(s_, 0) < total[s_]:
            g.wait_ge(T.sem[s_], total[s_])
